import numpy as np, ml_dtypes
CORES = [25,29,65,69,153,157,193,197]
N = 8
BF = ml_dtypes.bfloat16
M, Q, CAP, V = 2048, 128, 48, 15
R = 2 ** 20; H = R - 2 ** 13
def shave(lo, hi, u, k):
    return [lo[i] + int((hi[i] - lo[i]) * k * u[3 + i]) for i in range(3)] + [hi[i] - int((hi[i] - lo[i]) * k * u[6 + i]) for i in range(3)]
def scene(rng, h, deep, uneven):
    U = rng.random((M, 12)).tolist(); u = U[0]; side = [int(h * (1 + 0.5 * u[i])) for i in range(3)]
    lo = [int(u[3 + i] * (2 * h - side[i])) - h for i in range(3)]; hi = [lo[i] + side[i] for i in range(3)]
    box = [lo + hi] * M; skip = [M] * M; todo = [(1, M, lo, hi, M, V - 1)]
    while todo:
        a, b, lo, hi, out, v = todo.pop(); u = U[a]; s = b - a
        if s <= 4 or (s <= v and (deep or u[0] < 0.3)):
            for n in range(a, b):
                w = U[n]; box[n] = shave(lo, hi, w, 0.25)
                k = n + 1 if deep or w[2] < 0.5 else n + 1 + int(w[11] * (b - n)); skip[n] = k if k < b else out
            if out > b:
                i = int(u[1] * 3); box[b - 1][3 + i] = box[b - 1][i] - 1
            continue
        c = 5 * 2 ** (v - 5) - 1; x = max(2, s - 1 - c); z = min(s - 3, c)
        m = a + 1 + (V - 2 if deep and a == 1 else x + int(u[9] * (z - x + 1)))
        i = int(u[1] * 3); cut = lo[i] + int((hi[i] - lo[i]) * (0.25 + 0.5 * u[10]))
        l2 = lo[:]; l2[i] = min(cut + 1, hi[i]); h2 = hi[:]; h2[i] = cut
        yes, no = ((lo, h2), (l2, hi)) if u[2] < 0.5 else ((l2, hi), (lo, h2))
        box[a] = shave(yes[0], yes[1], u, 0.125); skip[a] = m
        todo += [(a + 1, m) + yes + (out, v - 1), (m, b) + no + (out, v - 1)]
    w = 2 ** rng.integers(0, 17, M) if uneven else rng.integers(1, 2 ** 16 + 1, M)
    return np.concatenate([np.array(box, np.int64).T, np.array([skip], np.int64), (w * (2 * rng.integers(0, 2, M) - 1))[None]])
def scenes(rng, h, deep=False, uneven=False):
    t = np.zeros((N, 8, 16, M), np.int64)
    for r in range(N):
        for g in range(8):
            t[r, g, :8] = scene(rng, int(h[g]), deep, uneven)
    return t
def points(rng, h):
    h = np.asarray(h, np.int64).reshape(1, 8, 1, 1); return rng.integers(-h, h + 1, (N, 8, 3, Q))
def inbox(t, p):
    return ((t[:, :3, :1] <= p) & (p <= t[:, 3:6, :1])).all(-2)
def far(rng, n):
    return rng.integers(R - 2 ** 12, R + 1, (3, n))
def made(rng, t, p, s=0):
    for r in range(N):
        for q in [(r + s + i) % N for i in range(N)]:
            if q == r: continue
            k = inbox(t[q], p[r])
            for g in range(8):
                i = rng.permutation(np.flatnonzero(k[g]))[CAP:]
                if len(i): p[r, g][:, i] = far(rng, len(i))
    return {"nodes": t.reshape(N, 128, M).astype(np.int32), "pts": p.reshape(N, 24, Q).astype(np.int32)}
def setup_inputs(rng):
    return made(rng, scenes(rng, [H] * 8), points(rng, [H] * 8))
def setup_inputs_faces(rng):
    t = scenes(rng, [H] * 8); p = np.zeros((N, 8, 3, Q), np.int64)
    for g in range(8):
        q = rng.integers(0, N, (N, 1, Q)); n = rng.integers(0, M, (N, 1, Q)) * (rng.random((N, 1, Q)) > 0.25)
        p[:, g] = t[q, g, np.arange(3)[:, None] + 3 * rng.integers(0, 2, (N, 3, Q)), n] + rng.integers(-1, 2, (N, 3, Q))
    return made(rng, t, p)
def setup_inputs_full(rng):
    t = scenes(rng, [H] * 8); p = points(rng, [H] * 8); s = int(rng.integers(1, N))
    for r in range(N):
        b = t[(r + s) % N, :, :6, :1]; p[r] = b[:, :3] + np.floor(rng.random((8, 3, Q)) * (b[:, 3:] - b[:, :3] + 1)).astype(np.int64)
    return made(rng, t, p, s)
def setup_inputs_few(rng):
    t = scenes(rng, [H] * 8); p = points(rng, [H] * 8); o = rng.permutation(N); b, c = o[:2]; e = o[2:]; t[e, :, 3, 0] = t[e, :, 0, 0] - 1
    w = t[c, :, :6, :1]; p[c] = w[:, :3] + np.floor(rng.random((8, 3, Q)) * (w[:, 3:] - w[:, :3] + 1)).astype(np.int64)
    for g in range(8):
        p[b, g] = far(rng, Q); v = t[b, g, :3, 0] + np.floor(rng.random(3) * (t[b, g, 3:6, 0] - t[b, g, :3, 0] + 1)).astype(np.int64)
        p[b, g, :, :4] = v[:, None]; p[b, g, :, Q - 4:] = v[:, None]
    return made(rng, t, p)
def setup_inputs_deep(rng):
    return made(rng, scenes(rng, [H] * 8, deep=True), points(rng, [H] * 8))
def setup_inputs_spread(rng):
    h = 2 ** rng.integers(5, 20, 8); p = points(rng, h)
    return made(rng, scenes(rng, h, uneven=True), p >> (rng.integers(0, 6, (N, 8, 1, Q)) * (rng.random((N, 8, 1, Q)) < 0.25)))
def walk(t, p):
    nd = t.transpose(0, 2, 1); x = p.transpose(0, 1, 3, 2); c = np.zeros((N, 8, Q), np.int64); s = np.zeros_like(c); v = np.zeros_like(c)
    while (c < M).any():
        live = c < M; b = nd[np.arange(8)[:, None], np.minimum(c, M - 1)]
        hit = live & (b[..., :3] <= x).all(-1) & (x <= b[..., 3:6]).all(-1)
        s += hit * b[..., 7]; v += live; c = np.where(live, np.where(hit, c + 1, b[..., 6]), c)
    return s, v
def check_inputs(d):
    t = d["nodes"].astype(np.int64).reshape(N, 8, 16, M); p = d["pts"].astype(np.int64).reshape(N, 8, 3, Q); k = t[:, :, 6]; bad = []
    if (k <= np.arange(M)).any() or (k > M).any() or (k[:, :, 0] != M).any(): return ["skips"]
    if np.abs(t[:, :, :6]).max() > R or np.abs(p).max() > R: bad.append("coordinates")
    if np.abs(t[:, :, 7]).max() > 2 ** 16: bad.append("weights")
    if t[:, :, 8:].any(): bad.append("rows of zeros")
    n = np.stack([np.sum(inbox(t[q], p), axis=-1) for q in range(N)])
    n[np.arange(N), np.arange(N)] = 0
    if n.max() > CAP: bad.append("points in another rank's first box")
    if max(walk(t[q], p)[1].max() for q in range(N)) > V: bad.append("visits")
    return bad
def reference(nodes, pts):
    t = nodes.astype(np.int64).reshape(N, 8, 16, M); p = pts.astype(np.int64).reshape(N, 8, 3, Q); y = np.zeros((N, 8, Q), np.int64)
    for q in range(N):
        y += walk(t[q], p)[0]
    return {"y": y.astype(np.float32)}

@@ -1,0 +1,357 @@
+from concourse.bass import DstId, RemoteDMATransfer
+from concourse.mybir import AluOpType as Op, AxisListType, ActivationFunctionType as Fn
+
+V = 15
+SCRATCH = {
+    "pin": ("sbuf", [128, 64], "int32"), "pq": ("sbuf", [128, 64], "int32"), "msg": ("sbuf", [128, 64], "float16"),
+    "land": ("sbuf", [128, 448], "float16"), "rmsg": ("sbuf", [128, 64], "float16"), "rres": ("sbuf", [128, 16], "float32"),
+    "coli": ("sbuf", [128, 8], "int32"), "colf": ("sbuf", [128, 32], "float32"), "colb": ("sbuf", [128, 8], "bfloat16"),
+    "i16": ("sbuf", [128, 16], "float32"), "i24": ("sbuf", [128, 24], "float32"), "vi": ("sbuf", [128, 128], "int32"),
+    "u1": ("sbuf", [128, 144], "float32"), "u2": ("sbuf", [128, 144], "float32"),
+    "e16": ("sbuf", [128, 16], "float32"), "j24": ("sbuf", [128, 24], "float32"),
+    "lpf": ("sbuf", [128, 128], "float32"), "lp": ("sbuf", [128, 256], "float16"),
+    "zx": ("sbuf", [128, 144], "bfloat16"), "zw": ("sbuf", [128, 144], "bfloat16"), "zq": ("sbuf", [128, 144], "bfloat16"),
+    "sk": ("sbuf", [128, 128], "int32"), "wt": ("sbuf", [128, 128], "int32"), "n0": ("sbuf", [128, 8], "int32"),
+    "pa1": ("sbuf", [128, 128], "int32"), "pa0": ("sbuf", [128, 128], "int32"), "pz": ("sbuf", [128, 128], "int32"),
+    "ph": ("sbuf", [128, 128], "int32"), "pl": ("sbuf", [128, 128], "int32"), "v2k": ("sbuf", [128, 128], "int32"),
+    "tm": ("sbuf", [128, 128], "int32"), "hv": ("sbuf", [128, 128], "int32"), "a0r": ("sbuf", [128, 128], "int32"),
+    "hitl": ("sbuf", [128, 128], "uint16"), "missl": ("sbuf", [128, 128], "uint16"),
+    "basei": ("sbuf", [128, 2048], "int32"), "basef": ("sbuf", [128, 2048], "float32"),
+    "tab": ("sbuf", [128, 4098], "float32"),
+    "rland": ("sbuf", [128, 64], "float32"), "s32": ("sbuf", [128, 32], "float32"), "s16": ("sbuf", [128, 16], "float32"),
+    "ysum": ("sbuf", [128, 8], "float32"),
+    "psm": ("psum", [128, 8], "float32"),
+}
+SEMAPHORES = ["vc", "gi0", "gi1", "m0", "dP", "dS", "dW", "dN", "dB0", "dB1", "dZ", "dPc", "dY",
+              "kmsg", "klp", "kz", "ka", "kw", "kbase", "ht", "w47", "ys",
+              "pa", "pb", "rs", "rm", "rr", "ls", "rl"]
+for _b in "AB":
+    SCRATCH.update({
+        "off" + _b: ("sbuf", [128, 32], "uint16"), "P" + _b: ("sbuf", [128, 512], "float32"), "D" + _b: ("sbuf", [128, 512], "bfloat16"),
+        "C0" + _b: ("sbuf", [128, 512], "bfloat16"), "C1" + _b: ("sbuf", [128, 512], "bfloat16"),
+        "R" + _b: ("sbuf", [128, 32], "float32"), "t1" + _b: ("sbuf", [128, 64], "float32"), "t2" + _b: ("sbuf", [128, 64], "float32"),
+        "t3" + _b: ("sbuf", [128, 64], "float32"),
+        "pp" + _b: ("psum", [128, 512], "float32"), "X" + _b: ("psum", [128, 64], "float32"), "W" + _b: ("psum", [128, 64], "float32"),
+    })
+    SEMAPHORES += [k + _b for k in ("pp", "pc", "g", "c", "o", "x", "wa", "wb", "q", "kr")]
+
+
+def mask_of(engs):
+    m = 0
+    for e in engs:
+        m |= 1 << e
+    return m
+
+
+def rank_program(g, core, T, topo):
+    cores = list(T.cores)
+
+    def direct(c):
+        return [d for d in cores if d != c and topo.may_write(c, d)]
+
+    def cross(c):
+        return [d for d in cores if d != c and not topo.may_write(c, d)]
+
+    def shares(c):
+        x = cross(c)
+        rl = [k for k in topo.cores_of(c) if k not in cores and topo.die(k) == topo.die(c) and all(topo.may_write(k, d) for d in x)][:2]
+        n = -(-len(x) // len(rl))
+        return [(k, x[i * n:(i + 1) * n]) for i, k in enumerate(rl)]
+
+    def slot(dst, src):
+        return (direct(dst) + cross(dst)).index(src)
+
+    def tr(src_ap, dst_ap, dst, engs, sem):
+        rid, pid = topo.addr(dst, core)
+        return RemoteDMATransfer(dst_ids=[DstId(rid=rid, pnc=pid)], dma_engine_mask=mask_of(engs), remote_sem=T.sem[sem],
+                                 srcs=[src_ap], dsts=[dst_ap], alu_op=0)
+
+    if T.rank_of(core) is None:
+        for c in cores:
+            for k, (rel, dests) in enumerate(shares(c)):
+                if rel != core:
+                    continue
+                engs = [topo.engines(core, d)[4 * i:4 * i + 4] for i, d in enumerate(dests)]
+                g.wait_ge(T.sem.rm, 4)
+                g.remote_dma_fused([tr(T.rmsg[:, :], T.land[:, 64 * slot(d, c):64 * slot(d, c) + 64], d, engs[i], "pb")
+                                    for i, d in enumerate(dests)], local_sem=T.sem.rl)
+                g.wait_ge(T.sem.rr, 4)
+                g.remote_dma_fused([tr(T.rres[:, 8 * i:8 * i + 8], T.rland[:, 8 * slot(d, c) + 8:8 * slot(d, c) + 16], d, engs[i], "rs")
+                                    for i, d in enumerate(dests)], local_sem=T.sem.rl)
+                g.wait_ge(T.sem.rl, 16)
+        return
+
+    vec, ten, sca, syn = g.vector, g.tensor, g.scalar, g.sync
+    nv = [0]
+
+    def v(ins):
+        ins.then_inc(T.sem.vc, 1)
+        nv[0] += 1
+
+    def vw():
+        vec.wait_ge(T.sem.vc, nv[0])
+
+    def pub(*names):
+        vw()
+        for name in names:
+            vec.sem_inc(T.sem[name], 1)
+
+    def ts(out, in0, s1, op0, s2=None, op1=None):
+        if op1 is None:
+            return vec.tensor_scalar(out=out, in0=in0, scalar1=s1, scalar2=None, op0=op0)
+        return vec.tensor_scalar(out=out, in0=in0, scalar1=s1, scalar2=s2, op0=op0, op1=op1)
+
+    def cf(k):
+        return T.colf[:, k:k + 1]
+
+    def ci(k):
+        return T.coli[:, k:k + 1]
+
+    for h in range(2):
+        q = syn if h == 0 else sca
+        for lo in range(2):
+            k = 64 * h + 32 * lo
+            q.dma_start(out=T.pin[k:k + 24, :], in_=T.pts[:, 64 * h:64 * h + 64]).then_inc(T.sem.dP, 16)
+    syn.dma_start(out=T.wt[:, :], in_=T.nodes[7::16, :]).then_inc(T.sem.dW, 16)
+    sca.dma_start(out=T.sk[:, :], in_=T.nodes[6::16, :]).then_inc(T.sem.dS, 16)
+    sca.dma_start(out=T.n0[:, :], in_=T.nodes[:, 0:8]).then_inc(T.sem.dN, 16)
+    syn.wait_ge(T.sem.m0, 1)
+    sca.wait_ge(T.sem.m0, 1)
+
+    def load(q, gg, h):
+        a, b = (0, 1024) if h == 0 else (1024, 2047)
+        q.dma_start(out=T.basei[16 * gg:16 * gg + 8, a:b], in_=T.nodes[16 * gg:16 * gg + 8, a + 1:b + 1]).then_inc(T.sem["dB%d" % h], 16)
+    for gg in range(4):
+        load(syn, gg, 0)
+        load(sca, gg + 4, 0)
+    for a in (13, 14, 15):
+        sca.dma_start(out=T.basei[a::16, 0:2047], in_=T.nodes[a::16, 1:2048]).then_inc(T.sem.dZ, 16)
+    for gg in range(4):
+        load(sca, gg + 4, 1)
+    syn.wait_ge(T.sem.ka, 1)
+    for row, name in ((8, "pa1"), (9, "pa0"), (12, "pz")):
+        syn.dma_start(out=T.basei[row::16, 0:2048], in_=T[name][:, :]).then_inc(T.sem.dPc, 16)
+    syn.wait_ge(T.sem.kw, 1)
+    for row, name in ((10, "ph"), (11, "pl")):
+        syn.dma_start(out=T.basei[row::16, 0:2048], in_=T[name][:, :]).then_inc(T.sem.dPc, 16)
+    for gg in range(4):
+        load(syn, gg, 1)
+
+    fl = {"allow_small_or_imprecise_dtypes": True}
+    g.iota(T.coli[:, 0:1], [[0, 1]], 0, 1).then_inc(T.sem.gi0, 1)
+    g.iota(T.i16[:, :], [[1, 16]], 0, 0, **fl).then_inc(T.sem.gi0, 1)
+    g.iota(T.i24[:, :], [[1, 24]], 0, 0, **fl).then_inc(T.sem.gi0, 1)
+    g.iota(T.vi[:, :], [[1, 128]], 1, 128).then_inc(T.sem.gi1, 1)
+    g.iota(T.u1[:, :], [[1, 144]], 0, 0, **fl).then_inc(T.sem.gi1, 1)
+    g.iota(T.u2[:, :], [[1, 72], [0, 2]], 0, 0, **fl).then_inc(T.sem.gi1, 1)
+
+    vec.memset(T.basei[:, 2040:2048], 0).then_inc(T.sem.m0, 1)
+    v(vec.memset(T.pq[:, :], 0))
+    v(vec.memset(T.lpf[:, :], 0.0))
+    vec.wait_ge(T.sem.gi0, 3)
+    v(ts(ci(1), ci(0), 15, Op.bitwise_and))
+    v(ts(ci(2), ci(0), 4, Op.arith_shift_right))
+    v(ts(ci(3), ci(0), 31, Op.bitwise_and))
+    v(ts(ci(4), ci(0), 1, Op.bitwise_and))
+    v(ts(ci(5), ci(0), 5, Op.arith_shift_right, 1, Op.bitwise_and))
+    v(ts(ci(6), ci(0), 6, Op.arith_shift_right))
+    vw()
+    v(vec.tensor_copy(out=cf(0), in_=ci(1)))
+    v(ts(cf(1), ci(2), 16.0, Op.mult, 15.0, Op.add))
+    v(ts(cf(2), ci(2), 8.0, Op.mult, 7.0, Op.add))
+    v(vec.tensor_copy(out=cf(3), in_=ci(3)))
+    v(vec.tensor_copy(out=cf(4), in_=ci(4)))
+    v(ts(cf(5), ci(4), -1.0, Op.mult, 1.0, Op.add))
+    v(ts(cf(6), ci(5), -1023.0, Op.mult, 1024.0, Op.add))
+    v(ts(cf(21), ci(6), -1.0, Op.mult, 1.0, Op.add))
+    v(vec.tensor_copy(out=cf(22), in_=ci(6)))
+    vw()
+    v(ts(T.e16[:, :], T.i16[:, :], cf(0), Op.is_equal))
+    v(ts(T.j24[:, :], T.i24[:, :], cf(3), Op.is_equal, cf(6), Op.mult))
+    vec.wait_ge(T.sem.gi1, 3)
+    v(ts(T.pa1[:, :], T.vi[:, :], 127, Op.bitwise_and))
+    v(ts(T.a0r[:, :], T.vi[:, :], 7, Op.arith_shift_right, 15, Op.bitwise_and))
+    v(ts(T.v2k[:, :], T.vi[:, :], 2047, Op.bitwise_and))
+    vw()
+    v(ts(T.tm[:, :], T.v2k[:, :], 0.0, Op.is_equal))
+    v(ts(T.pz[:, :], T.v2k[:, :], 2047.0, Op.not_equal))
+    for a in range(6):
+        v(vec.tensor_copy(out=T.lpf[:, a::16], in_=T.j24[:, a % 3::3]))
+    vw()
+    v(vec.tensor_tensor(out=T.pa0[:, :], in0=T.a0r[:, :], in1=T.tm[:, :], op=Op.subtract))
+    v(ts(T.lp[:, 0:128], T.lpf[:, :], cf(21), Op.mult))
+    v(ts(T.lp[:, 128:256], T.lpf[:, :], cf(22), Op.mult))
+    pub("ka")
+    vec.wait_ge(T.sem.dP, 64)
+    for h in range(2):
+        v(ts(T.pq[64 * h:64 * h + 24, :], T.pin[64 * h:64 * h + 24, :], 10, Op.arith_shift_right))
+        v(ts(T.pq[64 * h + 32:64 * h + 56, :], T.pin[64 * h + 32:64 * h + 56, :], 1023, Op.bitwise_and))
+    vw()
+    v(vec.tensor_copy(out=T.msg[:, :], in_=T.pq[:, :]))
+    pub("kmsg", "klp")
+    vec.wait_ge(T.sem.dW, 16)
+    v(ts(T.ph[:, :], T.wt[:, :], 8, Op.arith_shift_right))
+    v(ts(T.pl[:, :], T.wt[:, :], 255, Op.bitwise_and))
+    pub("kw")
+    vec.wait_ge(T.sem.dS, 16)
+    v(ts(T.missl[:, :], T.sk[:, :], -1.0, Op.add))
+    v(ts(T.hv[:, :], T.vi[:, :], -1.0, Op.add))
+    v(vec.tensor_reduce(out=cf(7), in_=T.e16[:, 0:3], axis=AxisListType.X, op=Op.add))
+    v(vec.tensor_reduce(out=cf(8), in_=T.e16[:, 3:6], axis=AxisListType.X, op=Op.add))
+    v(ts(cf(13), T.e16[:, 10:11], 256.0, Op.mult, T.e16[:, 11:12], Op.add))
+    v(ts(cf(15), T.e16[:, 10:11], -1.0, Op.mult, 1.0, Op.add))
+    vec.wait_ge(T.sem.dN, 16)
+    v(vec.tensor_copy(out=cf(19), in_=T.n0[:, 0:1]))
+    vw()
+    v(ts(T.v2k[:, :], T.hv[:, :], 2047, Op.bitwise_and))
+    v(vec.tensor_tensor(out=cf(9), in0=cf(7), in1=cf(8), op=Op.subtract))
+    v(vec.tensor_tensor(out=cf(16), in0=cf(15), in1=T.e16[:, 11:12], op=Op.subtract))
+    v(ts(cf(17), cf(7), 300.0, Op.mult, -300.0, Op.add))
+    v(ts(cf(18), cf(7), -299.0, Op.mult, 300.0, Op.add))
+    vw()
+    v(vec.tensor_copy(out=T.hitl[:, :], in_=T.v2k[:, :]))
+    v(ts(cf(10), cf(9), 11.0 / 64, Op.mult))
+    v(vec.tensor_tensor(out=cf(14), in0=cf(9), in1=T.e16[:, 12:13], op=Op.add))
+    v(ts(T.colb[:, 0:1], cf(8), 299.0, Op.mult, cf(17), Op.add))
+    v(ts(T.colb[:, 1:2], cf(8), -300.0, Op.mult, cf(18), Op.add))
+    vw()
+    v(ts(cf(11), T.e16[:, 9:10], 2.0, Op.mult, cf(10), Op.add))
+    v(ts(T.zw[:, :], T.u2[:, :], cf(2), Op.is_equal, cf(13), Op.mult))
+    v(ts(T.zq[:, :], T.u2[:, :], cf(2), Op.is_equal, cf(14), Op.mult))
+    vw()
+    v(ts(cf(12), T.e16[:, 8:9], 32.0, Op.mult, cf(11), Op.add))
+    vw()
+    v(ts(T.zx[:, :], T.u1[:, :], cf(1), Op.is_equal, cf(12), Op.mult))
+
+    dire, shar = direct(core), shares(core)
+    chip_mates = topo.cores_of(core)
+    g.wait_ge(T.sem.kmsg, 1)
+    wide = topo.engines(core, shar[0][0])
+    n_on = len(wide) // 2
+    rel_engs = [wide[n_on + 4 * i:n_on + 4 * i + 4] for i in range(len(shar))]
+    dir_engs, k = {}, 0
+    for d in dire:
+        if d in chip_mates:
+            dir_engs[d] = wide[n_on:n_on + 4]
+        else:
+            dir_engs[d] = topo.engines(core, d)[4 * k:4 * k + 4]
+            k += 1
+    g.remote_dma_fused([tr(T.msg[:, :], T.rmsg[:, :], rel, rel_engs[i], "rm") for i, (rel, _) in enumerate(shar)], local_sem=T.sem.ls)
+    g.remote_dma_fused([tr(T.msg[:, :], T.land[:, 64 * slot(d, core):64 * slot(d, core) + 64], d, dir_engs[d], "pa") for d in dire],
+                       local_sem=T.sem.ls)
+
+    vec.wait_ge(T.sem.dB0, 128)
+    vec.wait_ge(T.sem.dZ, 48)
+    vec.wait_ge(T.sem.dPc, 80)
+    v(vec.tensor_copy(out=T.basef[:, 0:1024], in_=T.basei[:, 0:1024]))
+    vec.wait_ge(T.sem.dB1, 128)
+    v(vec.tensor_copy(out=T.basef[:, 1024:2048], in_=T.basei[:, 1024:2048]))
+    pub("kbase")
+    v(vec.tensor_copy(out=T.colb[:, 2:3], in_=T.basef[:, 2047:2048]))
+    v(ts(T.tab[:, 0:1], T.basef[:, 2047:2048], cf(16), Op.mult))
+    v(ts(T.tab[:, 1:2], T.basef[:, 2047:2048], cf(16), Op.mult))
+    v(ts(T.tab[:, 3:4098:2], T.basef[:, 0:2048].indirect(T.missl[:, 0:128]), cf(16), Op.mult))
+    pub("kz")
+    sca.wait_ge(T.sem.kbase, 1)
+    sca.activation(out=T.tab[:, 2:4097:2], in_=T.basef[:, 0:2048].indirect(T.hitl[:, 0:128]), func=Fn.Copy).then_inc(T.sem.ht, 1)
+    for b in "AB":
+        sca.wait_ge(T.sem["g" + b], 1)
+        sca.activation(out=T["P" + b][:, :], in_=T["pp" + b][:, :], func=Fn.Copy).then_inc(T.sem["pc" + b], 1)
+
+    def spread(b, srcs):
+        for r, (buf, c0) in enumerate(srcs):
+            for h in range(2):
+                ten.matmul(T["pp" + b][:, 256 * h + r:256 * h + 253 + r:4], T.lp[:, 128 * h:128 * h + 128],
+                           T[buf][:, c0:c0 + 64], True, True).then_inc(T.sem["pp" + b], 1)
+
+    def tx(b, t):
+        for j in range(16):
+            ten.matmul(T["X" + b][:, 0:32], T.zx[:, 15 - j:143 - j], T["C%d%s" % (t % 2, b)][:, j:512:16], j == 0, j == 15).then_inc(T.sem["x" + b], 1)
+
+    def tw(b, t):
+        for p in range(8):
+            ten.matmul(T["W" + b][:, 0:64], T.zw[:, 14 - 2 * p:142 - 2 * p], T["C%d%s" % (t % 2, b)][:, 64 * p:64 * p + 64],
+                       t == 1 and p == 0, t == V - 1 and p == 7).then_inc(T.sem["w" + "ab"[t % 2] + b], 1)
+
+    def tq(b, t):
+        for p in range(8):
+            ten.matmul(T["X" + b][:, 0:64], T.zq[:, 14 - 2 * p:142 - 2 * p], T["C%d%s" % (t % 2, b)][:, 64 * p:64 * p + 64],
+                       p == 0, p == 7).then_inc(T.sem["q" + b], 1)
+
+    nd = len(dire)
+    ten.wait_ge(T.sem.klp, 1)
+    ten.wait_ge(T.sem.pa, 4 * nd)
+    spread("A", [("msg", 0)] + [("land", 64 * i) for i in range(nd)])
+    ten.wait_ge(T.sem.kz, 1)
+    for p in range(8):
+        ten.matmul(T.psm[:, 0:1], T.zw[:, 14 - 2 * p:142 - 2 * p], T.colb[:, 2:3], p == 0, p == 7).then_inc(T.sem.w47, 1)
+    ten.wait_ge(T.sem.pb, 4 * len(cross(core)))
+    spread("B", [("land", 64 * (nd + i)) for i in range(len(cross(core)))])
+    for t in range(V):
+        for b in "AB":
+            ten.wait_ge(T.sem["c" + b], t + 1)
+            if t < V - 1:
+                tx(b, t)
+            if t > 0:
+                tw(b, t)
+            if t == V - 1:
+                tq(b, t)
+
+    def clamp(b, t):
+        ts(T["C%d%s" % (t % 2, b)][:, :], T["D" + b][:, :], T.colb[:, 0:1], Op.max, T.colb[:, 1:2], Op.min).then_inc(T.sem["c" + b], 1)
+
+    for b in "AB":
+        vec.wait_ge(T.sem["pp" + b], 8)
+        ts(T["D" + b][:, :], T["pp" + b][:, :], -1.0, Op.mult, cf(19), Op.add).then_inc(T.sem["g" + b], 1)
+        vec.wait_ge(T.sem["g" + b], 1)
+        clamp(b, 0)
+    vec.wait_ge(T.sem.w47, 8)
+    v(vec.tensor_copy(out=cf(20), in_=T.psm[:, 0:1]))
+    vec.wait_ge(T.sem.ht, 1)
+    for t in range(1, V):
+        for b in "AB":
+            vec.wait_ge(T.sem["x" + b], 16 * t)
+            ts(T["off" + b][:, :], T["X" + b][:, 0:32], 2.4375, Op.add).then_inc(T.sem["o" + b], 1)
+            if t == 1:
+                vec.wait_ge(T.sem["pc" + b], 1)
+            vec.wait_ge(T.sem["o" + b], t)
+            vec.tensor_tensor(out=T["D" + b][:, :], in0=T.tab[:, 0:4098].indirect(T["off" + b][:, 0:32]), in1=T["P" + b][:, :],
+                              op=Op.subtract).then_inc(T.sem["g" + b], 1)
+            if t > 2:
+                vec.wait_ge(T.sem["w" + "ab"[t % 2] + b], 8 * ((t - 1) // 2))
+            vec.wait_ge(T.sem["g" + b], t + 1)
+            clamp(b, t)
+
+    for b in "AB":
+        vec.wait_ge(T.sem["wa" + b], 8 * ((V - 1) // 2))
+        vec.wait_ge(T.sem["wb" + b], 8 * (V // 2))
+        vec.wait_ge(T.sem["q" + b], 8)
+        vw()
+        v(ts(T["t1" + b][:, :], T["X" + b][:, 0:64], 0.5, Op.is_lt, cf(20), Op.mult))
+        vw()
+        v(vec.tensor_tensor(out=T["t2" + b][:, :], in0=T["W" + b][:, 0:64], in1=T["t1" + b][:, :], op=Op.add))
+        vw()
+        v(ts(T["t3" + b][:, 0:32], T["t2" + b][:, 0:32], cf(5), Op.mult))
+        v(ts(T["t3" + b][:, 32:64], T["t2" + b][:, 32:64], cf(4), Op.mult))
+        vw()
+        for r in range(4):
+            out = T.rland[:, 0:8] if (b == "A" and r == 0) else T["R" + b][:, 8 * r:8 * r + 8]
+            v(vec.tensor_tensor(out=out, in0=T["t3" + b][:, r:32:4], in1=T["t3" + b][:, 32 + r:64:4], op=Op.add))
+        pub("kr" + b)
+    g.wait_ge(T.sem.krA, 1)
+    g.remote_dma_fused([tr(T.RA[:, 8 * i + 8:8 * i + 16], T.rland[:, 8 * slot(d, core) + 8:8 * slot(d, core) + 16], d, dir_engs[d], "rs")
+                        for i, d in enumerate(dire)], local_sem=T.sem.ls)
+    g.wait_ge(T.sem.krB, 1)
+    g.remote_dma_fused([tr(T.RB[:, 16 * i:16 * i + 16], T.rres[:, :], rel, rel_engs[i], "rr") for i, (rel, _) in enumerate(shar)],
+                       local_sem=T.sem.ls)
+    vec.wait_ge(T.sem.rs, 4 * 7)
+    v(vec.tensor_tensor(out=T.s32[:, :], in0=T.rland[:, 0:32], in1=T.rland[:, 32:64], op=Op.add))
+    vw()
+    v(vec.tensor_tensor(out=T.s16[:, :], in0=T.s32[:, 0:16], in1=T.s32[:, 16:32], op=Op.add))
+    vw()
+    v(vec.tensor_tensor(out=T.ysum[:, :], in0=T.s16[:, 0:8], in1=T.s16[:, 8:16], op=Op.add))
+    pub("ys")
+    syn.wait_ge(T.sem.ys, 1)
+    syn.dma_start(out=T.y[:, :], in_=T.ysum[:, :]).then_inc(T.sem.dY, 16)
+    syn.wait_ge(T.sem.dY, 16)
+    g.wait_ge(T.sem.ls, 2 * (4 * len(shar) + 4 * nd))

@@ -2,15 +2,20 @@ from concourse.bass import DstId, RemoteDMATransfer
 from concourse.mybir import AluOpType as Op, AxisListType, ActivationFunctionType as Fn
 
 V = 15
+VC = 320
+EPS = 2.0 ** -12
+H1, H2 = range(2, 10), range(10, 12)
 SCRATCH = {
     "pin": ("sbuf", [128, 64], "int32"), "pq": ("sbuf", [128, 64], "int32"), "msg": ("sbuf", [128, 64], "float16"),
     "land": ("sbuf", [128, 448], "float16"), "rmsg": ("sbuf", [128, 64], "float16"), "rres": ("sbuf", [128, 16], "float32"),
     "coli": ("sbuf", [128, 8], "int32"), "colf": ("sbuf", [128, 32], "float32"), "colb": ("sbuf", [128, 8], "bfloat16"),
+    "colt": ("sbuf", [128, 8], "float32"),
     "i16": ("sbuf", [128, 16], "float32"), "i24": ("sbuf", [128, 24], "float32"), "vi": ("sbuf", [128, 128], "int32"),
     "u1": ("sbuf", [128, 144], "float32"), "u2": ("sbuf", [128, 144], "float32"),
     "e16": ("sbuf", [128, 16], "float32"), "j24": ("sbuf", [128, 24], "float32"),
     "lpf": ("sbuf", [128, 128], "float32"), "lp": ("sbuf", [128, 256], "float16"),
-    "zx": ("sbuf", [128, 144], "bfloat16"), "zw": ("sbuf", [128, 144], "bfloat16"), "zq": ("sbuf", [128, 144], "bfloat16"),
+    "zx": ("sbuf", [128, 144], "bfloat16"), "zo": ("sbuf", [128, 144], "bfloat16"), "zw": ("sbuf", [128, 144], "bfloat16"),
+    "zq": ("sbuf", [128, 144], "bfloat16"), "zh": ("sbuf", [128, 144], "bfloat16"),
     "sk": ("sbuf", [128, 128], "int32"), "wt": ("sbuf", [128, 128], "int32"), "n0": ("sbuf", [128, 8], "int32"),
     "pa1": ("sbuf", [128, 128], "int32"), "pa0": ("sbuf", [128, 128], "int32"), "pz": ("sbuf", [128, 128], "int32"),
     "ph": ("sbuf", [128, 128], "int32"), "pl": ("sbuf", [128, 128], "int32"), "v2k": ("sbuf", [128, 128], "int32"),
@@ -20,20 +25,21 @@ SCRATCH = {
     "tab": ("sbuf", [128, 4098], "float32"),
     "rland": ("sbuf", [128, 64], "float32"), "s32": ("sbuf", [128, 32], "float32"), "s16": ("sbuf", [128, 16], "float32"),
     "ysum": ("sbuf", [128, 8], "float32"),
-    "psm": ("psum", [128, 8], "float32"),
+    "psm": ("psum", [128, 144], "float32"),
 }
 SEMAPHORES = ["vc", "gi0", "gi1", "m0", "dP", "dS", "dW", "dN", "dB0", "dB1", "dZ", "dPc", "dY",
-              "kmsg", "klp", "kz", "ka", "kw", "kbase", "ht", "w47", "ys",
+              "kmsg", "klp", "kz", "ka", "kw", "kbase", "kc", "kn", "kh", "ke", "kt", "ht", "w47", "ys",
               "pa", "pb", "rs", "rm", "rr", "ls", "rl"]
 for _b in "AB":
     SCRATCH.update({
         "off" + _b: ("sbuf", [128, 32], "uint16"), "P" + _b: ("sbuf", [128, 512], "float32"), "D" + _b: ("sbuf", [128, 512], "bfloat16"),
         "C0" + _b: ("sbuf", [128, 512], "bfloat16"), "C1" + _b: ("sbuf", [128, 512], "bfloat16"),
-        "R" + _b: ("sbuf", [128, 32], "float32"), "t1" + _b: ("sbuf", [128, 64], "float32"), "t2" + _b: ("sbuf", [128, 64], "float32"),
-        "t3" + _b: ("sbuf", [128, 64], "float32"),
+        "h1" + _b: ("sbuf", [128, 512], "bfloat16"), "h2" + _b: ("sbuf", [128, 512], "bfloat16"),
+        "R" + _b: ("sbuf", [128, 32], "float32"), "t0" + _b: ("sbuf", [128, 64], "float32"), "t1" + _b: ("sbuf", [128, 64], "float32"),
+        "t2" + _b: ("sbuf", [128, 64], "float32"), "t3" + _b: ("sbuf", [128, 64], "float32"), "t4" + _b: ("sbuf", [128, 64], "float32"),
         "pp" + _b: ("psum", [128, 512], "float32"), "X" + _b: ("psum", [128, 64], "float32"), "W" + _b: ("psum", [128, 64], "float32"),
     })
-    SEMAPHORES += [k + _b for k in ("pp", "pc", "g", "c", "o", "x", "wa", "wb", "q", "kr")]
+    SEMAPHORES += [k + _b for k in ("pp", "pc", "sx", "sy", "g", "c", "s", "o", "x", "wa", "wb", "qo", "q", "kr", "hx", "hy", "hz", "hw")]
 
 
 def mask_of(engs):
@@ -101,11 +107,17 @@ def rank_program(g, core, T, topo):
             return vec.tensor_scalar(out=out, in0=in0, scalar1=s1, scalar2=None, op0=op0)
         return vec.tensor_scalar(out=out, in0=in0, scalar1=s1, scalar2=s2, op0=op0, op1=op1)
 
+    def tt(out, a, b, op):
+        return vec.tensor_tensor(out=out, in0=a, in1=b, op=op)
+
     def cf(k):
         return T.colf[:, k:k + 1]
 
     def ci(k):
         return T.coli[:, k:k + 1]
+
+    def ek(k):
+        return T.e16[:, k:k + 1]
 
     for h in range(2):
         q = syn if h == 0 else sca
@@ -120,67 +132,50 @@ def rank_program(g, core, T, topo):
 
     def load(q, gg, h):
         a, b = (0, 1024) if h == 0 else (1024, 2047)
-        q.dma_start(out=T.basei[16 * gg:16 * gg + 8, a:b], in_=T.nodes[16 * gg:16 * gg + 8, a + 1:b + 1]).then_inc(T.sem["dB%d" % h], 16)
+        q.dma_start(out=T.basei[16 * gg:16 * gg + 7, a:b], in_=T.nodes[16 * gg:16 * gg + 7, a + 1:b + 1]).then_inc(T.sem["dB%d" % h], 16)
     for gg in range(4):
         load(syn, gg, 0)
         load(sca, gg + 4, 0)
-    for a in (13, 14, 15):
+    for a in (11, 12, 13, 14):
         sca.dma_start(out=T.basei[a::16, 0:2047], in_=T.nodes[a::16, 1:2048]).then_inc(T.sem.dZ, 16)
     for gg in range(4):
         load(sca, gg + 4, 1)
     syn.wait_ge(T.sem.ka, 1)
-    for row, name in ((8, "pa1"), (9, "pa0"), (12, "pz")):
+    for row, name in ((8, "pa1"), (9, "pa0"), (10, "pz")):
         syn.dma_start(out=T.basei[row::16, 0:2048], in_=T[name][:, :]).then_inc(T.sem.dPc, 16)
     syn.wait_ge(T.sem.kw, 1)
-    for row, name in ((10, "ph"), (11, "pl")):
+    for row, name in ((7, "ph"), (15, "pl")):
         syn.dma_start(out=T.basei[row::16, 0:2048], in_=T[name][:, :]).then_inc(T.sem.dPc, 16)
     for gg in range(4):
         load(syn, gg, 1)
 
     fl = {"allow_small_or_imprecise_dtypes": True}
     g.iota(T.coli[:, 0:1], [[0, 1]], 0, 1).then_inc(T.sem.gi0, 1)
-    g.iota(T.i16[:, :], [[1, 16]], 0, 0, **fl).then_inc(T.sem.gi0, 1)
-    g.iota(T.i24[:, :], [[1, 24]], 0, 0, **fl).then_inc(T.sem.gi0, 1)
-    g.iota(T.vi[:, :], [[1, 128]], 1, 128).then_inc(T.sem.gi1, 1)
+    g.iota(T.vi[:, :], [[1, 128]], 1, 128).then_inc(T.sem.gi0, 1)
+    g.iota(T.i16[:, :], [[1, 16]], 0, 0, **fl).then_inc(T.sem.gi1, 1)
+    g.iota(T.i24[:, :], [[1, 24]], 0, 0, **fl).then_inc(T.sem.gi1, 1)
     g.iota(T.u1[:, :], [[1, 144]], 0, 0, **fl).then_inc(T.sem.gi1, 1)
     g.iota(T.u2[:, :], [[1, 72], [0, 2]], 0, 0, **fl).then_inc(T.sem.gi1, 1)
 
     vec.memset(T.basei[:, 2040:2048], 0).then_inc(T.sem.m0, 1)
     v(vec.memset(T.pq[:, :], 0))
     v(vec.memset(T.lpf[:, :], 0.0))
-    vec.wait_ge(T.sem.gi0, 3)
-    v(ts(ci(1), ci(0), 15, Op.bitwise_and))
-    v(ts(ci(2), ci(0), 4, Op.arith_shift_right))
-    v(ts(ci(3), ci(0), 31, Op.bitwise_and))
-    v(ts(ci(4), ci(0), 1, Op.bitwise_and))
-    v(ts(ci(5), ci(0), 5, Op.arith_shift_right, 1, Op.bitwise_and))
-    v(ts(ci(6), ci(0), 6, Op.arith_shift_right))
-    vw()
-    v(vec.tensor_copy(out=cf(0), in_=ci(1)))
-    v(ts(cf(1), ci(2), 16.0, Op.mult, 15.0, Op.add))
-    v(ts(cf(2), ci(2), 8.0, Op.mult, 7.0, Op.add))
-    v(vec.tensor_copy(out=cf(3), in_=ci(3)))
-    v(vec.tensor_copy(out=cf(4), in_=ci(4)))
-    v(ts(cf(5), ci(4), -1.0, Op.mult, 1.0, Op.add))
-    v(ts(cf(6), ci(5), -1023.0, Op.mult, 1024.0, Op.add))
-    v(ts(cf(21), ci(6), -1.0, Op.mult, 1.0, Op.add))
-    v(vec.tensor_copy(out=cf(22), in_=ci(6)))
-    vw()
-    v(ts(T.e16[:, :], T.i16[:, :], cf(0), Op.is_equal))
-    v(ts(T.j24[:, :], T.i24[:, :], cf(3), Op.is_equal, cf(6), Op.mult))
-    vec.wait_ge(T.sem.gi1, 3)
+    vec.wait_ge(T.sem.gi0, 2)
     v(ts(T.pa1[:, :], T.vi[:, :], 127, Op.bitwise_and))
     v(ts(T.a0r[:, :], T.vi[:, :], 7, Op.arith_shift_right, 15, Op.bitwise_and))
     v(ts(T.v2k[:, :], T.vi[:, :], 2047, Op.bitwise_and))
     vw()
     v(ts(T.tm[:, :], T.v2k[:, :], 0.0, Op.is_equal))
     v(ts(T.pz[:, :], T.v2k[:, :], 2047.0, Op.not_equal))
-    for a in range(6):
-        v(vec.tensor_copy(out=T.lpf[:, a::16], in_=T.j24[:, a % 3::3]))
+    v(ts(ci(1), ci(0), 15, Op.bitwise_and))
+    v(ts(ci(2), ci(0), 4, Op.arith_shift_right))
+    v(ts(ci(3), ci(0), 31, Op.bitwise_and))
+    v(ts(ci(4), ci(0), 1, Op.bitwise_and))
+    v(ts(ci(5), ci(0), 5, Op.arith_shift_right, 1, Op.bitwise_and))
+    v(ts(ci(6), ci(0), 6, Op.arith_shift_right))
+    v(ts(ci(7), ci(0), 1, Op.arith_shift_right, 7, Op.bitwise_and))
     vw()
-    v(vec.tensor_tensor(out=T.pa0[:, :], in0=T.a0r[:, :], in1=T.tm[:, :], op=Op.subtract))
-    v(ts(T.lp[:, 0:128], T.lpf[:, :], cf(21), Op.mult))
-    v(ts(T.lp[:, 128:256], T.lpf[:, :], cf(22), Op.mult))
+    v(tt(T.pa0[:, :], T.a0r[:, :], T.tm[:, :], Op.subtract))
     pub("ka")
     vec.wait_ge(T.sem.dP, 64)
     for h in range(2):
@@ -188,40 +183,73 @@ def rank_program(g, core, T, topo):
         v(ts(T.pq[64 * h + 32:64 * h + 56, :], T.pin[64 * h + 32:64 * h + 56, :], 1023, Op.bitwise_and))
     vw()
     v(vec.tensor_copy(out=T.msg[:, :], in_=T.pq[:, :]))
-    pub("kmsg", "klp")
+    pub("kmsg")
     vec.wait_ge(T.sem.dW, 16)
     v(ts(T.ph[:, :], T.wt[:, :], 8, Op.arith_shift_right))
     v(ts(T.pl[:, :], T.wt[:, :], 255, Op.bitwise_and))
     pub("kw")
+    v(vec.tensor_copy(out=cf(0), in_=ci(1)))
+    v(ts(cf(1), ci(2), 16.0, Op.mult, 15.0, Op.add))
+    v(ts(cf(2), ci(2), 8.0, Op.mult, 7.0, Op.add))
+    v(vec.tensor_copy(out=cf(3), in_=ci(3)))
+    v(vec.tensor_copy(out=cf(4), in_=ci(4)))
+    v(ts(cf(5), ci(4), -1.0, Op.mult, 1.0, Op.add))
+    v(ts(cf(6), ci(5), -2046.0, Op.mult, 2048.0, Op.add))
+    v(ts(cf(21), ci(6), -1.0, Op.mult, 1.0, Op.add))
+    v(vec.tensor_copy(out=cf(22), in_=ci(6)))
+    v(ts(cf(26), ci(7), 8.0, Op.mult, 7.0, Op.add))
+    v(ts(cf(27), ci(4), -255.0 / EPS, Op.mult, 256.0 / EPS, Op.add))
+    vec.wait_ge(T.sem.gi1, 4)
+    vw()
+    v(ts(T.e16[:, :], T.i16[:, :], cf(0), Op.is_equal))
+    v(ts(T.j24[:, :], T.i24[:, :], cf(3), Op.is_equal, cf(6), Op.mult))
     vec.wait_ge(T.sem.dS, 16)
     v(ts(T.missl[:, :], T.sk[:, :], -1.0, Op.add))
     v(ts(T.hv[:, :], T.vi[:, :], -1.0, Op.add))
+    pub("ke")
+    for a in range(6):
+        v(vec.tensor_copy(out=T.lpf[:, a::16], in_=T.j24[:, a % 3::3]))
+    v(ts(T.v2k[:, :], T.hv[:, :], 2047, Op.bitwise_and))
     v(vec.tensor_reduce(out=cf(7), in_=T.e16[:, 0:3], axis=AxisListType.X, op=Op.add))
     v(vec.tensor_reduce(out=cf(8), in_=T.e16[:, 3:6], axis=AxisListType.X, op=Op.add))
-    v(ts(cf(13), T.e16[:, 10:11], 256.0, Op.mult, T.e16[:, 11:12], Op.add))
-    v(ts(cf(15), T.e16[:, 10:11], -1.0, Op.mult, 1.0, Op.add))
-    vec.wait_ge(T.sem.dN, 16)
-    v(vec.tensor_copy(out=cf(19), in_=T.n0[:, 0:1]))
+    v(vec.tensor_reduce(out=cf(17), in_=T.e16[:, 0:6], axis=AxisListType.X, op=Op.add))
+    v(ts(cf(13), ek(7), 256.0 / EPS, Op.mult))
+    v(ts(cf(15), ek(7), -1.0, Op.mult, 1.0, Op.add))
     vw()
-    v(ts(T.v2k[:, :], T.hv[:, :], 2047, Op.bitwise_and))
-    v(vec.tensor_tensor(out=cf(9), in0=cf(7), in1=cf(8), op=Op.subtract))
-    v(vec.tensor_tensor(out=cf(16), in0=cf(15), in1=T.e16[:, 11:12], op=Op.subtract))
-    v(ts(cf(17), cf(7), 300.0, Op.mult, -300.0, Op.add))
-    v(ts(cf(18), cf(7), -299.0, Op.mult, 300.0, Op.add))
-    vw()
+    v(ts(T.lp[:, 0:128], T.lpf[:, :], cf(21), Op.mult))
+    v(ts(T.lp[:, 128:256], T.lpf[:, :], cf(22), Op.mult))
     v(vec.tensor_copy(out=T.hitl[:, :], in_=T.v2k[:, :]))
-    v(ts(cf(10), cf(9), 11.0 / 64, Op.mult))
-    v(vec.tensor_tensor(out=cf(14), in0=cf(9), in1=T.e16[:, 12:13], op=Op.add))
-    v(ts(T.colb[:, 0:1], cf(8), 299.0, Op.mult, cf(17), Op.add))
-    v(ts(T.colb[:, 1:2], cf(8), -300.0, Op.mult, cf(18), Op.add))
+    v(tt(cf(9), cf(7), cf(8), Op.subtract))
+    v(tt(cf(16), cf(15), ek(15), Op.subtract))
+    v(ts(cf(10), cf(17), -EPS, Op.mult, EPS, Op.add))
+    v(ts(cf(28), cf(17), 7.0, Op.mult, 1.0, Op.add))
+    v(ts(cf(30), ek(15), 1.0 / EPS, Op.mult, cf(13), Op.add))
+    pub("klp")
+    v(ts(cf(18), cf(9), -1.0, Op.mult))
+    v(ts(cf(29), cf(9), -8.0, Op.mult))
+    v(ts(cf(11), cf(9), 11.0 / 128, Op.mult))
+    v(ts(cf(23), cf(9), -4096.0, Op.mult))
+    v(ts(cf(14), ek(10), 2.0 / EPS, Op.mult, cf(9), Op.add))
+    v(ts(cf(7), ek(6), -EPS, Op.mult, cf(10), Op.add))
+    vec.wait_ge(T.sem.dN, 16)
     vw()
-    v(ts(cf(11), T.e16[:, 9:10], 2.0, Op.mult, cf(10), Op.add))
-    v(ts(T.zw[:, :], T.u2[:, :], cf(2), Op.is_equal, cf(13), Op.mult))
+    v(ts(cf(12), cf(17), 2.0, Op.mult, cf(7), Op.add))
+    v(ts(cf(19), T.n0[:, 0:1], 16.0, Op.mult, cf(29), Op.add))
+    v(ts(cf(8), T.n0[:, 1:2], 16.0, Op.mult, cf(29), Op.add))
+    v(ts(cf(31), ek(9), 2.0 / EPS, Op.mult, cf(11), Op.add))
+    v(ts(T.zo[:, :], T.u1[:, :], cf(1), Op.is_equal, cf(23), Op.mult))
+    v(ts(T.zw[:, :], T.u2[:, :], cf(2), Op.is_equal, cf(30), Op.mult))
     v(ts(T.zq[:, :], T.u2[:, :], cf(2), Op.is_equal, cf(14), Op.mult))
+    v(ts(T.zh[:, :], T.u2[:, :], cf(26), Op.is_equal, cf(27), Op.mult))
+    vec.wait_ge(T.sem.kt, 1)
     vw()
-    v(ts(cf(12), T.e16[:, 8:9], 32.0, Op.mult, cf(11), Op.add))
-    vw()
-    v(ts(T.zx[:, :], T.u1[:, :], cf(1), Op.is_equal, cf(12), Op.mult))
+    v(tt(cf(20), cf(8), T.colt[:, 0:1], Op.add))
+    v(ts(cf(13), ek(8), 32.0 / EPS, Op.mult, cf(31), Op.add))
+    pub("kn")
+    v(ts(T.zx[:, :], T.u1[:, :], cf(1), Op.is_equal, cf(13), Op.mult))
+    for b in "AB":
+        v(vec.memset(T["h2" + b][:, :], 0.0))
+    pub("kz", "kh")
 
     dire, shar = direct(core), shares(core)
     chip_mates = topo.cores_of(core)
@@ -240,23 +268,34 @@ def rank_program(g, core, T, topo):
     g.remote_dma_fused([tr(T.msg[:, :], T.land[:, 64 * slot(d, core):64 * slot(d, core) + 64], d, dir_engs[d], "pa") for d in dire],
                        local_sem=T.sem.ls)
 
-    vec.wait_ge(T.sem.dB0, 128)
-    vec.wait_ge(T.sem.dZ, 48)
-    vec.wait_ge(T.sem.dPc, 80)
-    v(vec.tensor_copy(out=T.basef[:, 0:1024], in_=T.basei[:, 0:1024]))
-    vec.wait_ge(T.sem.dB1, 128)
-    v(vec.tensor_copy(out=T.basef[:, 1024:2048], in_=T.basei[:, 1024:2048]))
-    pub("kbase")
-    v(vec.tensor_copy(out=T.colb[:, 2:3], in_=T.basef[:, 2047:2048]))
-    v(ts(T.tab[:, 0:1], T.basef[:, 2047:2048], cf(16), Op.mult))
-    v(ts(T.tab[:, 1:2], T.basef[:, 2047:2048], cf(16), Op.mult))
-    v(ts(T.tab[:, 3:4098:2], T.basef[:, 0:2048].indirect(T.missl[:, 0:128]), cf(16), Op.mult))
-    pub("kz")
+    def first(b):
+        sca.wait_ge(T.sem["pp" + b], 8)
+        for dst, col, sem in (("C0", 19, "sx"), ("C1", 20, "sy")):
+            sca.activation(out=T[dst + b][:, :], in_=T["pp" + b][:, :], func=Fn.Tanh, bias=cf(col), scale=-8.0).then_inc(T.sem[sem + b], 1)
+
+    sca.wait_ge(T.sem.ke, 1)
+    sca.activation(out=T.colt[:, 0:1], in_=ek(8), func=Fn.Tanh, scale=EPS).then_inc(T.sem.kt, 1)
+    sca.wait_ge(T.sem.kn, 1)
+    first("A")
     sca.wait_ge(T.sem.kbase, 1)
     sca.activation(out=T.tab[:, 2:4097:2], in_=T.basef[:, 0:2048].indirect(T.hitl[:, 0:128]), func=Fn.Copy).then_inc(T.sem.ht, 1)
+    first("B")
     for b in "AB":
-        sca.wait_ge(T.sem["g" + b], 1)
         sca.activation(out=T["P" + b][:, :], in_=T["pp" + b][:, :], func=Fn.Copy).then_inc(T.sem["pc" + b], 1)
+
+    vec.wait_ge(T.sem.dB0, 128)
+    vec.wait_ge(T.sem.dZ, 64)
+    vec.wait_ge(T.sem.dPc, 80)
+    v(ts(T.basef[:, 0:1024], T.basei[:, 0:1024], cf(12), Op.mult, cf(18), Op.add))
+    vec.wait_ge(T.sem.dB1, 128)
+    v(ts(T.basef[:, 1024:2048], T.basei[:, 1024:2048], cf(12), Op.mult, cf(18), Op.add))
+    pub("kbase")
+    v(vec.tensor_copy(out=T.colb[:, 0:1], in_=T.basef[:, 2047:2048]))
+    v(vec.tensor_copy(out=T.colb[:, 1:2], in_=T.basef[:, 0:1]))
+    v(ts(T.tab[:, 0:1], T.basef[:, 2047:2048], cf(16), Op.mult))
+    v(ts(T.tab[:, 1:2], T.basef[:, 2047:2048], cf(16), Op.mult))
+    pub("kc")
+    v(ts(T.tab[:, 3:4098:2], T.basef[:, 0:2048].indirect(T.missl[:, 0:128]), cf(16), Op.mult))
 
     def spread(b, srcs):
         for r, (buf, c0) in enumerate(srcs):
@@ -264,79 +303,112 @@ def rank_program(g, core, T, topo):
                 ten.matmul(T["pp" + b][:, 256 * h + r:256 * h + 253 + r:4], T.lp[:, 128 * h:128 * h + 128],
                            T[buf][:, c0:c0 + 64], True, True).then_inc(T.sem["pp" + b], 1)
 
-    def tx(b, t):
+    def tx(b, t, z="zx"):
         for j in range(16):
-            ten.matmul(T["X" + b][:, 0:32], T.zx[:, 15 - j:143 - j], T["C%d%s" % (t % 2, b)][:, j:512:16], j == 0, j == 15).then_inc(T.sem["x" + b], 1)
+            ten.matmul(T["X" + b][:, 0:32], T[z][:, 15 - j:143 - j], T["C%d%s" % (t % 2, b)][:, j:512:16],
+                       j == 0 and t != 1, j == 15 and t != 0).then_inc(T.sem["x" + b], 1)
 
-    def tw(b, t):
+    def pairs(out, z, src, sem, start, stop):
         for p in range(8):
-            ten.matmul(T["W" + b][:, 0:64], T.zw[:, 14 - 2 * p:142 - 2 * p], T["C%d%s" % (t % 2, b)][:, 64 * p:64 * p + 64],
-                       t == 1 and p == 0, t == V - 1 and p == 7).then_inc(T.sem["w" + "ab"[t % 2] + b], 1)
+            ten.matmul(out, T[z][:, 14 - 2 * p:142 - 2 * p], T[src][:, 64 * p:64 * p + 64],
+                       start and p == 0, stop and p == 7).then_inc(T.sem[sem], 1)
 
-    def tq(b, t):
-        for p in range(8):
-            ten.matmul(T["X" + b][:, 0:64], T.zq[:, 14 - 2 * p:142 - 2 * p], T["C%d%s" % (t % 2, b)][:, 64 * p:64 * p + 64],
-                       p == 0, p == 7).then_inc(T.sem["q" + b], 1)
+    def start(b):
+        for t, sem in ((0, "sx"), (1, "sy")):
+            ten.wait_ge(T.sem[sem + b], 1)
+            tx(b, t, "zo" if t == 0 else "zx")
+        o = 8 if b == "A" else 72
+        pairs(T.psm[:, o:o + 64], "zq", "C0" + b, "qo" + b, True, True)
 
-    nd = len(dire)
+    nd, nx = len(dire), len(cross(core))
+    ten.wait_ge(T.sem.kmsg, 1)
     ten.wait_ge(T.sem.klp, 1)
     ten.wait_ge(T.sem.pa, 4 * nd)
     spread("A", [("msg", 0)] + [("land", 64 * i) for i in range(nd)])
     ten.wait_ge(T.sem.kz, 1)
+    start("A")
+    ten.wait_ge(T.sem.pb, 4 * nx)
+    spread("B", [("land", 64 * (nd + i)) for i in range(nx)])
+    start("B")
+    ten.wait_ge(T.sem.kc, 1)
     for p in range(8):
-        ten.matmul(T.psm[:, 0:1], T.zw[:, 14 - 2 * p:142 - 2 * p], T.colb[:, 2:3], p == 0, p == 7).then_inc(T.sem.w47, 1)
-    ten.wait_ge(T.sem.pb, 4 * len(cross(core)))
-    spread("B", [("land", 64 * (nd + i)) for i in range(len(cross(core)))])
-    for t in range(V):
+        ten.matmul(T.psm[:, 0:2], T.zw[:, 14 - 2 * p:142 - 2 * p], T.colb[:, 0:2], p == 0, p == 7).then_inc(T.sem.w47, 1)
+    for t in range(2, V):
         for b in "AB":
-            ten.wait_ge(T.sem["c" + b], t + 1)
+            W, c = T["W" + b][:, 0:64], "C%d%s" % (t % 2, b)
+            ten.wait_ge(T.sem["c" + b], t - 1)
+            ten.wait_ge(T.sem["s" + b], t - 1)
             if t < V - 1:
                 tx(b, t)
-            if t > 0:
-                tw(b, t)
+            if t == 11:
+                ten.wait_ge(T.sem["hx" + b], 64)
+                ten.wait_ge(T.sem["hy" + b], 64)
+                pairs(W, "zh", "h1" + b, "wb" + b, True, False)
+            if t == 12:
+                pairs(W, "zw", c, "wa" + b, False, False)
+            if t == 13:
+                pairs(W, "zw", c, "wb" + b, False, False)
+                ten.wait_ge(T.sem["hz" + b], 16)
+                ten.wait_ge(T.sem["hw" + b], 16)
+                pairs(W, "zh", "h2" + b, "wb" + b, False, False)
             if t == V - 1:
-                tq(b, t)
+                pairs(T["X" + b][:, 0:64], "zq", c, "q" + b, True, True)
+                pairs(W, "zw", c, "wb" + b, False, True)
 
-    def clamp(b, t):
-        ts(T["C%d%s" % (t % 2, b)][:, :], T["D" + b][:, :], T.colb[:, 0:1], Op.max, T.colb[:, 1:2], Op.min).then_inc(T.sem["c" + b], 1)
-
-    for b in "AB":
-        vec.wait_ge(T.sem["pp" + b], 8)
-        ts(T["D" + b][:, :], T["pp" + b][:, :], -1.0, Op.mult, cf(19), Op.add).then_inc(T.sem["g" + b], 1)
-        vec.wait_ge(T.sem["g" + b], 1)
-        clamp(b, 0)
-    vec.wait_ge(T.sem.w47, 8)
-    v(vec.tensor_copy(out=cf(20), in_=T.psm[:, 0:1]))
-    vec.wait_ge(T.sem.ht, 1)
-    for t in range(1, V):
+    syn.wait_ge(T.sem.kh, 1)
+    for t in list(H1) + list(H2):
         for b in "AB":
+            syn.wait_ge(T.sem["c" + b], t - 1)
+            syn.wait_ge(T.sem["s" + b], t - 1)
+            dst, k, sem = ("h1", t - H1[0], "hx" if t % 2 == 0 else "hy") if t in H1 else ("h2", t - H2[0], "hz" if t % 2 == 0 else "hw")
+            syn.dma_start(out=T[dst + b][16 * k:16 * k + 16, :], in_=T["C%d%s" % (t % 2, b)][7::8, :]).then_inc(T.sem[sem + b], 16)
+
+    vw()
+    vec.wait_ge(T.sem.ht, 1)
+    for t in range(2, V):
+        if t == 4:
+            vec.wait_ge(T.sem.w47, 8)
+            v(vec.tensor_copy(out=T.colf[:, 24:26], in_=T.psm[:, 0:2]))
+            vw()
+            v(ts(T.t0A[:, :], T.psm[:, 8:72], -5.0, Op.is_lt, cf(25), Op.mult))
+            v(ts(T.t0B[:, :], T.psm[:, 72:136], -5.0, Op.is_lt, cf(25), Op.mult))
+        for b in "AB":
+            D, C = T["D" + b], T["C%d%s" % (t % 2, b)]
+            if t == 2:
+                vec.wait_ge(T.sem["qo" + b], 8)
+            elif t - 2 in H1:
+                vec.wait_ge(T.sem[("hx" if t % 2 == 0 else "hy") + b], 16 * ((t - 2) // 2))
+            elif t - 2 in H2:
+                vec.wait_ge(T.sem[("hz" if t % 2 == 0 else "hw") + b], 16)
+            elif t == 14:
+                vec.wait_ge(T.sem["wa" + b], 8)
             vec.wait_ge(T.sem["x" + b], 16 * t)
-            ts(T["off" + b][:, :], T["X" + b][:, 0:32], 2.4375, Op.add).then_inc(T.sem["o" + b], 1)
-            if t == 1:
+            ts(T["off" + b][:, :], T["X" + b][:, 0:32], 2.953125 - (24576.0 if t == 2 else 0.0), Op.add).then_inc(T.sem["o" + b], 1)
+            if t == 2:
                 vec.wait_ge(T.sem["pc" + b], 1)
-            vec.wait_ge(T.sem["o" + b], t)
-            vec.tensor_tensor(out=T["D" + b][:, :], in0=T.tab[:, 0:4098].indirect(T["off" + b][:, 0:32]), in1=T["P" + b][:, :],
-                              op=Op.subtract).then_inc(T.sem["g" + b], 1)
-            if t > 2:
-                vec.wait_ge(T.sem["w" + "ab"[t % 2] + b], 8 * ((t - 1) // 2))
-            vec.wait_ge(T.sem["g" + b], t + 1)
-            clamp(b, t)
+            vec.wait_ge(T.sem["o" + b], t - 1)
+            tt(D[:, :], T.tab[:, 0:4098].indirect(T["off" + b][:, 0:32]), T["P" + b][:, :], Op.subtract).then_inc(T.sem["g" + b], 1)
+            vec.wait_ge(T.sem["g" + b], t - 1)
+            ts(C[:, 0:VC], D[:, 0:VC], 1.0, Op.min, -1.0, Op.max).then_inc(T.sem["c" + b], 1)
+            sca.wait_ge(T.sem["g" + b], t - 1)
+            sca.activation(out=C[:, VC:512], in_=D[:, VC:512], func=Fn.Tanh, scale=cf(28)).then_inc(T.sem["s" + b], 1)
 
     for b in "AB":
-        vec.wait_ge(T.sem["wa" + b], 8 * ((V - 1) // 2))
-        vec.wait_ge(T.sem["wb" + b], 8 * (V // 2))
+        t1, t2, t3, t4 = [T[n + b] for n in ("t1", "t2", "t3", "t4")]
         vec.wait_ge(T.sem["q" + b], 8)
+        v(ts(t1[:, :], T["X" + b][:, 0:64], -5.0, Op.is_lt, cf(24), Op.mult))
         vw()
-        v(ts(T["t1" + b][:, :], T["X" + b][:, 0:64], 0.5, Op.is_lt, cf(20), Op.mult))
+        v(tt(t4[:, :], t1[:, :], T["t0" + b][:, :], Op.add))
+        vec.wait_ge(T.sem["wb" + b], 32)
         vw()
-        v(vec.tensor_tensor(out=T["t2" + b][:, :], in0=T["W" + b][:, 0:64], in1=T["t1" + b][:, :], op=Op.add))
+        v(tt(t2[:, :], T["W" + b][:, 0:64], t4[:, :], Op.add))
         vw()
-        v(ts(T["t3" + b][:, 0:32], T["t2" + b][:, 0:32], cf(5), Op.mult))
-        v(ts(T["t3" + b][:, 32:64], T["t2" + b][:, 32:64], cf(4), Op.mult))
+        v(ts(t3[:, 0:32], t2[:, 0:32], cf(5), Op.mult))
+        v(ts(t3[:, 32:64], t2[:, 32:64], cf(4), Op.mult))
         vw()
         for r in range(4):
             out = T.rland[:, 0:8] if (b == "A" and r == 0) else T["R" + b][:, 8 * r:8 * r + 8]
-            v(vec.tensor_tensor(out=out, in0=T["t3" + b][:, r:32:4], in1=T["t3" + b][:, 32 + r:64:4], op=Op.add))
+            v(tt(out, t3[:, r:32:4], t3[:, 32 + r:64:4], Op.add))
         pub("kr" + b)
     g.wait_ge(T.sem.krA, 1)
     g.remote_dma_fused([tr(T.RA[:, 8 * i + 8:8 * i + 16], T.rland[:, 8 * slot(d, core) + 8:8 * slot(d, core) + 16], d, dir_engs[d], "rs")
@@ -345,11 +417,11 @@ def rank_program(g, core, T, topo):
     g.remote_dma_fused([tr(T.RB[:, 16 * i:16 * i + 16], T.rres[:, :], rel, rel_engs[i], "rr") for i, (rel, _) in enumerate(shar)],
                        local_sem=T.sem.ls)
     vec.wait_ge(T.sem.rs, 4 * 7)
-    v(vec.tensor_tensor(out=T.s32[:, :], in0=T.rland[:, 0:32], in1=T.rland[:, 32:64], op=Op.add))
+    v(tt(T.s32[:, :], T.rland[:, 0:32], T.rland[:, 32:64], Op.add))
     vw()
-    v(vec.tensor_tensor(out=T.s16[:, :], in0=T.s32[:, 0:16], in1=T.s32[:, 16:32], op=Op.add))
+    v(tt(T.s16[:, :], T.s32[:, 0:16], T.s32[:, 16:32], Op.add))
     vw()
-    v(vec.tensor_tensor(out=T.ysum[:, :], in0=T.s16[:, 0:8], in1=T.s16[:, 8:16], op=Op.add))
+    v(tt(T.ysum[:, :], T.s16[:, 0:8], T.s16[:, 8:16], Op.add))
     pub("ys")
     syn.wait_ge(T.sem.ys, 1)
     syn.dma_start(out=T.y[:, :], in_=T.ysum[:, :]).then_inc(T.sem.dY, 16)

@@ -14,7 +14,7 @@ SCRATCH = {
     "u1": ("sbuf", [128, 144], "float32"), "u2": ("sbuf", [128, 144], "float32"),
     "e16": ("sbuf", [128, 16], "float32"), "j24": ("sbuf", [128, 24], "float32"),
     "lpf": ("sbuf", [128, 128], "float32"), "lp": ("sbuf", [128, 256], "float16"),
-    "zx": ("sbuf", [128, 144], "bfloat16"), "zo": ("sbuf", [128, 144], "bfloat16"), "zw": ("sbuf", [128, 144], "bfloat16"),
+    "zx": ("sbuf", [128, 144], "bfloat16"), "zw": ("sbuf", [128, 144], "bfloat16"),
     "zq": ("sbuf", [128, 144], "bfloat16"), "zh": ("sbuf", [128, 144], "bfloat16"),
     "sk": ("sbuf", [128, 128], "int32"), "wt": ("sbuf", [128, 128], "int32"), "n0": ("sbuf", [128, 8], "int32"),
     "pa1": ("sbuf", [128, 128], "int32"), "pa0": ("sbuf", [128, 128], "int32"), "pz": ("sbuf", [128, 128], "int32"),
@@ -29,17 +29,17 @@ SCRATCH = {
 }
 SEMAPHORES = ["vc", "gi0", "gi1", "m0", "dP", "dS", "dW", "dN", "dB0", "dB1", "dZ", "dPc", "dY",
               "kmsg", "klp", "kz", "ka", "kw", "kbase", "kc", "kn", "kh", "ke", "kt", "ht", "w47", "ys",
-              "pa", "pb", "rs", "rm", "rr", "ls", "rl"]
+              "pa0", "pa1", "pa2", "pb0", "pb1", "pb2", "pb3", "rs", "rm", "rr", "ls", "rl"]
 for _b in "AB":
     SCRATCH.update({
         "off" + _b: ("sbuf", [128, 32], "uint16"), "P" + _b: ("sbuf", [128, 512], "float32"), "D" + _b: ("sbuf", [128, 512], "bfloat16"),
-        "C0" + _b: ("sbuf", [128, 512], "bfloat16"), "C1" + _b: ("sbuf", [128, 512], "bfloat16"),
+        "C0" + _b: ("sbuf", [128, 512], "bfloat16"), "C1" + _b: ("sbuf", [128, 512], "bfloat16"), "F" + _b: ("sbuf", [128, 512], "bfloat16"),
         "h1" + _b: ("sbuf", [128, 512], "bfloat16"), "h2" + _b: ("sbuf", [128, 512], "bfloat16"),
-        "R" + _b: ("sbuf", [128, 32], "float32"), "t0" + _b: ("sbuf", [128, 64], "float32"), "t1" + _b: ("sbuf", [128, 64], "float32"),
+        "R" + _b: ("sbuf", [128, 32], "float32"), "fm" + _b: ("sbuf", [128, 64], "float32"), "t1" + _b: ("sbuf", [128, 64], "float32"),
         "t2" + _b: ("sbuf", [128, 64], "float32"), "t3" + _b: ("sbuf", [128, 64], "float32"), "t4" + _b: ("sbuf", [128, 64], "float32"),
         "pp" + _b: ("psum", [128, 512], "float32"), "X" + _b: ("psum", [128, 64], "float32"), "W" + _b: ("psum", [128, 64], "float32"),
     })
-    SEMAPHORES += [k + _b for k in ("pp", "pc", "sx", "sy", "g", "c", "s", "o", "x", "wa", "wb", "qo", "q", "kr", "hx", "hy", "hz", "hw")]
+    SEMAPHORES += [k + _b for k in ("pp", "pc", "sy", "f", "g", "c", "s", "o", "x", "wa", "wb", "qo", "q", "kr", "hx", "hy", "hz", "hw")]
 
 
 def mask_of(engs):
@@ -79,9 +79,9 @@ def rank_program(g, core, T, topo):
                     continue
                 engs = [topo.engines(core, d)[4 * i:4 * i + 4] for i, d in enumerate(dests)]
                 g.wait_ge(T.sem.rm, 4)
-                g.remote_dma_fused([tr(T.rmsg[:, :], T.land[:, 64 * slot(d, c):64 * slot(d, c) + 64], d, engs[i], "pb")
-                                    for i, d in enumerate(dests)], local_sem=T.sem.rl)
-                g.wait_ge(T.sem.rr, 4)
+                g.remote_dma_fused([tr(T.rmsg[:, :], T.land[:, 64 * slot(d, c):64 * slot(d, c) + 64], d, engs[i],
+                                       "pb%d" % cross(d).index(c)) for i, d in enumerate(dests)], local_sem=T.sem.rl)
+                g.wait_ge(T.sem.rr, 8)
                 g.remote_dma_fused([tr(T.rres[:, 8 * i:8 * i + 8], T.rland[:, 8 * slot(d, c) + 8:8 * slot(d, c) + 16], d, engs[i], "rs")
                                     for i, d in enumerate(dests)], local_sem=T.sem.rl)
                 g.wait_ge(T.sem.rl, 16)
@@ -122,7 +122,7 @@ def rank_program(g, core, T, topo):
     for h in range(2):
         q = syn if h == 0 else sca
         for lo in range(2):
-            k = 64 * h + 32 * lo
+            k = 64 * lo + 24 * h
             q.dma_start(out=T.pin[k:k + 24, :], in_=T.pts[:, 64 * h:64 * h + 64]).then_inc(T.sem.dP, 16)
     syn.dma_start(out=T.wt[:, :], in_=T.nodes[7::16, :]).then_inc(T.sem.dW, 16)
     sca.dma_start(out=T.sk[:, :], in_=T.nodes[6::16, :]).then_inc(T.sem.dS, 16)
@@ -169,21 +169,18 @@ def rank_program(g, core, T, topo):
     v(ts(T.pz[:, :], T.v2k[:, :], 2047.0, Op.not_equal))
     v(ts(ci(1), ci(0), 15, Op.bitwise_and))
     v(ts(ci(2), ci(0), 4, Op.arith_shift_right))
-    v(ts(ci(3), ci(0), 31, Op.bitwise_and))
+    v(ts(ci(3), ci(0), 63, Op.bitwise_and))
     v(ts(ci(4), ci(0), 1, Op.bitwise_and))
-    v(ts(ci(5), ci(0), 5, Op.arith_shift_right, 1, Op.bitwise_and))
     v(ts(ci(6), ci(0), 6, Op.arith_shift_right))
     v(ts(ci(7), ci(0), 1, Op.arith_shift_right, 7, Op.bitwise_and))
     vw()
     v(tt(T.pa0[:, :], T.a0r[:, :], T.tm[:, :], Op.subtract))
     pub("ka")
     vec.wait_ge(T.sem.dP, 64)
-    for h in range(2):
-        v(ts(T.pq[64 * h:64 * h + 24, :], T.pin[64 * h:64 * h + 24, :], 10, Op.arith_shift_right))
-        v(ts(T.pq[64 * h + 32:64 * h + 56, :], T.pin[64 * h + 32:64 * h + 56, :], 1023, Op.bitwise_and))
+    v(ts(T.pq[0:48, :], T.pin[0:48, :], 10, Op.arith_shift_right))
+    v(ts(T.pq[64:112, :], T.pin[64:112, :], 1023, Op.bitwise_and))
     vw()
-    v(vec.tensor_copy(out=T.msg[:, :], in_=T.pq[:, :]))
-    pub("kmsg")
+    vec.tensor_copy(out=T.msg[:, :], in_=T.pq[:, :]).then_inc(T.sem.kmsg, 1)
     vec.wait_ge(T.sem.dW, 16)
     v(ts(T.ph[:, :], T.wt[:, :], 8, Op.arith_shift_right))
     v(ts(T.pl[:, :], T.wt[:, :], 255, Op.bitwise_and))
@@ -191,24 +188,23 @@ def rank_program(g, core, T, topo):
     v(vec.tensor_copy(out=cf(0), in_=ci(1)))
     v(ts(cf(1), ci(2), 16.0, Op.mult, 15.0, Op.add))
     v(ts(cf(2), ci(2), 8.0, Op.mult, 7.0, Op.add))
-    v(vec.tensor_copy(out=cf(3), in_=ci(3)))
+    v(vec.tensor_copy(out=cf(31), in_=ci(3)))
     v(vec.tensor_copy(out=cf(4), in_=ci(4)))
     v(ts(cf(5), ci(4), -1.0, Op.mult, 1.0, Op.add))
-    v(ts(cf(6), ci(5), -2046.0, Op.mult, 2048.0, Op.add))
-    v(ts(cf(21), ci(6), -1.0, Op.mult, 1.0, Op.add))
-    v(vec.tensor_copy(out=cf(22), in_=ci(6)))
+    v(ts(cf(6), ci(6), -2046.0, Op.mult, 2048.0, Op.add))
+    v(ts(cf(22), ci(3), 23.5, Op.is_ge))
+    v(ts(cf(21), ci(3), 23.5, Op.is_lt))
     v(ts(cf(26), ci(7), 8.0, Op.mult, 7.0, Op.add))
     v(ts(cf(27), ci(4), -255.0 / EPS, Op.mult, 256.0 / EPS, Op.add))
     vec.wait_ge(T.sem.gi1, 4)
     vw()
     v(ts(T.e16[:, :], T.i16[:, :], cf(0), Op.is_equal))
-    v(ts(T.j24[:, :], T.i24[:, :], cf(3), Op.is_equal, cf(6), Op.mult))
+    v(ts(cf(3), cf(22), -24.0, Op.mult, cf(31), Op.add))
     vec.wait_ge(T.sem.dS, 16)
     v(ts(T.missl[:, :], T.sk[:, :], -1.0, Op.add))
     v(ts(T.hv[:, :], T.vi[:, :], -1.0, Op.add))
     pub("ke")
-    for a in range(6):
-        v(vec.tensor_copy(out=T.lpf[:, a::16], in_=T.j24[:, a % 3::3]))
+    v(ts(T.j24[:, :], T.i24[:, :], cf(3), Op.is_equal, cf(6), Op.mult))
     v(ts(T.v2k[:, :], T.hv[:, :], 2047, Op.bitwise_and))
     v(vec.tensor_reduce(out=cf(7), in_=T.e16[:, 0:3], axis=AxisListType.X, op=Op.add))
     v(vec.tensor_reduce(out=cf(8), in_=T.e16[:, 3:6], axis=AxisListType.X, op=Op.add))
@@ -216,28 +212,28 @@ def rank_program(g, core, T, topo):
     v(ts(cf(13), ek(7), 256.0 / EPS, Op.mult))
     v(ts(cf(15), ek(7), -1.0, Op.mult, 1.0, Op.add))
     vw()
-    v(ts(T.lp[:, 0:128], T.lpf[:, :], cf(21), Op.mult))
-    v(ts(T.lp[:, 128:256], T.lpf[:, :], cf(22), Op.mult))
+    for a in range(6):
+        v(vec.tensor_copy(out=T.lpf[:, a::16], in_=T.j24[:, a % 3::3]))
     v(vec.tensor_copy(out=T.hitl[:, :], in_=T.v2k[:, :]))
     v(tt(cf(9), cf(7), cf(8), Op.subtract))
     v(tt(cf(16), cf(15), ek(15), Op.subtract))
     v(ts(cf(10), cf(17), -EPS, Op.mult, EPS, Op.add))
     v(ts(cf(28), cf(17), 7.0, Op.mult, 1.0, Op.add))
     v(ts(cf(30), ek(15), 1.0 / EPS, Op.mult, cf(13), Op.add))
-    pub("klp")
+    vw()
+    v(ts(T.lp[:, 0:128], T.lpf[:, :], cf(21), Op.mult))
+    v(ts(T.lp[:, 128:256], T.lpf[:, :], cf(22), Op.mult))
     v(ts(cf(18), cf(9), -1.0, Op.mult))
     v(ts(cf(29), cf(9), -8.0, Op.mult))
     v(ts(cf(11), cf(9), 11.0 / 128, Op.mult))
-    v(ts(cf(23), cf(9), -4096.0, Op.mult))
     v(ts(cf(14), ek(10), 2.0 / EPS, Op.mult, cf(9), Op.add))
     v(ts(cf(7), ek(6), -EPS, Op.mult, cf(10), Op.add))
+    pub("klp")
     vec.wait_ge(T.sem.dN, 16)
-    vw()
     v(ts(cf(12), cf(17), 2.0, Op.mult, cf(7), Op.add))
     v(ts(cf(19), T.n0[:, 0:1], 16.0, Op.mult, cf(29), Op.add))
     v(ts(cf(8), T.n0[:, 1:2], 16.0, Op.mult, cf(29), Op.add))
     v(ts(cf(31), ek(9), 2.0 / EPS, Op.mult, cf(11), Op.add))
-    v(ts(T.zo[:, :], T.u1[:, :], cf(1), Op.is_equal, cf(23), Op.mult))
     v(ts(T.zw[:, :], T.u2[:, :], cf(2), Op.is_equal, cf(30), Op.mult))
     v(ts(T.zq[:, :], T.u2[:, :], cf(2), Op.is_equal, cf(14), Op.mult))
     v(ts(T.zh[:, :], T.u2[:, :], cf(26), Op.is_equal, cf(27), Op.mult))
@@ -257,6 +253,7 @@ def rank_program(g, core, T, topo):
     wide = topo.engines(core, shar[0][0])
     n_on = len(wide) // 2
     rel_engs = [wide[n_on + 4 * i:n_on + 4 * i + 4] for i in range(len(shar))]
+    res_engs = [wide[8 * i:8 * i + 8] for i in range(len(shar))]
     dir_engs, k = {}, 0
     for d in dire:
         if d in chip_mates:
@@ -265,81 +262,78 @@ def rank_program(g, core, T, topo):
             dir_engs[d] = topo.engines(core, d)[4 * k:4 * k + 4]
             k += 1
     g.remote_dma_fused([tr(T.msg[:, :], T.rmsg[:, :], rel, rel_engs[i], "rm") for i, (rel, _) in enumerate(shar)], local_sem=T.sem.ls)
-    g.remote_dma_fused([tr(T.msg[:, :], T.land[:, 64 * slot(d, core):64 * slot(d, core) + 64], d, dir_engs[d], "pa") for d in dire],
-                       local_sem=T.sem.ls)
+    g.remote_dma_fused([tr(T.msg[:, :], T.land[:, 64 * slot(d, core):64 * slot(d, core) + 64], d, dir_engs[d],
+                           "pa%d" % direct(d).index(core)) for d in dire], local_sem=T.sem.ls)
 
     def first(b):
         sca.wait_ge(T.sem["pp" + b], 8)
-        for dst, col, sem in (("C0", 19, "sx"), ("C1", 20, "sy")):
-            sca.activation(out=T[dst + b][:, :], in_=T["pp" + b][:, :], func=Fn.Tanh, bias=cf(col), scale=-8.0).then_inc(T.sem[sem + b], 1)
+        sca.activation(out=T["C1" + b][:, :], in_=T["pp" + b][:, :], func=Fn.Tanh, bias=cf(20), scale=-8.0).then_inc(T.sem["sy" + b], 1)
+        sca.activation(out=T["P" + b][:, :], in_=T["pp" + b][:, :], func=Fn.Copy).then_inc(T.sem["pc" + b], 1)
 
     sca.wait_ge(T.sem.ke, 1)
     sca.activation(out=T.colt[:, 0:1], in_=ek(8), func=Fn.Tanh, scale=EPS).then_inc(T.sem.kt, 1)
     sca.wait_ge(T.sem.kn, 1)
     first("A")
-    sca.wait_ge(T.sem.kbase, 1)
+    sca.wait_ge(T.sem.kbase, 2)
     sca.activation(out=T.tab[:, 2:4097:2], in_=T.basef[:, 0:2048].indirect(T.hitl[:, 0:128]), func=Fn.Copy).then_inc(T.sem.ht, 1)
     first("B")
-    for b in "AB":
-        sca.activation(out=T["P" + b][:, :], in_=T["pp" + b][:, :], func=Fn.Copy).then_inc(T.sem["pc" + b], 1)
 
     vec.wait_ge(T.sem.dB0, 128)
     vec.wait_ge(T.sem.dZ, 64)
     vec.wait_ge(T.sem.dPc, 80)
-    v(ts(T.basef[:, 0:1024], T.basei[:, 0:1024], cf(12), Op.mult, cf(18), Op.add))
+    ts(T.basef[:, 0:1024], T.basei[:, 0:1024], cf(12), Op.mult, cf(18), Op.add).then_inc(T.sem.kbase, 1)
     vec.wait_ge(T.sem.dB1, 128)
-    v(ts(T.basef[:, 1024:2048], T.basei[:, 1024:2048], cf(12), Op.mult, cf(18), Op.add))
-    pub("kbase")
+    ts(T.basef[:, 1024:2048], T.basei[:, 1024:2048], cf(12), Op.mult, cf(18), Op.add).then_inc(T.sem.kbase, 1)
+    vec.wait_ge(T.sem.kbase, 2)
+    v(ts(T.tab[:, 3:4098:2], T.basef[:, 0:2048].indirect(T.missl[:, 0:128]), cf(16), Op.mult))
     v(vec.tensor_copy(out=T.colb[:, 0:1], in_=T.basef[:, 2047:2048]))
     v(vec.tensor_copy(out=T.colb[:, 1:2], in_=T.basef[:, 0:1]))
     v(ts(T.tab[:, 0:1], T.basef[:, 2047:2048], cf(16), Op.mult))
     v(ts(T.tab[:, 1:2], T.basef[:, 2047:2048], cf(16), Op.mult))
     pub("kc")
-    v(ts(T.tab[:, 3:4098:2], T.basef[:, 0:2048].indirect(T.missl[:, 0:128]), cf(16), Op.mult))
 
     def spread(b, srcs):
-        for r, (buf, c0) in enumerate(srcs):
+        for r, (buf, c0, sem, n) in enumerate(srcs):
+            ten.wait_ge(T.sem[sem], n)
             for h in range(2):
                 ten.matmul(T["pp" + b][:, 256 * h + r:256 * h + 253 + r:4], T.lp[:, 128 * h:128 * h + 128],
                            T[buf][:, c0:c0 + 64], True, True).then_inc(T.sem["pp" + b], 1)
 
-    def tx(b, t, z="zx"):
+    def tx(b, t):
         for j in range(16):
-            ten.matmul(T["X" + b][:, 0:32], T[z][:, 15 - j:143 - j], T["C%d%s" % (t % 2, b)][:, j:512:16],
-                       j == 0 and t != 1, j == 15 and t != 0).then_inc(T.sem["x" + b], 1)
+            ten.matmul(T["X" + b][:, 0:32], T.zx[:, 15 - j:143 - j], T["C%d%s" % (t % 2, b)][:, j:512:16],
+                       j == 0, j == 15).then_inc(T.sem["x" + b], 1)
 
     def pairs(out, z, src, sem, start, stop):
         for p in range(8):
             ten.matmul(out, T[z][:, 14 - 2 * p:142 - 2 * p], T[src][:, 64 * p:64 * p + 64],
                        start and p == 0, stop and p == 7).then_inc(T.sem[sem], 1)
 
-    def start(b):
-        for t, sem in ((0, "sx"), (1, "sy")):
-            ten.wait_ge(T.sem[sem + b], 1)
-            tx(b, t, "zo" if t == 0 else "zx")
-        o = 8 if b == "A" else 72
-        pairs(T.psm[:, o:o + 64], "zq", "C0" + b, "qo" + b, True, True)
-
     nd, nx = len(dire), len(cross(core))
-    ten.wait_ge(T.sem.kmsg, 1)
     ten.wait_ge(T.sem.klp, 1)
-    ten.wait_ge(T.sem.pa, 4 * nd)
-    spread("A", [("msg", 0)] + [("land", 64 * i) for i in range(nd)])
+    spread("A", [("msg", 0, "kmsg", 1)] + [("land", 64 * i, "pa%d" % i, 4) for i in range(nd)])
     ten.wait_ge(T.sem.kz, 1)
-    start("A")
-    ten.wait_ge(T.sem.pb, 4 * nx)
-    spread("B", [("land", 64 * (nd + i)) for i in range(nx)])
-    start("B")
-    ten.wait_ge(T.sem.kc, 1)
-    for p in range(8):
-        ten.matmul(T.psm[:, 0:2], T.zw[:, 14 - 2 * p:142 - 2 * p], T.colb[:, 0:2], p == 0, p == 7).then_inc(T.sem.w47, 1)
+    ten.wait_ge(T.sem.syA, 1)
+    tx("A", 1)
+    spread("B", [("land", 64 * (nd + i), "pb%d" % i, 4) for i in range(nx)])
+    ten.wait_ge(T.sem.syB, 1)
+    tx("B", 1)
     for t in range(2, V):
         for b in "AB":
             W, c = T["W" + b][:, 0:64], "C%d%s" % (t % 2, b)
             ten.wait_ge(T.sem["c" + b], t - 1)
-            ten.wait_ge(T.sem["s" + b], t - 1)
+            if t > 2 or b == "B":
+                ten.wait_ge(T.sem["s" + b], t - 1 if b == "B" else t - 2)
             if t < V - 1:
                 tx(b, t)
+            if t == 3 and b == "A":
+                ten.wait_ge(T.sem.kc, 1)
+                for p in range(8):
+                    ten.matmul(T.psm[:, 0:2], T.zw[:, 14 - 2 * p:142 - 2 * p], T.colb[:, 0:2], p == 0, p == 7).then_inc(T.sem.w47, 1)
+            if t == 8:
+                ten.wait_ge(T.sem["f" + b], 4)
+                o = 8 if b == "A" else 72
+                pairs(T.psm[:, o:o + 64], "zq", "F" + b, "qo" + b, True, True)
             if t == 11:
                 ten.wait_ge(T.sem["hx" + b], 64)
                 ten.wait_ge(T.sem["hy" + b], 64)
@@ -359,71 +353,74 @@ def rank_program(g, core, T, topo):
     for t in list(H1) + list(H2):
         for b in "AB":
             syn.wait_ge(T.sem["c" + b], t - 1)
-            syn.wait_ge(T.sem["s" + b], t - 1)
+            if t > 2 or b == "B":
+                syn.wait_ge(T.sem["s" + b], t - 1 if b == "B" else t - 2)
             dst, k, sem = ("h1", t - H1[0], "hx" if t % 2 == 0 else "hy") if t in H1 else ("h2", t - H2[0], "hz" if t % 2 == 0 else "hw")
             syn.dma_start(out=T[dst + b][16 * k:16 * k + 16, :], in_=T["C%d%s" % (t % 2, b)][7::8, :]).then_inc(T.sem[sem + b], 16)
 
-    vw()
     vec.wait_ge(T.sem.ht, 1)
     for t in range(2, V):
-        if t == 4:
-            vec.wait_ge(T.sem.w47, 8)
+        if t == 10:
+            for sem in ("w47", "qoA", "qoB"):
+                vec.wait_ge(T.sem[sem], 8)
             v(vec.tensor_copy(out=T.colf[:, 24:26], in_=T.psm[:, 0:2]))
-            vw()
-            v(ts(T.t0A[:, :], T.psm[:, 8:72], -5.0, Op.is_lt, cf(25), Op.mult))
-            v(ts(T.t0B[:, :], T.psm[:, 72:136], -5.0, Op.is_lt, cf(25), Op.mult))
+            for b, o in (("A", 8), ("B", 72)):
+                v(ts(T["fm" + b][:, 0:32], T.psm[:, o:o + 32], -5.0, Op.is_lt, cf(5), Op.mult))
+                v(ts(T["fm" + b][:, 32:64], T.psm[:, o + 32:o + 64], -5.0, Op.is_lt, cf(4), Op.mult))
         for b in "AB":
             D, C = T["D" + b], T["C%d%s" % (t % 2, b)]
-            if t == 2:
-                vec.wait_ge(T.sem["qo" + b], 8)
-            elif t - 2 in H1:
+            if t - 2 in H1:
                 vec.wait_ge(T.sem[("hx" if t % 2 == 0 else "hy") + b], 16 * ((t - 2) // 2))
             elif t - 2 in H2:
                 vec.wait_ge(T.sem[("hz" if t % 2 == 0 else "hw") + b], 16)
             elif t == 14:
                 vec.wait_ge(T.sem["wa" + b], 8)
-            vec.wait_ge(T.sem["x" + b], 16 * t)
-            ts(T["off" + b][:, :], T["X" + b][:, 0:32], 2.953125 - (24576.0 if t == 2 else 0.0), Op.add).then_inc(T.sem["o" + b], 1)
             if t == 2:
                 vec.wait_ge(T.sem["pc" + b], 1)
+            vec.wait_ge(T.sem["x" + b], 16 * (t - 1))
+            ts(T["off" + b][:, :], T["X" + b][:, 0:32], 2.953125, Op.add).then_inc(T.sem["o" + b], 1)
             vec.wait_ge(T.sem["o" + b], t - 1)
             tt(D[:, :], T.tab[:, 0:4098].indirect(T["off" + b][:, 0:32]), T["P" + b][:, :], Op.subtract).then_inc(T.sem["g" + b], 1)
             vec.wait_ge(T.sem["g" + b], t - 1)
-            ts(C[:, 0:VC], D[:, 0:VC], 1.0, Op.min, -1.0, Op.max).then_inc(T.sem["c" + b], 1)
-            sca.wait_ge(T.sem["g" + b], t - 1)
-            sca.activation(out=C[:, VC:512], in_=D[:, VC:512], func=Fn.Tanh, scale=cf(28)).then_inc(T.sem["s" + b], 1)
+            n = 512 if t == 2 and b == "A" else VC
+            ts(C[:, 0:n], D[:, 0:n], 1.0, Op.min, -1.0, Op.max).then_inc(T.sem["c" + b], 1)
+            if n == VC:
+                sca.wait_ge(T.sem["g" + b], t - 1)
+                sca.activation(out=C[:, VC:512], in_=D[:, VC:512], func=Fn.Tanh, scale=cf(28)).then_inc(T.sem["s" + b], 1)
+            if 3 <= t < 7:
+                a = 128 * (t - 3)
+                sca.activation(out=T["F" + b][:, a:a + 128], in_=T["pp" + b][:, a:a + 128], func=Fn.Tanh, bias=cf(19),
+                               scale=-8.0).then_inc(T.sem["f" + b], 1)
 
     for b in "AB":
         t1, t2, t3, t4 = [T[n + b] for n in ("t1", "t2", "t3", "t4")]
         vec.wait_ge(T.sem["q" + b], 8)
         v(ts(t1[:, :], T["X" + b][:, 0:64], -5.0, Op.is_lt, cf(24), Op.mult))
         vw()
-        v(tt(t4[:, :], t1[:, :], T["t0" + b][:, :], Op.add))
+        v(ts(t4[:, :], t1[:, :], cf(25), Op.add))
         vec.wait_ge(T.sem["wb" + b], 32)
         vw()
         v(tt(t2[:, :], T["W" + b][:, 0:64], t4[:, :], Op.add))
         vw()
-        v(ts(t3[:, 0:32], t2[:, 0:32], cf(5), Op.mult))
-        v(ts(t3[:, 32:64], t2[:, 32:64], cf(4), Op.mult))
+        v(tt(t3[:, :], t2[:, :], T["fm" + b][:, :], Op.mult))
         vw()
         for r in range(4):
             out = T.rland[:, 0:8] if (b == "A" and r == 0) else T["R" + b][:, 8 * r:8 * r + 8]
-            v(tt(out, t3[:, r:32:4], t3[:, 32 + r:64:4], Op.add))
-        pub("kr" + b)
-    g.wait_ge(T.sem.krA, 1)
+            tt(out, t3[:, r:32:4], t3[:, 32 + r:64:4], Op.add).then_inc(T.sem["kr" + b], 1)
+    g.wait_ge(T.sem.krA, 4)
     g.remote_dma_fused([tr(T.RA[:, 8 * i + 8:8 * i + 16], T.rland[:, 8 * slot(d, core) + 8:8 * slot(d, core) + 16], d, dir_engs[d], "rs")
                         for i, d in enumerate(dire)], local_sem=T.sem.ls)
-    g.wait_ge(T.sem.krB, 1)
-    g.remote_dma_fused([tr(T.RB[:, 16 * i:16 * i + 16], T.rres[:, :], rel, rel_engs[i], "rr") for i, (rel, _) in enumerate(shar)],
+    g.wait_ge(T.sem.krB, 4)
+    g.remote_dma_fused([tr(T.RB[:, 16 * i:16 * i + 16], T.rres[:, :], rel, res_engs[i], "rr") for i, (rel, _) in enumerate(shar)],
                        local_sem=T.sem.ls)
+    vec.wait_ge(T.sem.krA, 4)
     vec.wait_ge(T.sem.rs, 4 * 7)
     v(tt(T.s32[:, :], T.rland[:, 0:32], T.rland[:, 32:64], Op.add))
     vw()
     v(tt(T.s16[:, :], T.s32[:, 0:16], T.s32[:, 16:32], Op.add))
     vw()
-    v(tt(T.ysum[:, :], T.s16[:, 0:8], T.s16[:, 8:16], Op.add))
-    pub("ys")
+    tt(T.ysum[:, :], T.s16[:, 0:8], T.s16[:, 8:16], Op.add).then_inc(T.sem.ys, 1)
     syn.wait_ge(T.sem.ys, 1)
     syn.dma_start(out=T.y[:, :], in_=T.ysum[:, :]).then_inc(T.sem.dY, 16)
     syn.wait_ge(T.sem.dY, 16)
-    g.wait_ge(T.sem.ls, 2 * (4 * len(shar) + 4 * nd))
+    g.wait_ge(T.sem.ls, 12 * len(shar) + 8 * nd)

@@ -1,25 +1,24 @@
 from concourse.bass import DstId, RemoteDMATransfer
-from concourse.mybir import AluOpType as Op, AxisListType, ActivationFunctionType as Fn
+from concourse.mybir import AluOpType as Op, ActivationFunctionType as Fn
 
 V = 15
+HS = 104
 VC = 320
 EPS = 2.0 ** -12
 H1, H2 = range(2, 10), range(10, 12)
 SCRATCH = {
     "pin": ("sbuf", [128, 64], "int32"), "pq": ("sbuf", [128, 64], "int32"), "msg": ("sbuf", [128, 64], "float16"),
     "land": ("sbuf", [128, 448], "float16"), "rmsg": ("sbuf", [128, 64], "float16"), "rres": ("sbuf", [128, 16], "float32"),
-    "coli": ("sbuf", [128, 8], "int32"), "colf": ("sbuf", [128, 32], "float32"), "colb": ("sbuf", [128, 8], "bfloat16"),
+    "coli": ("sbuf", [128, 8], "int32"), "colf": ("sbuf", [128, 48], "float32"), "colb": ("sbuf", [128, 8], "bfloat16"),
     "colt": ("sbuf", [128, 8], "float32"),
-    "i16": ("sbuf", [128, 16], "float32"), "i24": ("sbuf", [128, 24], "float32"), "vi": ("sbuf", [128, 128], "int32"),
+    "pc": ("sbuf", [128, 128], "int32"), "pat": ("sbuf", [128, 128], "float32"),
     "u1": ("sbuf", [128, 144], "float32"), "u2": ("sbuf", [128, 144], "float32"),
-    "e16": ("sbuf", [128, 16], "float32"), "j24": ("sbuf", [128, 24], "float32"),
-    "lpf": ("sbuf", [128, 128], "float32"), "lp": ("sbuf", [128, 256], "float16"),
+    "lp": ("sbuf", [128, 256], "float16"),
     "zx": ("sbuf", [128, 144], "bfloat16"), "zw": ("sbuf", [128, 144], "bfloat16"),
-    "zq": ("sbuf", [128, 144], "bfloat16"), "zh": ("sbuf", [128, 144], "bfloat16"),
+    "zq": ("sbuf", [128, 144], "bfloat16"), "zh": ("sbuf", [128, 144], "bfloat16"), "zp": ("sbuf", [128, 144], "bfloat16"),
     "sk": ("sbuf", [128, 128], "int32"), "wt": ("sbuf", [128, 128], "int32"), "n0": ("sbuf", [128, 8], "int32"),
     "pa1": ("sbuf", [128, 128], "int32"), "pa0": ("sbuf", [128, 128], "int32"), "pz": ("sbuf", [128, 128], "int32"),
-    "ph": ("sbuf", [128, 128], "int32"), "pl": ("sbuf", [128, 128], "int32"), "v2k": ("sbuf", [128, 128], "int32"),
-    "tm": ("sbuf", [128, 128], "int32"), "hv": ("sbuf", [128, 128], "int32"), "a0r": ("sbuf", [128, 128], "int32"),
+    "ph": ("sbuf", [128, 128], "int32"), "pl": ("sbuf", [128, 128], "int32"),
     "hitl": ("sbuf", [128, 128], "uint16"), "missl": ("sbuf", [128, 128], "uint16"),
     "basei": ("sbuf", [128, 2048], "int32"), "basef": ("sbuf", [128, 2048], "float32"),
     "tab": ("sbuf", [128, 4098], "float32"),
@@ -27,8 +26,8 @@ SCRATCH = {
     "ysum": ("sbuf", [128, 8], "float32"),
     "psm": ("psum", [128, 144], "float32"),
 }
-SEMAPHORES = ["vc", "gi0", "gi1", "m0", "dP", "dS", "dW", "dN", "dB0", "dB1", "dZ", "dPc", "dY",
-              "kmsg", "klp", "kz", "ka", "kw", "kbase", "kc", "kn", "kh", "ke", "kt", "ht", "w47", "ys",
+SEMAPHORES = ["vc", "gi0", "gi1", "gi2", "gi3", "gi4", "kp", "m0", "dP", "dS", "dW", "dN", "dB0", "dB1", "dZ", "dPc", "dY",
+              "kmsg", "klp", "kz", "ka", "kw", "kbase", "kn", "ke", "kt", "kl", "kq", "kzw", "ht", "w47", "ys",
               "pa0", "pa1", "pa2", "pb0", "pb1", "pb2", "pb3", "rs", "rm", "rr", "ls", "rl"]
 for _b in "AB":
     SCRATCH.update({
@@ -94,8 +93,8 @@ def rank_program(g, core, T, topo):
         ins.then_inc(T.sem.vc, 1)
         nv[0] += 1
 
-    def vw():
-        vec.wait_ge(T.sem.vc, nv[0])
+    def vw(n=0):
+        vec.wait_ge(T.sem.vc, nv[0] - n)
 
     def pub(*names):
         vw()
@@ -110,14 +109,14 @@ def rank_program(g, core, T, topo):
     def tt(out, a, b, op):
         return vec.tensor_tensor(out=out, in0=a, in1=b, op=op)
 
-    def cf(k):
+    col = {}
+
+    def cf(name):
+        k = col.setdefault(name, len(col) + 2)
         return T.colf[:, k:k + 1]
 
     def ci(k):
         return T.coli[:, k:k + 1]
-
-    def ek(k):
-        return T.e16[:, k:k + 1]
 
     for h in range(2):
         q = syn if h == 0 else sca
@@ -143,38 +142,47 @@ def rank_program(g, core, T, topo):
     syn.wait_ge(T.sem.ka, 1)
     for row, name in ((8, "pa1"), (9, "pa0"), (10, "pz")):
         syn.dma_start(out=T.basei[row::16, 0:2048], in_=T[name][:, :]).then_inc(T.sem.dPc, 16)
+    for gg in range(4):
+        load(syn, gg, 1)
     syn.wait_ge(T.sem.kw, 1)
     for row, name in ((7, "ph"), (15, "pl")):
         syn.dma_start(out=T.basei[row::16, 0:2048], in_=T[name][:, :]).then_inc(T.sem.dPc, 16)
-    for gg in range(4):
-        load(syn, gg, 1)
 
     fl = {"allow_small_or_imprecise_dtypes": True}
     g.iota(T.coli[:, 0:1], [[0, 1]], 0, 1).then_inc(T.sem.gi0, 1)
-    g.iota(T.vi[:, :], [[1, 128]], 1, 128).then_inc(T.sem.gi0, 1)
-    g.iota(T.i16[:, :], [[1, 16]], 0, 0, **fl).then_inc(T.sem.gi1, 1)
-    g.iota(T.i24[:, :], [[1, 24]], 0, 0, **fl).then_inc(T.sem.gi1, 1)
-    g.iota(T.u1[:, :], [[1, 144]], 0, 0, **fl).then_inc(T.sem.gi1, 1)
-    g.iota(T.u2[:, :], [[1, 72], [0, 2]], 0, 0, **fl).then_inc(T.sem.gi1, 1)
+    g.iota(T.pa1[:, 0:127], [[1, 127]], 1, 0).then_inc(T.sem.gi1, 1)
+    g.iota(T.pa1[:, 127:128], [[0, 1]], 0, 0).then_inc(T.sem.gi1, 1)
+    g.iota(T.pc[:, :], [[1, 128]], 0, 0).then_inc(T.sem.gi1, 1)
+    g.wait_ge(T.sem.kp, 1)
+    for a in range(6):
+        g.iota(T.pat[:, a::16], [[3, 8]], a % 3, 0, **fl).then_inc(T.sem.gi2, 1)
+    g.iota(T.u1[:, :], [[1, 144]], 0, 0, **fl).then_inc(T.sem.gi3, 1)
 
     vec.memset(T.basei[:, 2040:2048], 0).then_inc(T.sem.m0, 1)
+    vec.memset(T.pat[:, :], -99.0).then_inc(T.sem.kp, 1)
     v(vec.memset(T.pq[:, :], 0))
-    v(vec.memset(T.lpf[:, :], 0.0))
-    vec.wait_ge(T.sem.gi0, 2)
-    v(ts(T.pa1[:, :], T.vi[:, :], 127, Op.bitwise_and))
-    v(ts(T.a0r[:, :], T.vi[:, :], 7, Op.arith_shift_right, 15, Op.bitwise_and))
-    v(ts(T.v2k[:, :], T.vi[:, :], 2047, Op.bitwise_and))
-    vw()
-    v(ts(T.tm[:, :], T.v2k[:, :], 0.0, Op.is_equal))
-    v(ts(T.pz[:, :], T.v2k[:, :], 2047.0, Op.not_equal))
+    vec.wait_ge(T.sem.gi0, 1)
     v(ts(ci(1), ci(0), 15, Op.bitwise_and))
     v(ts(ci(2), ci(0), 4, Op.arith_shift_right))
     v(ts(ci(3), ci(0), 63, Op.bitwise_and))
     v(ts(ci(4), ci(0), 1, Op.bitwise_and))
+    v(ts(ci(5), ci(0), 7, Op.bitwise_and))
     v(ts(ci(6), ci(0), 6, Op.arith_shift_right))
     v(ts(ci(7), ci(0), 1, Op.arith_shift_right, 7, Op.bitwise_and))
     vw()
-    v(tt(T.pa0[:, :], T.a0r[:, :], T.tm[:, :], Op.subtract))
+    v(vec.tensor_copy(out=cf("a"), in_=ci(1)))
+    v(ts(cf("a128"), ci(1), 128.0, Op.mult))
+    v(ts(cf("p63"), ci(3), 1.0, Op.mult))
+    v(ts(cf("w"), ci(6), -2046.0, Op.mult, 2048.0, Op.add))
+    v(ts(cf("w7"), ci(5), 7.0, Op.is_equal))
+    vw()
+    vec.wait_ge(T.sem.gi1, 3)
+    v(ts(T.pa0[:, 0:127], T.pc[:, 0:127], 0.0, Op.mult, cf("a"), Op.add))
+    v(ts(cf("nx"), cf("a"), 14.5, Op.is_ge, -17.0, Op.mult))
+    v(ts(cf("p24"), cf("p63"), -24.0, Op.add))
+    v(ts(T.pz[:, :], T.pa1[:, :], cf("a128"), Op.add, 2047.0, Op.not_equal))
+    vw(2)
+    v(ts(T.pa0[:, 127:128], cf("nx"), 1.0, Op.add, cf("a"), Op.add))
     pub("ka")
     vec.wait_ge(T.sem.dP, 64)
     v(ts(T.pq[0:48, :], T.pin[0:48, :], 10, Op.arith_shift_right))
@@ -184,68 +192,47 @@ def rank_program(g, core, T, topo):
     vec.wait_ge(T.sem.dW, 16)
     v(ts(T.ph[:, :], T.wt[:, :], 8, Op.arith_shift_right))
     v(ts(T.pl[:, :], T.wt[:, :], 255, Op.bitwise_and))
-    pub("kw")
-    v(vec.tensor_copy(out=cf(0), in_=ci(1)))
-    v(ts(cf(1), ci(2), 16.0, Op.mult, 15.0, Op.add))
-    v(ts(cf(2), ci(2), 8.0, Op.mult, 7.0, Op.add))
-    v(vec.tensor_copy(out=cf(31), in_=ci(3)))
-    v(vec.tensor_copy(out=cf(4), in_=ci(4)))
-    v(ts(cf(5), ci(4), -1.0, Op.mult, 1.0, Op.add))
-    v(ts(cf(6), ci(6), -2046.0, Op.mult, 2048.0, Op.add))
-    v(ts(cf(22), ci(3), 23.5, Op.is_ge))
-    v(ts(cf(21), ci(3), 23.5, Op.is_lt))
-    v(ts(cf(26), ci(7), 8.0, Op.mult, 7.0, Op.add))
-    v(ts(cf(27), ci(4), -255.0 / EPS, Op.mult, 256.0 / EPS, Op.add))
-    vec.wait_ge(T.sem.gi1, 4)
-    vw()
-    v(ts(T.e16[:, :], T.i16[:, :], cf(0), Op.is_equal))
-    v(ts(cf(3), cf(22), -24.0, Op.mult, cf(31), Op.add))
+    v(ts(cf("k8"), cf("a"), 8.0, Op.is_equal, EPS, Op.mult))
+    pub("kw", "ke")
+    v(ts(cf("bd"), cf("a"), 5.5, Op.is_lt))
+    v(ts(cf("lw"), cf("a"), 2.5, Op.is_lt))
+    v(ts(cf("r6"), cf("a"), 6.0, Op.not_equal, EPS, Op.mult))
+    vec.wait_ge(T.sem.gi2, 6)
+    v(ts(T.lp[:, 0:128], T.pat[:, :], cf("p63"), Op.is_equal, cf("w"), Op.mult))
+    v(ts(T.lp[:, 128:256], T.pat[:, :], cf("p24"), Op.is_equal, cf("w"), Op.mult))
+    vw(2)
+    v(ts(cf("sg"), cf("lw"), 2.0, Op.mult, cf("bd"), Op.subtract))
+    v(ts(cf("b2"), cf("bd"), 2.0 - EPS, Op.mult))
+    pub("klp")
+    v(ts(cf("sc"), cf("b2"), cf("r6"), Op.add))
+    v(ts(cf("ng"), cf("sg"), -1.0, Op.mult))
+    v(ts(cf("n8"), cf("sg"), -8.0, Op.mult))
+    v(ts(cf("nw"), cf("w7"), -1.0, Op.mult, 1.0, Op.add))
+    v(ts(cf("x8"), cf("k8"), 32.0 / EPS / EPS, Op.mult))
+    v(ts(cf("x9"), cf("a"), 9.0, Op.is_equal, 2.0 / EPS, Op.mult))
+    v(ts(cf("th"), cf("bd"), 7.0, Op.mult, 1.0, Op.add))
+    v(ts(cf("k15"), cf("a"), 15.0, Op.is_equal, -255.0 / EPS, Op.mult))
+    v(ts(cf("u2"), ci(2), 8.0, Op.mult, 7.0, Op.add))
+    v(ts(cf("u3"), ci(7), 8.0, Op.mult, 7.0, Op.add))
+    v(ts(cf("wh"), ci(4), -255.0 / EPS, Op.mult, 256.0 / EPS, Op.add))
+    v(ts(cf("k10"), cf("a"), 10.0, Op.is_equal, 2.0 / EPS, Op.mult))
+    vec.wait_ge(T.sem.dN, 16)
+    vw(5)
+    v(ts(cf("s0"), T.n0[:, 0:1], 16.0, Op.mult, cf("n8"), Op.add))
+    v(ts(cf("s1"), T.n0[:, 1:2], 16.0, Op.mult, cf("n8"), Op.add))
+    v(ts(cf("x1"), cf("sg"), 11.0 / 128, Op.mult, cf("x8"), Op.add))
+    v(ts(cf("u"), ci(2), 16.0, Op.mult, 15.0, Op.add))
+    vw(1)
+    v(ts(cf("xx"), cf("x1"), cf("x9"), Op.add))
     vec.wait_ge(T.sem.dS, 16)
     v(ts(T.missl[:, :], T.sk[:, :], -1.0, Op.add))
-    v(ts(T.hv[:, :], T.vi[:, :], -1.0, Op.add))
-    pub("ke")
-    v(ts(T.j24[:, :], T.i24[:, :], cf(3), Op.is_equal, cf(6), Op.mult))
-    v(ts(T.v2k[:, :], T.hv[:, :], 2047, Op.bitwise_and))
-    v(vec.tensor_reduce(out=cf(7), in_=T.e16[:, 0:3], axis=AxisListType.X, op=Op.add))
-    v(vec.tensor_reduce(out=cf(8), in_=T.e16[:, 3:6], axis=AxisListType.X, op=Op.add))
-    v(vec.tensor_reduce(out=cf(17), in_=T.e16[:, 0:6], axis=AxisListType.X, op=Op.add))
-    v(ts(cf(13), ek(7), 256.0 / EPS, Op.mult))
-    v(ts(cf(15), ek(7), -1.0, Op.mult, 1.0, Op.add))
-    vw()
-    for a in range(6):
-        v(vec.tensor_copy(out=T.lpf[:, a::16], in_=T.j24[:, a % 3::3]))
-    v(vec.tensor_copy(out=T.hitl[:, :], in_=T.v2k[:, :]))
-    v(tt(cf(9), cf(7), cf(8), Op.subtract))
-    v(tt(cf(16), cf(15), ek(15), Op.subtract))
-    v(ts(cf(10), cf(17), -EPS, Op.mult, EPS, Op.add))
-    v(ts(cf(28), cf(17), 7.0, Op.mult, 1.0, Op.add))
-    v(ts(cf(30), ek(15), 1.0 / EPS, Op.mult, cf(13), Op.add))
-    vw()
-    v(ts(T.lp[:, 0:128], T.lpf[:, :], cf(21), Op.mult))
-    v(ts(T.lp[:, 128:256], T.lpf[:, :], cf(22), Op.mult))
-    v(ts(cf(18), cf(9), -1.0, Op.mult))
-    v(ts(cf(29), cf(9), -8.0, Op.mult))
-    v(ts(cf(11), cf(9), 11.0 / 128, Op.mult))
-    v(ts(cf(14), ek(10), 2.0 / EPS, Op.mult, cf(9), Op.add))
-    v(ts(cf(7), ek(6), -EPS, Op.mult, cf(10), Op.add))
-    pub("klp")
-    vec.wait_ge(T.sem.dN, 16)
-    v(ts(cf(12), cf(17), 2.0, Op.mult, cf(7), Op.add))
-    v(ts(cf(19), T.n0[:, 0:1], 16.0, Op.mult, cf(29), Op.add))
-    v(ts(cf(8), T.n0[:, 1:2], 16.0, Op.mult, cf(29), Op.add))
-    v(ts(cf(31), ek(9), 2.0 / EPS, Op.mult, cf(11), Op.add))
-    v(ts(T.zw[:, :], T.u2[:, :], cf(2), Op.is_equal, cf(30), Op.mult))
-    v(ts(T.zq[:, :], T.u2[:, :], cf(2), Op.is_equal, cf(14), Op.mult))
-    v(ts(T.zh[:, :], T.u2[:, :], cf(26), Op.is_equal, cf(27), Op.mult))
+    v(ts(T.hitl[:, :], T.pc[:, :], cf("a128"), Op.add))
+    vec.wait_ge(T.sem.gi3, 1)
+    vw(2)
+    v(ts(T.zx[:, :], T.u1[:, :], cf("u"), Op.is_equal, cf("xx"), Op.mult))
     vec.wait_ge(T.sem.kt, 1)
-    vw()
-    v(tt(cf(20), cf(8), T.colt[:, 0:1], Op.add))
-    v(ts(cf(13), ek(8), 32.0 / EPS, Op.mult, cf(31), Op.add))
-    pub("kn")
-    v(ts(T.zx[:, :], T.u1[:, :], cf(1), Op.is_equal, cf(13), Op.mult))
-    for b in "AB":
-        v(vec.memset(T["h2" + b][:, :], 0.0))
-    pub("kz", "kh")
+    v(ts(cf("c1"), cf("s1"), T.colt[:, 0:1], Op.add))
+    pub("kz", "kl", "kn")
 
     dire, shar = direct(core), shares(core)
     chip_mates = topo.cores_of(core)
@@ -264,33 +251,34 @@ def rank_program(g, core, T, topo):
     g.remote_dma_fused([tr(T.msg[:, :], T.rmsg[:, :], rel, rel_engs[i], "rm") for i, (rel, _) in enumerate(shar)], local_sem=T.sem.ls)
     g.remote_dma_fused([tr(T.msg[:, :], T.land[:, 64 * slot(d, core):64 * slot(d, core) + 64], d, dir_engs[d],
                            "pa%d" % direct(d).index(core)) for d in dire], local_sem=T.sem.ls)
+    g.iota(T.u2[:, :], [[1, 72], [0, 2]], 0, 0, **fl).then_inc(T.sem.gi4, 1)
 
     def first(b):
         sca.wait_ge(T.sem["pp" + b], 8)
-        sca.activation(out=T["C1" + b][:, :], in_=T["pp" + b][:, :], func=Fn.Tanh, bias=cf(20), scale=-8.0).then_inc(T.sem["sy" + b], 1)
+        sca.activation(out=T["C1" + b][:, :], in_=T["pp" + b][:, :], func=Fn.Tanh, bias=cf("c1"), scale=-8.0).then_inc(T.sem["sy" + b], 1)
         sca.activation(out=T["P" + b][:, :], in_=T["pp" + b][:, :], func=Fn.Copy).then_inc(T.sem["pc" + b], 1)
 
     sca.wait_ge(T.sem.ke, 1)
-    sca.activation(out=T.colt[:, 0:1], in_=ek(8), func=Fn.Tanh, scale=EPS).then_inc(T.sem.kt, 1)
+    sca.activation(out=T.colt[:, 0:1], in_=cf("k8"), func=Fn.Tanh).then_inc(T.sem.kt, 1)
+    sca.wait_ge(T.sem.kl, 1)
+    sca.wait_ge(T.sem.kbase, 2)
+    sca.activation(out=T.tab[:, 2:32 * HS + 1:2], in_=T.basef[:, 0:2048].indirect(T.hitl[:, 0:HS]), func=Fn.Copy).then_inc(T.sem.ht, 1)
     sca.wait_ge(T.sem.kn, 1)
     first("A")
-    sca.wait_ge(T.sem.kbase, 2)
-    sca.activation(out=T.tab[:, 2:4097:2], in_=T.basef[:, 0:2048].indirect(T.hitl[:, 0:128]), func=Fn.Copy).then_inc(T.sem.ht, 1)
     first("B")
 
     vec.wait_ge(T.sem.dB0, 128)
     vec.wait_ge(T.sem.dZ, 64)
     vec.wait_ge(T.sem.dPc, 80)
-    ts(T.basef[:, 0:1024], T.basei[:, 0:1024], cf(12), Op.mult, cf(18), Op.add).then_inc(T.sem.kbase, 1)
+    ts(T.basef[:, 0:1024], T.basei[:, 0:1024], cf("sc"), Op.mult, cf("ng"), Op.add).then_inc(T.sem.kbase, 1)
     vec.wait_ge(T.sem.dB1, 128)
-    ts(T.basef[:, 1024:2048], T.basei[:, 1024:2048], cf(12), Op.mult, cf(18), Op.add).then_inc(T.sem.kbase, 1)
+    ts(T.basef[:, 1024:2048], T.basei[:, 1024:2048], cf("sc"), Op.mult, cf("ng"), Op.add).then_inc(T.sem.kbase, 1)
     vec.wait_ge(T.sem.kbase, 2)
-    v(ts(T.tab[:, 3:4098:2], T.basef[:, 0:2048].indirect(T.missl[:, 0:128]), cf(16), Op.mult))
-    v(vec.tensor_copy(out=T.colb[:, 0:1], in_=T.basef[:, 2047:2048]))
-    v(vec.tensor_copy(out=T.colb[:, 1:2], in_=T.basef[:, 0:1]))
-    v(ts(T.tab[:, 0:1], T.basef[:, 2047:2048], cf(16), Op.mult))
-    v(ts(T.tab[:, 1:2], T.basef[:, 2047:2048], cf(16), Op.mult))
-    pub("kc")
+    v(ts(T.tab[:, 3:4098:2], T.basef[:, 0:2048].indirect(T.missl[:, 0:128]), cf("nw"), Op.mult))
+    v(vec.tensor_copy(out=T.tab[:, 32 * HS + 2:4097:2], in_=T.basef[:, 0:2048].indirect(T.hitl[:, HS:128])))
+    v(ts(T.tab[:, 0:1], T.basef[:, 2047:2048], cf("nw"), Op.mult))
+    v(ts(T.tab[:, 1:2], T.basef[:, 2047:2048], cf("nw"), Op.mult))
+    vw()
 
     def spread(b, srcs):
         for r, (buf, c0, sem, n) in enumerate(srcs):
@@ -304,9 +292,9 @@ def rank_program(g, core, T, topo):
             ten.matmul(T["X" + b][:, 0:32], T.zx[:, 15 - j:143 - j], T["C%d%s" % (t % 2, b)][:, j:512:16],
                        j == 0, j == 15).then_inc(T.sem["x" + b], 1)
 
-    def pairs(out, z, src, sem, start, stop):
+    def pairs(out, z, src, sem, start, stop, k=128):
         for p in range(8):
-            ten.matmul(out, T[z][:, 14 - 2 * p:142 - 2 * p], T[src][:, 64 * p:64 * p + 64],
+            ten.matmul(out, T[z][0:k, 14 - 2 * p:142 - 2 * p], T[src][0:k, 64 * p:64 * p + 64],
                        start and p == 0, stop and p == 7).then_inc(T.sem[sem], 1)
 
     nd, nx = len(dire), len(cross(core))
@@ -326,8 +314,9 @@ def rank_program(g, core, T, topo):
                 ten.wait_ge(T.sem["s" + b], t - 1 if b == "B" else t - 2)
             if t < V - 1:
                 tx(b, t)
-            if t == 3 and b == "A":
-                ten.wait_ge(T.sem.kc, 1)
+            if t == 5 and b == "A":
+                ten.wait_ge(T.sem.kq, 1)
+                ten.wait_ge(T.sem.kzw, 2)
                 for p in range(8):
                     ten.matmul(T.psm[:, 0:2], T.zw[:, 14 - 2 * p:142 - 2 * p], T.colb[:, 0:2], p == 0, p == 7).then_inc(T.sem.w47, 1)
             if t == 8:
@@ -344,12 +333,11 @@ def rank_program(g, core, T, topo):
                 pairs(W, "zw", c, "wb" + b, False, False)
                 ten.wait_ge(T.sem["hz" + b], 16)
                 ten.wait_ge(T.sem["hw" + b], 16)
-                pairs(W, "zh", "h2" + b, "wb" + b, False, False)
+                pairs(W, "zh", "h2" + b, "wb" + b, False, False, 16 * len(H2))
             if t == V - 1:
                 pairs(T["X" + b][:, 0:64], "zq", c, "q" + b, True, True)
                 pairs(W, "zw", c, "wb" + b, False, True)
 
-    syn.wait_ge(T.sem.kh, 1)
     for t in list(H1) + list(H2):
         for b in "AB":
             syn.wait_ge(T.sem["c" + b], t - 1)
@@ -358,61 +346,90 @@ def rank_program(g, core, T, topo):
             dst, k, sem = ("h1", t - H1[0], "hx" if t % 2 == 0 else "hy") if t in H1 else ("h2", t - H2[0], "hz" if t % 2 == 0 else "hw")
             syn.dma_start(out=T[dst + b][16 * k:16 * k + 16, :], in_=T["C%d%s" % (t % 2, b)][7::8, :]).then_inc(T.sem[sem + b], 16)
 
+    def clamp(b, t):
+        n = 512 if t == 2 and b == "A" else VC
+        vec.wait_ge(T.sem["g" + b], t - 1)
+        ts(T["C%d%s" % (t % 2, b)][:, 0:n], T["D" + b][:, 0:n], 1.0, Op.min, -1.0, Op.max).then_inc(T.sem["c" + b], 1)
+
     vec.wait_ge(T.sem.ht, 1)
+    last = None
     for t in range(2, V):
-        if t == 10:
-            for sem in ("w47", "qoA", "qoB"):
-                vec.wait_ge(T.sem[sem], 8)
-            v(vec.tensor_copy(out=T.colf[:, 24:26], in_=T.psm[:, 0:2]))
-            for b, o in (("A", 8), ("B", 72)):
-                v(ts(T["fm" + b][:, 0:32], T.psm[:, o:o + 32], -5.0, Op.is_lt, cf(5), Op.mult))
-                v(ts(T["fm" + b][:, 32:64], T.psm[:, o + 32:o + 64], -5.0, Op.is_lt, cf(4), Op.mult))
         for b in "AB":
             D, C = T["D" + b], T["C%d%s" % (t % 2, b)]
+            if t == 2:
+                vec.wait_ge(T.sem["pc" + b], 1)
+            vec.wait_ge(T.sem["x" + b], 16 * (t - 1))
+            ts(T["off" + b][:, :], T["X" + b][:, 0:32], 2.953125, Op.add).then_inc(T.sem["o" + b], 1)
+            if last:
+                clamp(*last)
             if t - 2 in H1:
                 vec.wait_ge(T.sem[("hx" if t % 2 == 0 else "hy") + b], 16 * ((t - 2) // 2))
             elif t - 2 in H2:
                 vec.wait_ge(T.sem[("hz" if t % 2 == 0 else "hw") + b], 16)
             elif t == 14:
                 vec.wait_ge(T.sem["wa" + b], 8)
-            if t == 2:
-                vec.wait_ge(T.sem["pc" + b], 1)
-            vec.wait_ge(T.sem["x" + b], 16 * (t - 1))
-            ts(T["off" + b][:, :], T["X" + b][:, 0:32], 2.953125, Op.add).then_inc(T.sem["o" + b], 1)
             vec.wait_ge(T.sem["o" + b], t - 1)
             tt(D[:, :], T.tab[:, 0:4098].indirect(T["off" + b][:, 0:32]), T["P" + b][:, :], Op.subtract).then_inc(T.sem["g" + b], 1)
-            vec.wait_ge(T.sem["g" + b], t - 1)
-            n = 512 if t == 2 and b == "A" else VC
-            ts(C[:, 0:n], D[:, 0:n], 1.0, Op.min, -1.0, Op.max).then_inc(T.sem["c" + b], 1)
-            if n == VC:
+            last = (b, t)
+            if t == 2 and b == "A":
+                clamp(*last)
+                last = None
+                v(ts(cf("wz"), cf("k15"), 256.0 / EPS, Op.add, cf("w7"), Op.mult))
+                v(ts(cf("qz"), cf("k10"), cf("sg"), Op.add))
+                vec.wait_ge(T.sem.gi4, 1)
+                v(ts(T.zp[:, :], T.u2[:, :], cf("u2"), Op.is_equal))
+                v(ts(T.zh[:, :], T.u2[:, :], cf("u3"), Op.is_equal, cf("wh"), Op.mult))
+                v(vec.tensor_copy(out=T.colb[:, 0:1], in_=T.basef[:, 2047:2048]))
+                v(vec.tensor_copy(out=T.colb[:, 1:2], in_=T.basef[:, 0:1]))
+                pub("kq")
+            else:
                 sca.wait_ge(T.sem["g" + b], t - 1)
-                sca.activation(out=C[:, VC:512], in_=D[:, VC:512], func=Fn.Tanh, scale=cf(28)).then_inc(T.sem["s" + b], 1)
-            if 3 <= t < 7:
-                a = 128 * (t - 3)
-                sca.activation(out=T["F" + b][:, a:a + 128], in_=T["pp" + b][:, a:a + 128], func=Fn.Tanh, bias=cf(19),
+                sca.activation(out=C[:, VC:512], in_=D[:, VC:512], func=Fn.Tanh, scale=cf("th")).then_inc(T.sem["s" + b], 1)
+            if t == 3 and b == "A":
+                sca.wait_ge(T.sem.kq, 1)
+                sca.activation(out=T.zw[:, :], in_=T.zp[:, :], func=Fn.Copy, scale=cf("wz")).then_inc(T.sem.kzw, 1)
+            if t == 3 and b == "B":
+                sca.activation(out=T.zq[:, :], in_=T.zp[:, :], func=Fn.Copy, scale=cf("qz")).then_inc(T.sem.kzw, 1)
+            if 4 <= t < 8:
+                a = 128 * (t - 4)
+                sca.activation(out=T["F" + b][:, a:a + 128], in_=T["pp" + b][:, a:a + 128], func=Fn.Tanh, bias=cf("s0"),
                                scale=-8.0).then_inc(T.sem["f" + b], 1)
+    clamp(*last)
+    v(vec.tensor_copy(out=cf("odd"), in_=ci(4)))
+    v(ts(cf("even"), ci(4), -1.0, Op.mult, 1.0, Op.add))
+    for sem in ("w47", "qoA", "qoB"):
+        vec.wait_ge(T.sem[sem], 8)
+    v(vec.tensor_copy(out=T.colf[:, 0:2], in_=T.psm[:, 0:2]))
+    vw(1)
+    for b, o in (("A", 8), ("B", 72)):
+        v(ts(T["fm" + b][:, 0:32], T.psm[:, o:o + 32], -5.0, Op.is_lt, cf("even"), Op.mult))
+        v(ts(T["fm" + b][:, 32:64], T.psm[:, o + 32:o + 64], -5.0, Op.is_lt, cf("odd"), Op.mult))
 
+    vw(4)
     for b in "AB":
-        t1, t2, t3, t4 = [T[n + b] for n in ("t1", "t2", "t3", "t4")]
         vec.wait_ge(T.sem["q" + b], 8)
-        v(ts(t1[:, :], T["X" + b][:, 0:64], -5.0, Op.is_lt, cf(24), Op.mult))
-        vw()
-        v(ts(t4[:, :], t1[:, :], cf(25), Op.add))
+        v(ts(T["t1" + b][:, :], T["X" + b][:, 0:64], -5.0, Op.is_lt, T.colf[:, 0:1], Op.mult))
+    for b in "AB":
+        vw(1)
+        v(ts(T["t4" + b][:, :], T["t1" + b][:, :], T.colf[:, 1:2], Op.add))
+    for b in "AB":
         vec.wait_ge(T.sem["wb" + b], 32)
-        vw()
-        v(tt(t2[:, :], T["W" + b][:, 0:64], t4[:, :], Op.add))
-        vw()
-        v(tt(t3[:, :], t2[:, :], T["fm" + b][:, :], Op.mult))
-        vw()
+        vw(1)
+        v(tt(T["t2" + b][:, :], T["W" + b][:, 0:64], T["t4" + b][:, :], Op.add))
+    for b in "AB":
+        vw(1)
+        v(tt(T["t3" + b][:, :], T["t2" + b][:, :], T["fm" + b][:, :], Op.mult))
+    vw()
+    for b in "BA":
         for r in range(4):
             out = T.rland[:, 0:8] if (b == "A" and r == 0) else T["R" + b][:, 8 * r:8 * r + 8]
-            tt(out, t3[:, r:32:4], t3[:, 32 + r:64:4], Op.add).then_inc(T.sem["kr" + b], 1)
-    g.wait_ge(T.sem.krA, 4)
-    g.remote_dma_fused([tr(T.RA[:, 8 * i + 8:8 * i + 16], T.rland[:, 8 * slot(d, core) + 8:8 * slot(d, core) + 16], d, dir_engs[d], "rs")
-                        for i, d in enumerate(dire)], local_sem=T.sem.ls)
+            tt(out, T["t3" + b][:, r:32:4], T["t3" + b][:, 32 + r:64:4], Op.add).then_inc(T.sem["kr" + b], 1)
     g.wait_ge(T.sem.krB, 4)
     g.remote_dma_fused([tr(T.RB[:, 16 * i:16 * i + 16], T.rres[:, :], rel, res_engs[i], "rr") for i, (rel, _) in enumerate(shar)],
                        local_sem=T.sem.ls)
+    g.wait_ge(T.sem.krA, 4)
+    g.remote_dma_fused([tr(T.RA[:, 8 * i + 8:8 * i + 16], T.rland[:, 8 * slot(d, core) + 8:8 * slot(d, core) + 16], d, dir_engs[d], "rs")
+                        for i, d in enumerate(dire)], local_sem=T.sem.ls)
     vec.wait_ge(T.sem.krA, 4)
     vec.wait_ge(T.sem.rs, 4 * 7)
     v(tt(T.s32[:, :], T.rland[:, 0:32], T.rland[:, 32:64], Op.add))

@@ -2,32 +2,34 @@ from concourse.bass import DstId, RemoteDMATransfer
 from concourse.mybir import AluOpType as Op, ActivationFunctionType as Fn
 
 V = 15
-HS = 104
-VC = 320
 EPS = 2.0 ** -12
+ORD = "BA"
+B0, B1 = ORD
 H1, H2 = range(2, 10), range(10, 12)
 SCRATCH = {
     "pin": ("sbuf", [128, 64], "int32"), "pq": ("sbuf", [128, 64], "int32"), "msg": ("sbuf", [128, 64], "float16"),
     "land": ("sbuf", [128, 448], "float16"), "rmsg": ("sbuf", [128, 64], "float16"), "rres": ("sbuf", [128, 16], "float32"),
-    "coli": ("sbuf", [128, 8], "int32"), "colf": ("sbuf", [128, 48], "float32"), "colb": ("sbuf", [128, 8], "bfloat16"),
-    "colt": ("sbuf", [128, 8], "float32"),
-    "pc": ("sbuf", [128, 128], "int32"), "pat": ("sbuf", [128, 128], "float32"),
+    "coli": ("sbuf", [128, 16], "int32"), "colf": ("sbuf", [128, 64], "float32"), "colb": ("sbuf", [128, 8], "bfloat16"),
+    "colt": ("sbuf", [128, 8], "bfloat16"), "colp": ("sbuf", [128, 8], "float32"), "cols": ("sbuf", [128, 16], "float32"),
+    "pat": ("sbuf", [128, 128], "float32"),
     "u1": ("sbuf", [128, 144], "float32"), "u2": ("sbuf", [128, 144], "float32"),
     "lp": ("sbuf", [128, 256], "float16"),
+    "skh": ("sbuf", [128, 128], "float16"), "idn": ("sbuf", [128, 128], "bfloat16"), "skt": ("sbuf", [128, 128], "float16"),
+    "zs": ("sbuf", [128, 96], "bfloat16"), "zt": ("sbuf", [128, 512], "float32"),
     "zx": ("sbuf", [128, 144], "bfloat16"), "zw": ("sbuf", [128, 144], "bfloat16"),
     "zq": ("sbuf", [128, 144], "bfloat16"), "zh": ("sbuf", [128, 144], "bfloat16"), "zp": ("sbuf", [128, 144], "bfloat16"),
     "sk": ("sbuf", [128, 128], "int32"), "wt": ("sbuf", [128, 128], "int32"), "n0": ("sbuf", [128, 8], "int32"),
     "pa1": ("sbuf", [128, 128], "int32"), "pa0": ("sbuf", [128, 128], "int32"), "pz": ("sbuf", [128, 128], "int32"),
     "ph": ("sbuf", [128, 128], "int32"), "pl": ("sbuf", [128, 128], "int32"),
-    "hitl": ("sbuf", [128, 128], "uint16"), "missl": ("sbuf", [128, 128], "uint16"),
+    "missl": ("sbuf", [128, 128], "uint16"),
     "basei": ("sbuf", [128, 2048], "int32"), "basef": ("sbuf", [128, 2048], "float32"),
     "tab": ("sbuf", [128, 4098], "float32"),
     "rland": ("sbuf", [128, 64], "float32"), "s32": ("sbuf", [128, 32], "float32"), "s16": ("sbuf", [128, 16], "float32"),
     "ysum": ("sbuf", [128, 8], "float32"),
     "psm": ("psum", [128, 144], "float32"),
 }
-SEMAPHORES = ["vc", "gi0", "gi1", "gi2", "gi3", "gi4", "kp", "m0", "dP", "dS", "dW", "dN", "dB0", "dB1", "dZ", "dPc", "dY",
-              "kmsg", "klp", "kz", "ka", "kw", "kbase", "kn", "ke", "kt", "kl", "kq", "kzw", "ht", "w47", "ys",
+SEMAPHORES = ["vc", "gi0", "gi1", "gi2", "gi3", "gi4", "gi5", "kp", "m0", "dP", "dS", "dW", "dN", "dB0", "dB1", "dZ", "dPc", "dY",
+              "kbase", "kt", "ku", "kv", "kx", "kzp", "kth", "kzw", "ksb", "ksc", "ksd", "ht", "w47", "ys", "lt", "ll",
               "pa0", "pa1", "pa2", "pb0", "pb1", "pb2", "pb3", "rs", "rm", "rr", "ls", "rl"]
 for _b in "AB":
     SCRATCH.update({
@@ -39,6 +41,7 @@ for _b in "AB":
         "pp" + _b: ("psum", [128, 512], "float32"), "X" + _b: ("psum", [128, 64], "float32"), "W" + _b: ("psum", [128, 64], "float32"),
     })
     SEMAPHORES += [k + _b for k in ("pp", "pc", "sy", "f", "g", "c", "s", "o", "x", "wa", "wb", "qo", "q", "kr", "hx", "hy", "hz", "hw")]
+NG, TH, SC, NW, EV, WH, WA, WZ, TA, KT, QZ, NWH = range(12)
 
 
 def mask_of(engs):
@@ -87,19 +90,21 @@ def rank_program(g, core, T, topo):
         return
 
     vec, ten, sca, syn = g.vector, g.tensor, g.scalar, g.sync
-    nv = [0]
+    nv, seen, made = [0], [0], {}
 
-    def v(ins):
+    def v(name, ins):
         ins.then_inc(T.sem.vc, 1)
         nv[0] += 1
+        made[name] = nv[0]
 
-    def vw(n=0):
-        vec.wait_ge(T.sem.vc, nv[0] - n)
+    def need(*names):
+        n = max(made[k] for k in names)
+        if n > seen[0]:
+            vec.wait_ge(T.sem.vc, n)
+            seen[0] = n
 
-    def pub(*names):
-        vw()
-        for name in names:
-            vec.sem_inc(T.sem[name], 1)
+    def vwait(q, *names):
+        q.wait_ge(T.sem.vc, max(made[k] for k in names))
 
     def ts(out, in0, s1, op0, s2=None, op1=None):
         if op1 is None:
@@ -117,6 +122,86 @@ def rank_program(g, core, T, topo):
 
     def ci(k):
         return T.coli[:, k:k + 1]
+
+    def cs(k):
+        return T.cols[:, k:k + 1]
+
+    def cv(name, in0, *args, deps=()):
+        if deps:
+            need(*deps)
+        v(name, ts(cf(name), in0, *args))
+
+    def iv(k, *args):
+        v("i%d" % k, ts(ci(k), ci(0), *args))
+
+    vec.memset(T.basei[:, 2040:2048], 0).then_inc(T.sem.m0, 1)
+    vec.memset(T.pat[:, :], -99.0).then_inc(T.sem.kp, 1)
+    v("pq", vec.memset(T.pq[:, :], 0))
+    vec.wait_ge(T.sem.gi0, 1)
+    iv(1, 15, Op.bitwise_and)
+    iv(3, 63, Op.bitwise_and)
+    iv(6, 6, Op.arith_shift_right)
+    cv("a", ci(1), 1.0, Op.mult, deps=["i1"])
+    cv("p63", ci(3), 1.0, Op.mult, deps=["i3"])
+    vec.wait_ge(T.sem.gi1, 2)
+    v("pa1", ts(T.pa1[:, :], T.pa1[:, :], 127, Op.bitwise_and))
+    cv("lt", cf("a"), 14.5, Op.is_lt, deps=["a"])
+    cv("nx", cf("a"), 14.5, Op.is_ge, -17.0, Op.mult)
+    vec.wait_ge(T.sem.dP, 64)
+    need("pq")
+    v("q0", ts(T.pq[0:48, :], T.pin[0:48, :], 10, Op.arith_shift_right))
+    v("q1", ts(T.pq[64:112, :], T.pin[64:112, :], 1023, Op.bitwise_and))
+    cv("a128", ci(1), 128.0, Op.mult)
+    need("q0", "q1")
+    v("msg", vec.tensor_copy(out=T.msg[:, :], in_=T.pq[:, :]))
+    iv(8, 4, Op.arith_shift_right, 1, Op.bitwise_and)
+    cv("na", ci(1), -1.0, Op.mult, -16.0, Op.add)
+    cv("nb", ci(1), -1.0, Op.mult, -1016.0, Op.add)
+    vec.wait_ge(T.sem.dS, 16)
+    v("skh", ts(T.skh[:, :], T.sk[:, :], -1.0, Op.add))
+    cv("ne", ci(8), -1000.0, Op.mult, cf("na"), Op.add, deps=["i8", "na"])
+    cv("no", ci(8), 1000.0, Op.mult, cf("nb"), Op.add, deps=["nb"])
+    need("lt", "nx", "pa1")
+    v("pa1e", ts(T.pa1[:, 127:128], T.pa1[:, 127:128], cf("lt"), Op.mult))
+    v("pa0e", ts(T.pa0[:, 127:128], cf("nx"), 16.0, Op.add))
+    vec.wait_ge(T.sem.gi3, 1)
+    need("a128")
+    v("pz", ts(T.pz[:, :], T.u1[:, 0:128], cf("a128"), Op.add, 2046.0, Op.not_equal))
+    vec.wait_ge(T.sem.dW, 16)
+    v("ph", ts(T.ph[:, :], T.wt[:, :], 8, Op.arith_shift_right))
+    v("pl", ts(T.pl[:, :], T.wt[:, :], 255, Op.bitwise_and))
+    cv("bd", cf("a"), 5.5, Op.is_lt)
+    cv("lw", cf("a"), 2.5, Op.is_lt)
+    cv("w", ci(6), -2046.0, Op.mult, 2048.0, Op.add, deps=["i6"])
+    cv("p24", cf("p63"), -24.0, Op.add, deps=["p63"])
+    cv("sg", cf("lw"), 2.0, Op.mult, cf("bd"), Op.subtract, deps=["lw", "bd"])
+    vec.wait_ge(T.sem.gi2, 6)
+    need("p24", "w")
+    v("lp0", ts(T.lp[:, 0:128], T.pat[:, :], cf("p63"), Op.is_equal, cf("w"), Op.mult))
+    v("lp1", ts(T.lp[:, 128:256], T.pat[:, :], cf("p24"), Op.is_equal, cf("w"), Op.mult))
+    iv(2, 4, Op.arith_shift_right)
+    iv(7, 1, Op.arith_shift_right, 7, Op.bitwise_and)
+    vec.wait_ge(T.sem.lt, 1)
+    v("skt", vec.tensor_copy(out=T.skt[:, :], in_=T.ppB[:, 0:128]))
+    iv(5, 7, Op.bitwise_and)
+    cv("n8", cf("sg"), -8.0, Op.mult, deps=["sg"])
+    cv("x8", cf("a"), 8.0, Op.is_equal, 32.0 / EPS, Op.mult)
+    cv("x9", cf("a"), 9.0, Op.is_equal, 2.0 / EPS, Op.mult)
+    vec.wait_ge(T.sem.dN, 16)
+    cv("s1", T.n0[:, 1:2], 16.0, Op.mult, cf("n8"), Op.add, deps=["n8"])
+    cv("x1", cf("sg"), 11.0 / 128, Op.mult, cf("x8"), Op.add, deps=["x8"])
+    cv("u", ci(2), 16.0, Op.mult, 15.0, Op.add, deps=["i2"])
+    cv("w7", ci(5), 7.0, Op.is_equal, deps=["i5"])
+    cv("xx", cf("x1"), cf("x9"), Op.add, deps=["x1", "x9"])
+    cv("nu2", ci(2), -8.0, Op.mult, -7.0, Op.add)
+    cv("nu3", ci(7), -8.0, Op.mult, -7.0, Op.add, deps=["i7"])
+    iv(4, 1, Op.bitwise_and)
+    need("xx", "u")
+    v("zx", ts(T.zx[:, :], T.u1[:, 0:144], cf("u"), Op.is_equal, cf("xx"), Op.mult))
+    cv("s0", T.n0[:, 0:1], 16.0, Op.mult, cf("n8"), Op.add)
+    cv("odd", ci(4), 1.0, Op.mult, deps=["i4"])
+    vec.wait_ge(T.sem.ll, 64)
+    v("missl", vec.tensor_copy(out=T.missl[:, :], in_=T.ppB[:, 128:256]))
 
     for h in range(2):
         q = syn if h == 0 else sca
@@ -139,104 +224,28 @@ def rank_program(g, core, T, topo):
         sca.dma_start(out=T.basei[a::16, 0:2047], in_=T.nodes[a::16, 1:2048]).then_inc(T.sem.dZ, 16)
     for gg in range(4):
         load(sca, gg + 4, 1)
-    syn.wait_ge(T.sem.ka, 1)
+    vwait(syn, "pa1e", "pa0e", "pz")
     for row, name in ((8, "pa1"), (9, "pa0"), (10, "pz")):
         syn.dma_start(out=T.basei[row::16, 0:2048], in_=T[name][:, :]).then_inc(T.sem.dPc, 16)
     for gg in range(4):
         load(syn, gg, 1)
-    syn.wait_ge(T.sem.kw, 1)
+    vwait(syn, "ph", "pl")
     for row, name in ((7, "ph"), (15, "pl")):
         syn.dma_start(out=T.basei[row::16, 0:2048], in_=T[name][:, :]).then_inc(T.sem.dPc, 16)
 
     fl = {"allow_small_or_imprecise_dtypes": True}
     g.iota(T.coli[:, 0:1], [[0, 1]], 0, 1).then_inc(T.sem.gi0, 1)
-    g.iota(T.pa1[:, 0:127], [[1, 127]], 1, 0).then_inc(T.sem.gi1, 1)
-    g.iota(T.pa1[:, 127:128], [[0, 1]], 0, 0).then_inc(T.sem.gi1, 1)
-    g.iota(T.pc[:, :], [[1, 128]], 0, 0).then_inc(T.sem.gi1, 1)
+    g.iota(T.colp[:, 0:1], [[0, 1]], 0, -1, **fl).then_inc(T.sem.gi5, 1)
+    g.iota(T.pa1[:, :], [[1, 8], [0, 16]], 0, 8).then_inc(T.sem.gi1, 1)
+    g.iota(T.pa0[:, :], [[0, 8], [1, 16]], 1, 0).then_inc(T.sem.gi1, 1)
+    g.iota(T.u1[:, :], [[1, 144]], 0, 0, **fl).then_inc(T.sem.gi3, 1)
     g.wait_ge(T.sem.kp, 1)
     for a in range(6):
         g.iota(T.pat[:, a::16], [[3, 8]], a % 3, 0, **fl).then_inc(T.sem.gi2, 1)
-    g.iota(T.u1[:, :], [[1, 144]], 0, 0, **fl).then_inc(T.sem.gi3, 1)
-
-    vec.memset(T.basei[:, 2040:2048], 0).then_inc(T.sem.m0, 1)
-    vec.memset(T.pat[:, :], -99.0).then_inc(T.sem.kp, 1)
-    v(vec.memset(T.pq[:, :], 0))
-    vec.wait_ge(T.sem.gi0, 1)
-    v(ts(ci(1), ci(0), 15, Op.bitwise_and))
-    v(ts(ci(2), ci(0), 4, Op.arith_shift_right))
-    v(ts(ci(3), ci(0), 63, Op.bitwise_and))
-    v(ts(ci(4), ci(0), 1, Op.bitwise_and))
-    v(ts(ci(5), ci(0), 7, Op.bitwise_and))
-    v(ts(ci(6), ci(0), 6, Op.arith_shift_right))
-    v(ts(ci(7), ci(0), 1, Op.arith_shift_right, 7, Op.bitwise_and))
-    vw()
-    v(vec.tensor_copy(out=cf("a"), in_=ci(1)))
-    v(ts(cf("a128"), ci(1), 128.0, Op.mult))
-    v(ts(cf("p63"), ci(3), 1.0, Op.mult))
-    v(ts(cf("w"), ci(6), -2046.0, Op.mult, 2048.0, Op.add))
-    v(ts(cf("w7"), ci(5), 7.0, Op.is_equal))
-    vw()
-    vec.wait_ge(T.sem.gi1, 3)
-    v(ts(T.pa0[:, 0:127], T.pc[:, 0:127], 0.0, Op.mult, cf("a"), Op.add))
-    v(ts(cf("nx"), cf("a"), 14.5, Op.is_ge, -17.0, Op.mult))
-    v(ts(cf("p24"), cf("p63"), -24.0, Op.add))
-    v(ts(T.pz[:, :], T.pa1[:, :], cf("a128"), Op.add, 2047.0, Op.not_equal))
-    vw(2)
-    v(ts(T.pa0[:, 127:128], cf("nx"), 1.0, Op.add, cf("a"), Op.add))
-    pub("ka")
-    vec.wait_ge(T.sem.dP, 64)
-    v(ts(T.pq[0:48, :], T.pin[0:48, :], 10, Op.arith_shift_right))
-    v(ts(T.pq[64:112, :], T.pin[64:112, :], 1023, Op.bitwise_and))
-    vw()
-    vec.tensor_copy(out=T.msg[:, :], in_=T.pq[:, :]).then_inc(T.sem.kmsg, 1)
-    vec.wait_ge(T.sem.dW, 16)
-    v(ts(T.ph[:, :], T.wt[:, :], 8, Op.arith_shift_right))
-    v(ts(T.pl[:, :], T.wt[:, :], 255, Op.bitwise_and))
-    v(ts(cf("k8"), cf("a"), 8.0, Op.is_equal, EPS, Op.mult))
-    pub("kw", "ke")
-    v(ts(cf("bd"), cf("a"), 5.5, Op.is_lt))
-    v(ts(cf("lw"), cf("a"), 2.5, Op.is_lt))
-    v(ts(cf("r6"), cf("a"), 6.0, Op.not_equal, EPS, Op.mult))
-    vec.wait_ge(T.sem.gi2, 6)
-    v(ts(T.lp[:, 0:128], T.pat[:, :], cf("p63"), Op.is_equal, cf("w"), Op.mult))
-    v(ts(T.lp[:, 128:256], T.pat[:, :], cf("p24"), Op.is_equal, cf("w"), Op.mult))
-    vw(2)
-    v(ts(cf("sg"), cf("lw"), 2.0, Op.mult, cf("bd"), Op.subtract))
-    v(ts(cf("b2"), cf("bd"), 2.0 - EPS, Op.mult))
-    pub("klp")
-    v(ts(cf("sc"), cf("b2"), cf("r6"), Op.add))
-    v(ts(cf("ng"), cf("sg"), -1.0, Op.mult))
-    v(ts(cf("n8"), cf("sg"), -8.0, Op.mult))
-    v(ts(cf("nw"), cf("w7"), -1.0, Op.mult, 1.0, Op.add))
-    v(ts(cf("x8"), cf("k8"), 32.0 / EPS / EPS, Op.mult))
-    v(ts(cf("x9"), cf("a"), 9.0, Op.is_equal, 2.0 / EPS, Op.mult))
-    v(ts(cf("th"), cf("bd"), 7.0, Op.mult, 1.0, Op.add))
-    v(ts(cf("k15"), cf("a"), 15.0, Op.is_equal, -255.0 / EPS, Op.mult))
-    v(ts(cf("u2"), ci(2), 8.0, Op.mult, 7.0, Op.add))
-    v(ts(cf("u3"), ci(7), 8.0, Op.mult, 7.0, Op.add))
-    v(ts(cf("wh"), ci(4), -255.0 / EPS, Op.mult, 256.0 / EPS, Op.add))
-    v(ts(cf("k10"), cf("a"), 10.0, Op.is_equal, 2.0 / EPS, Op.mult))
-    vec.wait_ge(T.sem.dN, 16)
-    vw(5)
-    v(ts(cf("s0"), T.n0[:, 0:1], 16.0, Op.mult, cf("n8"), Op.add))
-    v(ts(cf("s1"), T.n0[:, 1:2], 16.0, Op.mult, cf("n8"), Op.add))
-    v(ts(cf("x1"), cf("sg"), 11.0 / 128, Op.mult, cf("x8"), Op.add))
-    v(ts(cf("u"), ci(2), 16.0, Op.mult, 15.0, Op.add))
-    vw(1)
-    v(ts(cf("xx"), cf("x1"), cf("x9"), Op.add))
-    vec.wait_ge(T.sem.dS, 16)
-    v(ts(T.missl[:, :], T.sk[:, :], -1.0, Op.add))
-    v(ts(T.hitl[:, :], T.pc[:, :], cf("a128"), Op.add))
-    vec.wait_ge(T.sem.gi3, 1)
-    vw(2)
-    v(ts(T.zx[:, :], T.u1[:, :], cf("u"), Op.is_equal, cf("xx"), Op.mult))
-    vec.wait_ge(T.sem.kt, 1)
-    v(ts(cf("c1"), cf("s1"), T.colt[:, 0:1], Op.add))
-    pub("kz", "kl", "kn")
 
     dire, shar = direct(core), shares(core)
     chip_mates = topo.cores_of(core)
-    g.wait_ge(T.sem.kmsg, 1)
+    vwait(g, "msg")
     wide = topo.engines(core, shar[0][0])
     n_on = len(wide) // 2
     rel_engs = [wide[n_on + 4 * i:n_on + 4 * i + 4] for i in range(len(shar))]
@@ -253,42 +262,97 @@ def rank_program(g, core, T, topo):
                            "pa%d" % direct(d).index(core)) for d in dire], local_sem=T.sem.ls)
     g.iota(T.u2[:, :], [[1, 72], [0, 2]], 0, 0, **fl).then_inc(T.sem.gi4, 1)
 
+    def act(out, in_, func, sem, **kw):
+        sca.activation(out=out, in_=in_, func=func, **kw).then_inc(T.sem[sem], 1)
+
     def first(b):
         sca.wait_ge(T.sem["pp" + b], 8)
-        sca.activation(out=T["C1" + b][:, :], in_=T["pp" + b][:, :], func=Fn.Tanh, bias=cf("c1"), scale=-8.0).then_inc(T.sem["sy" + b], 1)
-        sca.activation(out=T["P" + b][:, :], in_=T["pp" + b][:, :], func=Fn.Copy).then_inc(T.sem["pc" + b], 1)
+        act(T["C1" + b][:, :], T["pp" + b][:, :], Fn.Tanh, "sy" + b, bias=cf("s1"), scale=-8.0)
+        act(T["P" + b][:, :], T["pp" + b][:, :], Fn.Copy, "pc" + b)
 
-    sca.wait_ge(T.sem.ke, 1)
-    sca.activation(out=T.colt[:, 0:1], in_=cf("k8"), func=Fn.Tanh).then_inc(T.sem.kt, 1)
-    sca.wait_ge(T.sem.kl, 1)
-    sca.wait_ge(T.sem.kbase, 2)
-    sca.activation(out=T.tab[:, 2:32 * HS + 1:2], in_=T.basef[:, 0:2048].indirect(T.hitl[:, 0:HS]), func=Fn.Copy).then_inc(T.sem.ht, 1)
-    sca.wait_ge(T.sem.kn, 1)
+    sca.wait_ge(T.sem.gi3, 1)
+    sca.wait_ge(T.sem.gi5, 1)
+    act(T.zt[:, 0:128], T.u1[:, 0:128], Fn.Abs, "ksb", bias=T.colp[:, 0:1])
+    sca.wait_ge(T.sem.ksb, 1)
+    act(T.idn[:, :], T.zt[:, 0:128], Fn.Relu, "ksc", bias=1.0, scale=-1.0)
+    vwait(sca, "ne", "no")
+    for k, name in ((0, "ne"), (1, "no")):
+        act(T.zt[:, 128 + 48 * k:176 + 48 * k], T.u1[:, 0:48], Fn.Abs, "ksb", bias=cf(name))
+    sca.wait_ge(T.sem.ksb, 3)
+    act(T.zs[:, :], T.zt[:, 128:224], Fn.Relu, "ksd", bias=1.0, scale=-1.0)
+    vwait(sca, "sg")
+    act(cs(NG), cf("sg"), Fn.Copy, "kt", scale=-1.0)
+    act(cs(SC), cf("bd"), Fn.Identity, "kt", bias=EPS, scale=2.0 - EPS)
+    act(cs(TH), cf("bd"), Fn.Identity, "kt", bias=1.0, scale=7.0)
+    act(T.colt[:, 0:1], cf("sg"), Fn.Tanh, "ku", scale=16.0)
+    act(cs(WA), cf("a"), Fn.Identity, "ku", bias=479.125 / EPS, scale=-31.875 / EPS)
+    act(cs(TA), cf("a"), Fn.Identity, "ku", bias=-10.0)
+    vwait(sca, "w7")
+    act(cs(NW), cf("w7"), Fn.Identity, "kv", bias=1.0, scale=-1.0)
+    sca.wait_ge(T.sem.ku, 3)
+    act(cs(WZ), cf("w7"), Fn.Copy, "kx", scale=cs(WA))
+    act(cs(TA), cs(TA), Fn.Abs, "kx")
+    vwait(sca, "s1")
+    sca.wait_ge(T.sem.kv, 1)
+    sca.wait_ge(T.sem.kx, 2)
     first("A")
+    for h in range(2):
+        sca.wait_ge(T.sem.kbase, h + 1)
+        act(T.tab[:, 2048 * h + 2:2048 * h + 2049:2], T.basef[:, 1024 * h:1024 * h + 1024], Fn.Copy, "ht")
+    for k in range(2):
+        act(T.tab[:, k:k + 1], T.basef[:, 2047:2048], Fn.Copy, "ht", scale=cs(NW))
     first("B")
+    vwait(sca, "nu2", "nu3", "odd", "s0")
+    sca.wait_ge(T.sem.gi4, 1)
+    act(T.zt[:, 224:368], T.u2[:, :], Fn.Abs, "kth", bias=cf("nu2"))
+    act(T.zt[:, 368:512], T.u2[:, :], Fn.Abs, "kth", bias=cf("nu3"))
+    act(cs(EV), cf("odd"), Fn.Identity, "kth", bias=1.0, scale=-1.0)
+    act(cs(WH), cf("odd"), Fn.Identity, "kth", bias=256.0 / EPS, scale=-255.0 / EPS)
+    act(cs(NWH), cf("odd"), Fn.Identity, "kth", bias=-256.0 / EPS, scale=255.0 / EPS)
+    act(cs(KT), cs(TA), Fn.Relu, "kth", bias=1.0, scale=-1.0)
+    sca.wait_ge(T.sem.kth, 6)
+    act(cs(QZ), cs(KT), Fn.Identity, "kzp", bias=T.colt[:, 0:1], scale=2.0 / EPS)
+    act(T.zp[:, :], T.zt[:, 224:368], Fn.Relu, "kzp", bias=1.0, scale=-1.0)
+    act(T.zh[:, :], T.zt[:, 368:512], Fn.Relu, "kzp", bias=cs(WH), scale=cs(NWH))
+    sca.wait_ge(T.sem.kzp, 3)
+    sca.wait_ge(T.sem.kt, 3)
 
+    vec.wait_ge(T.sem.kt, 3)
+    vec.wait_ge(T.sem.kv, 1)
+    need("missl")
     vec.wait_ge(T.sem.dB0, 128)
     vec.wait_ge(T.sem.dZ, 64)
     vec.wait_ge(T.sem.dPc, 80)
-    ts(T.basef[:, 0:1024], T.basei[:, 0:1024], cf("sc"), Op.mult, cf("ng"), Op.add).then_inc(T.sem.kbase, 1)
+    ts(T.basef[:, 0:1024], T.basei[:, 0:1024], cs(SC), Op.mult, cs(NG), Op.add).then_inc(T.sem.kbase, 1)
     vec.wait_ge(T.sem.dB1, 128)
-    ts(T.basef[:, 1024:2048], T.basei[:, 1024:2048], cf("sc"), Op.mult, cf("ng"), Op.add).then_inc(T.sem.kbase, 1)
+    ts(T.basef[:, 1024:2048], T.basei[:, 1024:2048], cs(SC), Op.mult, cs(NG), Op.add).then_inc(T.sem.kbase, 1)
     vec.wait_ge(T.sem.kbase, 2)
-    v(ts(T.tab[:, 3:4098:2], T.basef[:, 0:2048].indirect(T.missl[:, 0:128]), cf("nw"), Op.mult))
-    v(vec.tensor_copy(out=T.tab[:, 32 * HS + 2:4097:2], in_=T.basef[:, 0:2048].indirect(T.hitl[:, HS:128])))
-    v(ts(T.tab[:, 0:1], T.basef[:, 2047:2048], cf("nw"), Op.mult))
-    v(ts(T.tab[:, 1:2], T.basef[:, 2047:2048], cf("nw"), Op.mult))
-    vw()
+    v("tab", ts(T.tab[:, 3:4098:2], T.basef[:, 0:2048].indirect(T.missl[:, 0:128]), cs(NW), Op.mult))
+
+    vwait(ten, "skh")
+    ten.wait_ge(T.sem.ksc, 1)
+    ten.matmul(T.ppB[:, 0:128], T.skh[:, :], T.idn[:, :], True, True).then_inc(T.sem.lt, 1)
+    vwait(ten, "skt")
+    ten.wait_ge(T.sem.ksd, 1)
+    for c in range(8):
+        a = 32 * (c // 2)
+        if c % 2 == 0 and c > 0:
+            ten.wait_ge(T.sem.ll, 8 * c)
+        for gg in range(8):
+            h, z = 32 * (gg // 2), 48 * (c % 2) + 16 - 16 * (gg % 2)
+            ten.matmul(T.ppB[h:h + 32, 128 + c:256:8], T.zs[a:a + 32, z:z + 32], T.skt[a:a + 32, 16 * gg:16 * gg + 16],
+                       gg % 2 == 0, gg % 2 == 1).then_inc(T.sem.ll, 1)
 
     def spread(b, srcs):
-        for r, (buf, c0, sem, n) in enumerate(srcs):
-            ten.wait_ge(T.sem[sem], n)
+        for r, (buf, c0, sem) in enumerate(srcs):
+            if sem:
+                ten.wait_ge(T.sem[sem], 4)
             for h in range(2):
                 ten.matmul(T["pp" + b][:, 256 * h + r:256 * h + 253 + r:4], T.lp[:, 128 * h:128 * h + 128],
                            T[buf][:, c0:c0 + 64], True, True).then_inc(T.sem["pp" + b], 1)
 
-    def tx(b, t):
-        for j in range(16):
+    def tx(b, t, js):
+        for j in js:
             ten.matmul(T["X" + b][:, 0:32], T.zx[:, 15 - j:143 - j], T["C%d%s" % (t % 2, b)][:, j:512:16],
                        j == 0, j == 15).then_inc(T.sem["x" + b], 1)
 
@@ -298,25 +362,30 @@ def rank_program(g, core, T, topo):
                        start and p == 0, stop and p == 7).then_inc(T.sem[sem], 1)
 
     nd, nx = len(dire), len(cross(core))
-    ten.wait_ge(T.sem.klp, 1)
-    spread("A", [("msg", 0, "kmsg", 1)] + [("land", 64 * i, "pa%d" % i, 4) for i in range(nd)])
-    ten.wait_ge(T.sem.kz, 1)
-    ten.wait_ge(T.sem.syA, 1)
-    tx("A", 1)
-    spread("B", [("land", 64 * (nd + i), "pb%d" % i, 4) for i in range(nx)])
-    ten.wait_ge(T.sem.syB, 1)
-    tx("B", 1)
+    vwait(ten, "lp0", "lp1", "msg")
+    spread("A", [("msg", 0, None)] + [("land", 64 * i, "pa%d" % i) for i in range(nd)])
+    vwait(ten, "missl")
+    spread("B", [("land", 64 * (nd + i), "pb%d" % i) for i in range(nx)])
+    vwait(ten, "zx")
+    for b in "AB":
+        ten.wait_ge(T.sem["sy" + b], 1)
+        tx(b, 1, range(16))
+
+    def swait(q, b, t):
+        if t > 2 or b == B1:
+            q.wait_ge(T.sem["s" + b], t - 1 if b == B1 else t - 2)
+
     for t in range(2, V):
-        for b in "AB":
+        for b in ORD:
             W, c = T["W" + b][:, 0:64], "C%d%s" % (t % 2, b)
             ten.wait_ge(T.sem["c" + b], t - 1)
-            if t > 2 or b == "B":
-                ten.wait_ge(T.sem["s" + b], t - 1 if b == "B" else t - 2)
             if t < V - 1:
-                tx(b, t)
-            if t == 5 and b == "A":
-                ten.wait_ge(T.sem.kq, 1)
-                ten.wait_ge(T.sem.kzw, 2)
+                tx(b, t, range(0, 16, 2))
+            swait(ten, b, t)
+            if t < V - 1:
+                tx(b, t, range(1, 16, 2))
+            if t == 5 and b == B0:
+                ten.wait_ge(T.sem.kzw, 4)
                 for p in range(8):
                     ten.matmul(T.psm[:, 0:2], T.zw[:, 14 - 2 * p:142 - 2 * p], T.colb[:, 0:2], p == 0, p == 7).then_inc(T.sem.w47, 1)
             if t == 8:
@@ -339,27 +408,27 @@ def rank_program(g, core, T, topo):
                 pairs(W, "zw", c, "wb" + b, False, True)
 
     for t in list(H1) + list(H2):
-        for b in "AB":
+        for b in ORD:
             syn.wait_ge(T.sem["c" + b], t - 1)
-            if t > 2 or b == "B":
-                syn.wait_ge(T.sem["s" + b], t - 1 if b == "B" else t - 2)
+            swait(syn, b, t)
             dst, k, sem = ("h1", t - H1[0], "hx" if t % 2 == 0 else "hy") if t in H1 else ("h2", t - H2[0], "hz" if t % 2 == 0 else "hw")
             syn.dma_start(out=T[dst + b][16 * k:16 * k + 16, :], in_=T["C%d%s" % (t % 2, b)][7::8, :]).then_inc(T.sem[sem + b], 16)
 
     def clamp(b, t):
-        n = 512 if t == 2 and b == "A" else VC
+        n = 1 if t == 2 and b == B0 else 2
         vec.wait_ge(T.sem["g" + b], t - 1)
-        ts(T["C%d%s" % (t % 2, b)][:, 0:n], T["D" + b][:, 0:n], 1.0, Op.min, -1.0, Op.max).then_inc(T.sem["c" + b], 1)
+        ts(T["C%d%s" % (t % 2, b)][:, 0:512:n], T["D" + b][:, 0:512:n], 1.0, Op.min, -1.0, Op.max).then_inc(T.sem["c" + b], 1)
 
-    vec.wait_ge(T.sem.ht, 1)
+    vec.wait_ge(T.sem.ht, 4)
+    need("tab")
     last = None
     for t in range(2, V):
-        for b in "AB":
+        for b in ORD:
             D, C = T["D" + b], T["C%d%s" % (t % 2, b)]
             if t == 2:
                 vec.wait_ge(T.sem["pc" + b], 1)
             vec.wait_ge(T.sem["x" + b], 16 * (t - 1))
-            ts(T["off" + b][:, :], T["X" + b][:, 0:32], 2.953125, Op.add).then_inc(T.sem["o" + b], 1)
+            ts(T["off" + b][:, :], T["X" + b][:, 0:32], 2.953125 if t > 2 else 4.953125, Op.add).then_inc(T.sem["o" + b], 1)
             if last:
                 clamp(*last)
             if t - 2 in H1:
@@ -371,59 +440,67 @@ def rank_program(g, core, T, topo):
             vec.wait_ge(T.sem["o" + b], t - 1)
             tt(D[:, :], T.tab[:, 0:4098].indirect(T["off" + b][:, 0:32]), T["P" + b][:, :], Op.subtract).then_inc(T.sem["g" + b], 1)
             last = (b, t)
-            if t == 2 and b == "A":
-                clamp(*last)
-                last = None
-                v(ts(cf("wz"), cf("k15"), 256.0 / EPS, Op.add, cf("w7"), Op.mult))
-                v(ts(cf("qz"), cf("k10"), cf("sg"), Op.add))
-                vec.wait_ge(T.sem.gi4, 1)
-                v(ts(T.zp[:, :], T.u2[:, :], cf("u2"), Op.is_equal))
-                v(ts(T.zh[:, :], T.u2[:, :], cf("u3"), Op.is_equal, cf("wh"), Op.mult))
-                v(vec.tensor_copy(out=T.colb[:, 0:1], in_=T.basef[:, 2047:2048]))
-                v(vec.tensor_copy(out=T.colb[:, 1:2], in_=T.basef[:, 0:1]))
-                pub("kq")
-            else:
+            if t > 2 or b != B0:
                 sca.wait_ge(T.sem["g" + b], t - 1)
-                sca.activation(out=C[:, VC:512], in_=D[:, VC:512], func=Fn.Tanh, scale=cf("th")).then_inc(T.sem["s" + b], 1)
-            if t == 3 and b == "A":
-                sca.wait_ge(T.sem.kq, 1)
-                sca.activation(out=T.zw[:, :], in_=T.zp[:, :], func=Fn.Copy, scale=cf("wz")).then_inc(T.sem.kzw, 1)
-            if t == 3 and b == "B":
-                sca.activation(out=T.zq[:, :], in_=T.zp[:, :], func=Fn.Copy, scale=cf("qz")).then_inc(T.sem.kzw, 1)
+                act(C[:, 1:512:2], D[:, 1:512:2], Fn.Tanh, "s" + b, scale=cs(TH))
+            if t == 3 and b == B0:
+                for k, cc in ((0, 2047), (1, 0)):
+                    act(T.colb[:, k:k + 1], T.basef[:, cc:cc + 1], Fn.Copy, "kzw")
+                act(T.zw[:, :], T.zp[:, :], Fn.Copy, "kzw", scale=cs(WZ))
+            if t == 3 and b == B1:
+                act(T.zq[:, :], T.zp[:, :], Fn.Copy, "kzw", scale=cs(QZ))
             if 4 <= t < 8:
                 a = 128 * (t - 4)
-                sca.activation(out=T["F" + b][:, a:a + 128], in_=T["pp" + b][:, a:a + 128], func=Fn.Tanh, bias=cf("s0"),
-                               scale=-8.0).then_inc(T.sem["f" + b], 1)
-    clamp(*last)
-    v(vec.tensor_copy(out=cf("odd"), in_=ci(4)))
-    v(ts(cf("even"), ci(4), -1.0, Op.mult, 1.0, Op.add))
+                act(T["F" + b][:, a:a + 128], T["pp" + b][:, a:a + 128], Fn.Tanh, "f" + b, bias=cf("s0"), scale=-8.0)
+
     for sem in ("w47", "qoA", "qoB"):
         vec.wait_ge(T.sem[sem], 8)
-    v(vec.tensor_copy(out=T.colf[:, 0:2], in_=T.psm[:, 0:2]))
-    vw(1)
-    for b, o in (("A", 8), ("B", 72)):
-        v(ts(T["fm" + b][:, 0:32], T.psm[:, o:o + 32], -5.0, Op.is_lt, cf("even"), Op.mult))
-        v(ts(T["fm" + b][:, 32:64], T.psm[:, o + 32:o + 64], -5.0, Op.is_lt, cf("odd"), Op.mult))
+    v("w07", vec.tensor_copy(out=T.colf[:, 0:2], in_=T.psm[:, 0:2]))
+    clamp(*last)
 
-    vw(4)
-    for b in "AB":
+    def flag(b, h):
+        o = (8 if b == "A" else 72) + 32 * h
+        v("fm" + b, ts(T["fm" + b][:, 32 * h:32 * h + 32], T.psm[:, o:o + 32], -5.0, Op.is_lt, (cs(EV), cf("odd"))[h], Op.mult))
+
+    def end(b):
         vec.wait_ge(T.sem["q" + b], 8)
-        v(ts(T["t1" + b][:, :], T["X" + b][:, 0:64], -5.0, Op.is_lt, T.colf[:, 0:1], Op.mult))
-    for b in "AB":
-        vw(1)
-        v(ts(T["t4" + b][:, :], T["t1" + b][:, :], T.colf[:, 1:2], Op.add))
-    for b in "AB":
+        need("w07")
+        v("t1" + b, ts(T["t1" + b][:, :], T["X" + b][:, 0:64], -5.0, Op.is_lt, T.colf[:, 0:1], Op.mult))
+
+    def add0(b):
+        need("t1" + b)
+        v("t4" + b, ts(T["t4" + b][:, :], T["t1" + b][:, :], T.colf[:, 1:2], Op.add))
+
+    def addw(b):
         vec.wait_ge(T.sem["wb" + b], 32)
-        vw(1)
-        v(tt(T["t2" + b][:, :], T["W" + b][:, 0:64], T["t4" + b][:, :], Op.add))
-    for b in "AB":
-        vw(1)
-        v(tt(T["t3" + b][:, :], T["t2" + b][:, :], T["fm" + b][:, :], Op.mult))
-    vw()
-    for b in "BA":
+        need("t4" + b)
+        v("t2" + b, tt(T["t2" + b][:, :], T["W" + b][:, 0:64], T["t4" + b][:, :], Op.add))
+
+    def cutf(b):
+        need("t2" + b, "fm" + b)
+        v("t3" + b, tt(T["t3" + b][:, :], T["t2" + b][:, :], T["fm" + b][:, :], Op.mult))
+
+    def sums(b):
+        need("t3" + b)
         for r in range(4):
             out = T.rland[:, 0:8] if (b == "A" and r == 0) else T["R" + b][:, 8 * r:8 * r + 8]
             tt(out, T["t3" + b][:, r:32:4], T["t3" + b][:, 32 + r:64:4], Op.add).then_inc(T.sem["kr" + b], 1)
+
+    vec.wait_ge(T.sem.kth, 6)
+    flag("B", 0)
+    end("B")
+    flag("B", 1)
+    add0("B")
+    flag("A", 0)
+    addw("B")
+    flag("A", 1)
+    cutf("B")
+    end("A")
+    sums("B")
+    add0("A")
+    addw("A")
+    cutf("A")
+    sums("A")
     g.wait_ge(T.sem.krB, 4)
     g.remote_dma_fused([tr(T.RB[:, 16 * i:16 * i + 16], T.rres[:, :], rel, res_engs[i], "rr") for i, (rel, _) in enumerate(shar)],
                        local_sem=T.sem.ls)
@@ -432,10 +509,10 @@ def rank_program(g, core, T, topo):
                         for i, d in enumerate(dire)], local_sem=T.sem.ls)
     vec.wait_ge(T.sem.krA, 4)
     vec.wait_ge(T.sem.rs, 4 * 7)
-    v(tt(T.s32[:, :], T.rland[:, 0:32], T.rland[:, 32:64], Op.add))
-    vw()
-    v(tt(T.s16[:, :], T.s32[:, 0:16], T.s32[:, 16:32], Op.add))
-    vw()
+    v("s32", tt(T.s32[:, :], T.rland[:, 0:32], T.rland[:, 32:64], Op.add))
+    need("s32")
+    v("s16", tt(T.s16[:, :], T.s32[:, 0:16], T.s32[:, 16:32], Op.add))
+    need("s16")
     tt(T.ysum[:, :], T.s16[:, 0:8], T.s16[:, 8:16], Op.add).then_inc(T.sem.ys, 1)
     syn.wait_ge(T.sem.ys, 1)
     syn.dma_start(out=T.y[:, :], in_=T.ysum[:, :]).then_inc(T.sem.dY, 16)

from concourse.bass import DstId, RemoteDMATransfer
from concourse.mybir import AluOpType as Op, ActivationFunctionType as Fn

V = 15
EPS = 2.0 ** -12
ORD = "BA"
B0, B1 = ORD
H1, H2 = range(2, 10), range(10, 12)
SCRATCH = {
    "pin": ("sbuf", [128, 64], "int32"), "pq": ("sbuf", [128, 64], "int32"), "msg": ("sbuf", [128, 64], "float16"),
    "land": ("sbuf", [128, 448], "float16"), "rmsg": ("sbuf", [128, 64], "float16"), "rres": ("sbuf", [128, 16], "float32"),
    "coli": ("sbuf", [128, 16], "int32"), "colf": ("sbuf", [128, 64], "float32"), "colb": ("sbuf", [128, 8], "bfloat16"),
    "colt": ("sbuf", [128, 8], "bfloat16"), "colp": ("sbuf", [128, 8], "float32"), "cols": ("sbuf", [128, 16], "float32"),
    "pat": ("sbuf", [128, 128], "float32"),
    "u1": ("sbuf", [128, 144], "float32"), "u2": ("sbuf", [128, 144], "float32"),
    "lp": ("sbuf", [128, 256], "float16"),
    "skh": ("sbuf", [128, 128], "float16"), "idn": ("sbuf", [128, 128], "bfloat16"), "skt": ("sbuf", [128, 128], "float16"),
    "zs": ("sbuf", [128, 96], "bfloat16"), "zt": ("sbuf", [128, 512], "float32"),
    "zx": ("sbuf", [128, 144], "bfloat16"), "zw": ("sbuf", [128, 144], "bfloat16"),
    "zq": ("sbuf", [128, 144], "bfloat16"), "zh": ("sbuf", [128, 144], "bfloat16"), "zp": ("sbuf", [128, 144], "bfloat16"),
    "sk": ("sbuf", [128, 128], "int32"), "wt": ("sbuf", [128, 128], "int32"), "n0": ("sbuf", [128, 8], "int32"),
    "pa1": ("sbuf", [128, 128], "int32"), "pa0": ("sbuf", [128, 128], "int32"), "pz": ("sbuf", [128, 128], "int32"),
    "ph": ("sbuf", [128, 128], "int32"), "pl": ("sbuf", [128, 128], "int32"),
    "missl": ("sbuf", [128, 128], "uint16"),
    "basei": ("sbuf", [128, 2048], "int32"), "basef": ("sbuf", [128, 2048], "float32"),
    "tab": ("sbuf", [128, 4098], "float32"),
    "rland": ("sbuf", [128, 64], "float32"), "s32": ("sbuf", [128, 32], "float32"), "s16": ("sbuf", [128, 16], "float32"),
    "ysum": ("sbuf", [128, 8], "float32"),
    "psm": ("psum", [128, 144], "float32"),
}
SEMAPHORES = ["vc", "gi0", "gi1", "gi2", "gi3", "gi4", "gi5", "kp", "m0", "dP", "dS", "dW", "dN", "dB0", "dB1", "dZ", "dPc", "dY",
              "kbase", "kt", "ku", "kv", "kx", "kzp", "kth", "kzw", "ksb", "ksc", "ksd", "ht", "w47", "ys", "lt", "ll",
              "pa0", "pa1", "pa2", "pb0", "pb1", "pb2", "pb3", "rs", "rm", "rr", "ls", "rl"]
for _b in "AB":
    SCRATCH.update({
        "off" + _b: ("sbuf", [128, 32], "uint16"), "P" + _b: ("sbuf", [128, 512], "float32"), "D" + _b: ("sbuf", [128, 512], "bfloat16"),
        "C0" + _b: ("sbuf", [128, 512], "bfloat16"), "C1" + _b: ("sbuf", [128, 512], "bfloat16"), "F" + _b: ("sbuf", [128, 512], "bfloat16"),
        "h1" + _b: ("sbuf", [128, 512], "bfloat16"), "h2" + _b: ("sbuf", [128, 512], "bfloat16"),
        "R" + _b: ("sbuf", [128, 32], "float32"), "fm" + _b: ("sbuf", [128, 64], "float32"), "t1" + _b: ("sbuf", [128, 64], "float32"),
        "t2" + _b: ("sbuf", [128, 64], "float32"), "t3" + _b: ("sbuf", [128, 64], "float32"), "t4" + _b: ("sbuf", [128, 64], "float32"),
        "pp" + _b: ("psum", [128, 512], "float32"), "X" + _b: ("psum", [128, 64], "float32"), "W" + _b: ("psum", [128, 64], "float32"),
    })
    SEMAPHORES += [k + _b for k in ("pp", "pc", "sy", "f", "g", "c", "s", "o", "x", "wa", "wb", "qo", "q", "kr", "hx", "hy", "hz", "hw")]
NG, TH, SC, NW, EV, WH, WA, WZ, TA, KT, QZ, NWH = range(12)


def mask_of(engs):
    m = 0
    for e in engs:
        m |= 1 << e
    return m


def rank_program(g, core, T, topo):
    cores = list(T.cores)

    def direct(c):
        return [d for d in cores if d != c and topo.may_write(c, d)]

    def cross(c):
        return [d for d in cores if d != c and not topo.may_write(c, d)]

    def shares(c):
        x = cross(c)
        rl = [k for k in topo.cores_of(c) if k not in cores and topo.die(k) == topo.die(c) and all(topo.may_write(k, d) for d in x)][:2]
        n = -(-len(x) // len(rl))
        return [(k, x[i * n:(i + 1) * n]) for i, k in enumerate(rl)]

    def slot(dst, src):
        return (direct(dst) + cross(dst)).index(src)

    def tr(src_ap, dst_ap, dst, engs, sem):
        rid, pid = topo.addr(dst, core)
        return RemoteDMATransfer(dst_ids=[DstId(rid=rid, pnc=pid)], dma_engine_mask=mask_of(engs), remote_sem=T.sem[sem],
                                 srcs=[src_ap], dsts=[dst_ap], alu_op=0)

    if T.rank_of(core) is None:
        for c in cores:
            for k, (rel, dests) in enumerate(shares(c)):
                if rel != core:
                    continue
                engs = [topo.engines(core, d)[4 * i:4 * i + 4] for i, d in enumerate(dests)]
                g.wait_ge(T.sem.rm, 4)
                g.remote_dma_fused([tr(T.rmsg[:, :], T.land[:, 64 * slot(d, c):64 * slot(d, c) + 64], d, engs[i],
                                       "pb%d" % cross(d).index(c)) for i, d in enumerate(dests)], local_sem=T.sem.rl)
                g.wait_ge(T.sem.rr, 8)
                g.remote_dma_fused([tr(T.rres[:, 8 * i:8 * i + 8], T.rland[:, 8 * slot(d, c) + 8:8 * slot(d, c) + 16], d, engs[i], "rs")
                                    for i, d in enumerate(dests)], local_sem=T.sem.rl)
                g.wait_ge(T.sem.rl, 16)
        return

    vec, ten, sca, syn = g.vector, g.tensor, g.scalar, g.sync
    nv, seen, made = [0], [0], {}

    def v(name, ins):
        ins.then_inc(T.sem.vc, 1)
        nv[0] += 1
        made[name] = nv[0]

    def need(*names):
        n = max(made[k] for k in names)
        if n > seen[0]:
            vec.wait_ge(T.sem.vc, n)
            seen[0] = n

    def vwait(q, *names):
        q.wait_ge(T.sem.vc, max(made[k] for k in names))

    def ts(out, in0, s1, op0, s2=None, op1=None):
        if op1 is None:
            return vec.tensor_scalar(out=out, in0=in0, scalar1=s1, scalar2=None, op0=op0)
        return vec.tensor_scalar(out=out, in0=in0, scalar1=s1, scalar2=s2, op0=op0, op1=op1)

    def tt(out, a, b, op):
        return vec.tensor_tensor(out=out, in0=a, in1=b, op=op)

    col = {}

    def cf(name):
        k = col.setdefault(name, len(col) + 2)
        return T.colf[:, k:k + 1]

    def ci(k):
        return T.coli[:, k:k + 1]

    def cs(k):
        return T.cols[:, k:k + 1]

    def cv(name, in0, *args, deps=()):
        if deps:
            need(*deps)
        v(name, ts(cf(name), in0, *args))

    def iv(k, *args):
        v("i%d" % k, ts(ci(k), ci(0), *args))

    vec.memset(T.basei[:, 2040:2048], 0).then_inc(T.sem.m0, 1)
    vec.memset(T.pat[:, :], -99.0).then_inc(T.sem.kp, 1)
    v("pq", vec.memset(T.pq[:, :], 0))
    vec.wait_ge(T.sem.gi0, 1)
    iv(1, 15, Op.bitwise_and)
    iv(3, 63, Op.bitwise_and)
    iv(6, 6, Op.arith_shift_right)
    cv("a", ci(1), 1.0, Op.mult, deps=["i1"])
    cv("p63", ci(3), 1.0, Op.mult, deps=["i3"])
    vec.wait_ge(T.sem.gi1, 2)
    v("pa1", ts(T.pa1[:, :], T.pa1[:, :], 127, Op.bitwise_and))
    cv("lt", cf("a"), 14.5, Op.is_lt, deps=["a"])
    cv("nx", cf("a"), 14.5, Op.is_ge, -17.0, Op.mult)
    vec.wait_ge(T.sem.dP, 64)
    need("pq")
    v("q0", ts(T.pq[0:48, :], T.pin[0:48, :], 10, Op.arith_shift_right))
    v("q1", ts(T.pq[64:112, :], T.pin[64:112, :], 1023, Op.bitwise_and))
    cv("a128", ci(1), 128.0, Op.mult)
    need("q0", "q1")
    v("msg", vec.tensor_copy(out=T.msg[:, :], in_=T.pq[:, :]))
    iv(8, 4, Op.arith_shift_right, 1, Op.bitwise_and)
    cv("na", ci(1), -1.0, Op.mult, -16.0, Op.add)
    cv("nb", ci(1), -1.0, Op.mult, -1016.0, Op.add)
    vec.wait_ge(T.sem.dS, 16)
    v("skh", ts(T.skh[:, :], T.sk[:, :], -1.0, Op.add))
    cv("ne", ci(8), -1000.0, Op.mult, cf("na"), Op.add, deps=["i8", "na"])
    cv("no", ci(8), 1000.0, Op.mult, cf("nb"), Op.add, deps=["nb"])
    need("lt", "nx", "pa1")
    v("pa1e", ts(T.pa1[:, 127:128], T.pa1[:, 127:128], cf("lt"), Op.mult))
    v("pa0e", ts(T.pa0[:, 127:128], cf("nx"), 16.0, Op.add))
    vec.wait_ge(T.sem.gi3, 1)
    need("a128")
    v("pz", ts(T.pz[:, :], T.u1[:, 0:128], cf("a128"), Op.add, 2046.0, Op.not_equal))
    vec.wait_ge(T.sem.dW, 16)
    v("ph", ts(T.ph[:, :], T.wt[:, :], 8, Op.arith_shift_right))
    v("pl", ts(T.pl[:, :], T.wt[:, :], 255, Op.bitwise_and))
    cv("bd", cf("a"), 5.5, Op.is_lt)
    cv("lw", cf("a"), 2.5, Op.is_lt)
    cv("w", ci(6), -2046.0, Op.mult, 2048.0, Op.add, deps=["i6"])
    cv("p24", cf("p63"), -24.0, Op.add, deps=["p63"])
    cv("sg", cf("lw"), 2.0, Op.mult, cf("bd"), Op.subtract, deps=["lw", "bd"])
    vec.wait_ge(T.sem.gi2, 6)
    need("p24", "w")
    v("lp0", ts(T.lp[:, 0:128], T.pat[:, :], cf("p63"), Op.is_equal, cf("w"), Op.mult))
    v("lp1", ts(T.lp[:, 128:256], T.pat[:, :], cf("p24"), Op.is_equal, cf("w"), Op.mult))
    iv(2, 4, Op.arith_shift_right)
    iv(7, 1, Op.arith_shift_right, 7, Op.bitwise_and)
    vec.wait_ge(T.sem.lt, 1)
    v("skt", vec.tensor_copy(out=T.skt[:, :], in_=T.ppB[:, 0:128]))
    iv(5, 7, Op.bitwise_and)
    cv("n8", cf("sg"), -8.0, Op.mult, deps=["sg"])
    cv("x8", cf("a"), 8.0, Op.is_equal, 32.0 / EPS, Op.mult)
    cv("x9", cf("a"), 9.0, Op.is_equal, 2.0 / EPS, Op.mult)
    vec.wait_ge(T.sem.dN, 16)
    cv("s1", T.n0[:, 1:2], 16.0, Op.mult, cf("n8"), Op.add, deps=["n8"])
    cv("x1", cf("sg"), 11.0 / 128, Op.mult, cf("x8"), Op.add, deps=["x8"])
    cv("u", ci(2), 16.0, Op.mult, 15.0, Op.add, deps=["i2"])
    cv("w7", ci(5), 7.0, Op.is_equal, deps=["i5"])
    cv("xx", cf("x1"), cf("x9"), Op.add, deps=["x1", "x9"])
    cv("nu2", ci(2), -8.0, Op.mult, -7.0, Op.add)
    cv("nu3", ci(7), -8.0, Op.mult, -7.0, Op.add, deps=["i7"])
    iv(4, 1, Op.bitwise_and)
    need("xx", "u")
    v("zx", ts(T.zx[:, :], T.u1[:, 0:144], cf("u"), Op.is_equal, cf("xx"), Op.mult))
    cv("s0", T.n0[:, 0:1], 16.0, Op.mult, cf("n8"), Op.add)
    cv("odd", ci(4), 1.0, Op.mult, deps=["i4"])
    vec.wait_ge(T.sem.ll, 64)
    v("missl", vec.tensor_copy(out=T.missl[:, :], in_=T.ppB[:, 128:256]))

    for h in range(2):
        q = syn if h == 0 else sca
        for lo in range(2):
            k = 64 * lo + 24 * h
            q.dma_start(out=T.pin[k:k + 24, :], in_=T.pts[:, 64 * h:64 * h + 64]).then_inc(T.sem.dP, 16)
    syn.dma_start(out=T.wt[:, :], in_=T.nodes[7::16, :]).then_inc(T.sem.dW, 16)
    sca.dma_start(out=T.sk[:, :], in_=T.nodes[6::16, :]).then_inc(T.sem.dS, 16)
    sca.dma_start(out=T.n0[:, :], in_=T.nodes[:, 0:8]).then_inc(T.sem.dN, 16)
    syn.wait_ge(T.sem.m0, 1)
    sca.wait_ge(T.sem.m0, 1)

    def load(q, gg, h):
        a, b = (0, 1024) if h == 0 else (1024, 2047)
        q.dma_start(out=T.basei[16 * gg:16 * gg + 7, a:b], in_=T.nodes[16 * gg:16 * gg + 7, a + 1:b + 1]).then_inc(T.sem["dB%d" % h], 16)
    for gg in range(4):
        load(syn, gg, 0)
        load(sca, gg + 4, 0)
    for a in (11, 12, 13, 14):
        sca.dma_start(out=T.basei[a::16, 0:2047], in_=T.nodes[a::16, 1:2048]).then_inc(T.sem.dZ, 16)
    for gg in range(4):
        load(sca, gg + 4, 1)
    vwait(syn, "pa1e", "pa0e", "pz")
    for row, name in ((8, "pa1"), (9, "pa0"), (10, "pz")):
        syn.dma_start(out=T.basei[row::16, 0:2048], in_=T[name][:, :]).then_inc(T.sem.dPc, 16)
    for gg in range(4):
        load(syn, gg, 1)
    vwait(syn, "ph", "pl")
    for row, name in ((7, "ph"), (15, "pl")):
        syn.dma_start(out=T.basei[row::16, 0:2048], in_=T[name][:, :]).then_inc(T.sem.dPc, 16)

    fl = {"allow_small_or_imprecise_dtypes": True}
    g.iota(T.coli[:, 0:1], [[0, 1]], 0, 1).then_inc(T.sem.gi0, 1)
    g.iota(T.colp[:, 0:1], [[0, 1]], 0, -1, **fl).then_inc(T.sem.gi5, 1)
    g.iota(T.pa1[:, :], [[1, 8], [0, 16]], 0, 8).then_inc(T.sem.gi1, 1)
    g.iota(T.pa0[:, :], [[0, 8], [1, 16]], 1, 0).then_inc(T.sem.gi1, 1)
    g.iota(T.u1[:, :], [[1, 144]], 0, 0, **fl).then_inc(T.sem.gi3, 1)
    g.wait_ge(T.sem.kp, 1)
    for a in range(6):
        g.iota(T.pat[:, a::16], [[3, 8]], a % 3, 0, **fl).then_inc(T.sem.gi2, 1)

    dire, shar = direct(core), shares(core)
    chip_mates = topo.cores_of(core)
    vwait(g, "msg")
    wide = topo.engines(core, shar[0][0])
    n_on = len(wide) // 2
    rel_engs = [wide[n_on + 4 * i:n_on + 4 * i + 4] for i in range(len(shar))]
    res_engs = [wide[8 * i:8 * i + 8] for i in range(len(shar))]
    dir_engs, k = {}, 0
    for d in dire:
        if d in chip_mates:
            dir_engs[d] = wide[n_on:n_on + 4]
        else:
            dir_engs[d] = topo.engines(core, d)[4 * k:4 * k + 4]
            k += 1
    g.remote_dma_fused([tr(T.msg[:, :], T.rmsg[:, :], rel, rel_engs[i], "rm") for i, (rel, _) in enumerate(shar)], local_sem=T.sem.ls)
    g.remote_dma_fused([tr(T.msg[:, :], T.land[:, 64 * slot(d, core):64 * slot(d, core) + 64], d, dir_engs[d],
                           "pa%d" % direct(d).index(core)) for d in dire], local_sem=T.sem.ls)
    g.iota(T.u2[:, :], [[1, 72], [0, 2]], 0, 0, **fl).then_inc(T.sem.gi4, 1)

    def act(out, in_, func, sem, **kw):
        sca.activation(out=out, in_=in_, func=func, **kw).then_inc(T.sem[sem], 1)

    def first(b):
        sca.wait_ge(T.sem["pp" + b], 8)
        act(T["C1" + b][:, :], T["pp" + b][:, :], Fn.Tanh, "sy" + b, bias=cf("s1"), scale=-8.0)
        act(T["P" + b][:, :], T["pp" + b][:, :], Fn.Copy, "pc" + b)

    sca.wait_ge(T.sem.gi3, 1)
    sca.wait_ge(T.sem.gi5, 1)
    act(T.zt[:, 0:128], T.u1[:, 0:128], Fn.Abs, "ksb", bias=T.colp[:, 0:1])
    sca.wait_ge(T.sem.ksb, 1)
    act(T.idn[:, :], T.zt[:, 0:128], Fn.Relu, "ksc", bias=1.0, scale=-1.0)
    vwait(sca, "ne", "no")
    for k, name in ((0, "ne"), (1, "no")):
        act(T.zt[:, 128 + 48 * k:176 + 48 * k], T.u1[:, 0:48], Fn.Abs, "ksb", bias=cf(name))
    sca.wait_ge(T.sem.ksb, 3)
    act(T.zs[:, :], T.zt[:, 128:224], Fn.Relu, "ksd", bias=1.0, scale=-1.0)
    vwait(sca, "sg")
    act(cs(NG), cf("sg"), Fn.Copy, "kt", scale=-1.0)
    act(cs(SC), cf("bd"), Fn.Identity, "kt", bias=EPS, scale=2.0 - EPS)
    act(cs(TH), cf("bd"), Fn.Identity, "kt", bias=1.0, scale=7.0)
    act(T.colt[:, 0:1], cf("sg"), Fn.Tanh, "ku", scale=16.0)
    act(cs(WA), cf("a"), Fn.Identity, "ku", bias=479.125 / EPS, scale=-31.875 / EPS)
    act(cs(TA), cf("a"), Fn.Identity, "ku", bias=-10.0)
    vwait(sca, "w7")
    act(cs(NW), cf("w7"), Fn.Identity, "kv", bias=1.0, scale=-1.0)
    sca.wait_ge(T.sem.ku, 3)
    act(cs(WZ), cf("w7"), Fn.Copy, "kx", scale=cs(WA))
    act(cs(TA), cs(TA), Fn.Abs, "kx")
    vwait(sca, "s1")
    sca.wait_ge(T.sem.kv, 1)
    sca.wait_ge(T.sem.kx, 2)
    first("A")
    for h in range(2):
        sca.wait_ge(T.sem.kbase, h + 1)
        act(T.tab[:, 2048 * h + 2:2048 * h + 2049:2], T.basef[:, 1024 * h:1024 * h + 1024], Fn.Copy, "ht")
    for k in range(2):
        act(T.tab[:, k:k + 1], T.basef[:, 2047:2048], Fn.Copy, "ht", scale=cs(NW))
    first("B")
    vwait(sca, "nu2", "nu3", "odd", "s0")
    sca.wait_ge(T.sem.gi4, 1)
    act(T.zt[:, 224:368], T.u2[:, :], Fn.Abs, "kth", bias=cf("nu2"))
    act(T.zt[:, 368:512], T.u2[:, :], Fn.Abs, "kth", bias=cf("nu3"))
    act(cs(EV), cf("odd"), Fn.Identity, "kth", bias=1.0, scale=-1.0)
    act(cs(WH), cf("odd"), Fn.Identity, "kth", bias=256.0 / EPS, scale=-255.0 / EPS)
    act(cs(NWH), cf("odd"), Fn.Identity, "kth", bias=-256.0 / EPS, scale=255.0 / EPS)
    act(cs(KT), cs(TA), Fn.Relu, "kth", bias=1.0, scale=-1.0)
    sca.wait_ge(T.sem.kth, 6)
    act(cs(QZ), cs(KT), Fn.Identity, "kzp", bias=T.colt[:, 0:1], scale=2.0 / EPS)
    act(T.zp[:, :], T.zt[:, 224:368], Fn.Relu, "kzp", bias=1.0, scale=-1.0)
    act(T.zh[:, :], T.zt[:, 368:512], Fn.Relu, "kzp", bias=cs(WH), scale=cs(NWH))
    sca.wait_ge(T.sem.kzp, 3)
    sca.wait_ge(T.sem.kt, 3)

    vec.wait_ge(T.sem.kt, 3)
    vec.wait_ge(T.sem.kv, 1)
    need("missl")
    vec.wait_ge(T.sem.dB0, 128)
    vec.wait_ge(T.sem.dZ, 64)
    vec.wait_ge(T.sem.dPc, 80)
    ts(T.basef[:, 0:1024], T.basei[:, 0:1024], cs(SC), Op.mult, cs(NG), Op.add).then_inc(T.sem.kbase, 1)
    vec.wait_ge(T.sem.dB1, 128)
    ts(T.basef[:, 1024:2048], T.basei[:, 1024:2048], cs(SC), Op.mult, cs(NG), Op.add).then_inc(T.sem.kbase, 1)
    vec.wait_ge(T.sem.kbase, 2)
    v("tab", ts(T.tab[:, 3:4098:2], T.basef[:, 0:2048].indirect(T.missl[:, 0:128]), cs(NW), Op.mult))

    vwait(ten, "skh")
    ten.wait_ge(T.sem.ksc, 1)
    ten.matmul(T.ppB[:, 0:128], T.skh[:, :], T.idn[:, :], True, True).then_inc(T.sem.lt, 1)
    vwait(ten, "skt")
    ten.wait_ge(T.sem.ksd, 1)
    for c in range(8):
        a = 32 * (c // 2)
        if c % 2 == 0 and c > 0:
            ten.wait_ge(T.sem.ll, 8 * c)
        for gg in range(8):
            h, z = 32 * (gg // 2), 48 * (c % 2) + 16 - 16 * (gg % 2)
            ten.matmul(T.ppB[h:h + 32, 128 + c:256:8], T.zs[a:a + 32, z:z + 32], T.skt[a:a + 32, 16 * gg:16 * gg + 16],
                       gg % 2 == 0, gg % 2 == 1).then_inc(T.sem.ll, 1)

    def spread(b, srcs):
        for r, (buf, c0, sem) in enumerate(srcs):
            if sem:
                ten.wait_ge(T.sem[sem], 4)
            for h in range(2):
                ten.matmul(T["pp" + b][:, 256 * h + r:256 * h + 253 + r:4], T.lp[:, 128 * h:128 * h + 128],
                           T[buf][:, c0:c0 + 64], True, True).then_inc(T.sem["pp" + b], 1)

    def tx(b, t, js):
        for j in js:
            ten.matmul(T["X" + b][:, 0:32], T.zx[:, 15 - j:143 - j], T["C%d%s" % (t % 2, b)][:, j:512:16],
                       j == 0, j == 15).then_inc(T.sem["x" + b], 1)

    def pairs(out, z, src, sem, start, stop, k=128):
        for p in range(8):
            ten.matmul(out, T[z][0:k, 14 - 2 * p:142 - 2 * p], T[src][0:k, 64 * p:64 * p + 64],
                       start and p == 0, stop and p == 7).then_inc(T.sem[sem], 1)

    nd, nx = len(dire), len(cross(core))
    vwait(ten, "lp0", "lp1", "msg")
    spread("A", [("msg", 0, None)] + [("land", 64 * i, "pa%d" % i) for i in range(nd)])
    vwait(ten, "missl")
    spread("B", [("land", 64 * (nd + i), "pb%d" % i) for i in range(nx)])
    vwait(ten, "zx")
    for b in "AB":
        ten.wait_ge(T.sem["sy" + b], 1)
        tx(b, 1, range(16))

    def swait(q, b, t):
        if t > 2 or b == B1:
            q.wait_ge(T.sem["s" + b], t - 1 if b == B1 else t - 2)

    for t in range(2, V):
        for b in ORD:
            W, c = T["W" + b][:, 0:64], "C%d%s" % (t % 2, b)
            ten.wait_ge(T.sem["c" + b], t - 1)
            if t < V - 1:
                tx(b, t, range(0, 16, 2))
            swait(ten, b, t)
            if t < V - 1:
                tx(b, t, range(1, 16, 2))
            if t == 5 and b == B0:
                ten.wait_ge(T.sem.kzw, 4)
                for p in range(8):
                    ten.matmul(T.psm[:, 0:2], T.zw[:, 14 - 2 * p:142 - 2 * p], T.colb[:, 0:2], p == 0, p == 7).then_inc(T.sem.w47, 1)
            if t == 8:
                ten.wait_ge(T.sem["f" + b], 4)
                o = 8 if b == "A" else 72
                pairs(T.psm[:, o:o + 64], "zq", "F" + b, "qo" + b, True, True)
            if t == 11:
                ten.wait_ge(T.sem["hx" + b], 64)
                ten.wait_ge(T.sem["hy" + b], 64)
                pairs(W, "zh", "h1" + b, "wb" + b, True, False)
            if t == 12:
                pairs(W, "zw", c, "wa" + b, False, False)
            if t == 13:
                pairs(W, "zw", c, "wb" + b, False, False)
                ten.wait_ge(T.sem["hz" + b], 16)
                ten.wait_ge(T.sem["hw" + b], 16)
                pairs(W, "zh", "h2" + b, "wb" + b, False, False, 16 * len(H2))
            if t == V - 1:
                pairs(T["X" + b][:, 0:64], "zq", c, "q" + b, True, True)
                pairs(W, "zw", c, "wb" + b, False, True)

    for t in list(H1) + list(H2):
        for b in ORD:
            syn.wait_ge(T.sem["c" + b], t - 1)
            swait(syn, b, t)
            dst, k, sem = ("h1", t - H1[0], "hx" if t % 2 == 0 else "hy") if t in H1 else ("h2", t - H2[0], "hz" if t % 2 == 0 else "hw")
            syn.dma_start(out=T[dst + b][16 * k:16 * k + 16, :], in_=T["C%d%s" % (t % 2, b)][7::8, :]).then_inc(T.sem[sem + b], 16)

    def clamp(b, t):
        n = 1 if t == 2 and b == B0 else 2
        vec.wait_ge(T.sem["g" + b], t - 1)
        ts(T["C%d%s" % (t % 2, b)][:, 0:512:n], T["D" + b][:, 0:512:n], 1.0, Op.min, -1.0, Op.max).then_inc(T.sem["c" + b], 1)

    vec.wait_ge(T.sem.ht, 4)
    need("tab")
    last = None
    for t in range(2, V):
        for b in ORD:
            D, C = T["D" + b], T["C%d%s" % (t % 2, b)]
            if t == 2:
                vec.wait_ge(T.sem["pc" + b], 1)
            vec.wait_ge(T.sem["x" + b], 16 * (t - 1))
            ts(T["off" + b][:, :], T["X" + b][:, 0:32], 2.953125 if t > 2 else 4.953125, Op.add).then_inc(T.sem["o" + b], 1)
            if last:
                clamp(*last)
            if t - 2 in H1:
                vec.wait_ge(T.sem[("hx" if t % 2 == 0 else "hy") + b], 16 * ((t - 2) // 2))
            elif t - 2 in H2:
                vec.wait_ge(T.sem[("hz" if t % 2 == 0 else "hw") + b], 16)
            elif t == 14:
                vec.wait_ge(T.sem["wa" + b], 8)
            vec.wait_ge(T.sem["o" + b], t - 1)
            tt(D[:, :], T.tab[:, 0:4098].indirect(T["off" + b][:, 0:32]), T["P" + b][:, :], Op.subtract).then_inc(T.sem["g" + b], 1)
            last = (b, t)
            if t > 2 or b != B0:
                sca.wait_ge(T.sem["g" + b], t - 1)
                act(C[:, 1:512:2], D[:, 1:512:2], Fn.Tanh, "s" + b, scale=cs(TH))
            if t == 3 and b == B0:
                for k, cc in ((0, 2047), (1, 0)):
                    act(T.colb[:, k:k + 1], T.basef[:, cc:cc + 1], Fn.Copy, "kzw")
                act(T.zw[:, :], T.zp[:, :], Fn.Copy, "kzw", scale=cs(WZ))
            if t == 3 and b == B1:
                act(T.zq[:, :], T.zp[:, :], Fn.Copy, "kzw", scale=cs(QZ))
            if 4 <= t < 8:
                a = 128 * (t - 4)
                act(T["F" + b][:, a:a + 128], T["pp" + b][:, a:a + 128], Fn.Tanh, "f" + b, bias=cf("s0"), scale=-8.0)

    for sem in ("w47", "qoA", "qoB"):
        vec.wait_ge(T.sem[sem], 8)
    v("w07", vec.tensor_copy(out=T.colf[:, 0:2], in_=T.psm[:, 0:2]))
    clamp(*last)

    def flag(b, h):
        o = (8 if b == "A" else 72) + 32 * h
        v("fm" + b, ts(T["fm" + b][:, 32 * h:32 * h + 32], T.psm[:, o:o + 32], -5.0, Op.is_lt, (cs(EV), cf("odd"))[h], Op.mult))

    def end(b):
        vec.wait_ge(T.sem["q" + b], 8)
        need("w07")
        v("t1" + b, ts(T["t1" + b][:, :], T["X" + b][:, 0:64], -5.0, Op.is_lt, T.colf[:, 0:1], Op.mult))

    def add0(b):
        need("t1" + b)
        v("t4" + b, ts(T["t4" + b][:, :], T["t1" + b][:, :], T.colf[:, 1:2], Op.add))

    def addw(b):
        vec.wait_ge(T.sem["wb" + b], 32)
        need("t4" + b)
        v("t2" + b, tt(T["t2" + b][:, :], T["W" + b][:, 0:64], T["t4" + b][:, :], Op.add))

    def cutf(b):
        need("t2" + b, "fm" + b)
        v("t3" + b, tt(T["t3" + b][:, :], T["t2" + b][:, :], T["fm" + b][:, :], Op.mult))

    def sums(b):
        need("t3" + b)
        for r in range(4):
            out = T.rland[:, 0:8] if (b == "A" and r == 0) else T["R" + b][:, 8 * r:8 * r + 8]
            tt(out, T["t3" + b][:, r:32:4], T["t3" + b][:, 32 + r:64:4], Op.add).then_inc(T.sem["kr" + b], 1)

    vec.wait_ge(T.sem.kth, 6)
    flag("B", 0)
    end("B")
    flag("B", 1)
    add0("B")
    flag("A", 0)
    addw("B")
    flag("A", 1)
    cutf("B")
    end("A")
    sums("B")
    add0("A")
    addw("A")
    cutf("A")
    sums("A")
    g.wait_ge(T.sem.krB, 4)
    g.remote_dma_fused([tr(T.RB[:, 16 * i:16 * i + 16], T.rres[:, :], rel, res_engs[i], "rr") for i, (rel, _) in enumerate(shar)],
                       local_sem=T.sem.ls)
    g.wait_ge(T.sem.krA, 4)
    g.remote_dma_fused([tr(T.RA[:, 8 * i + 8:8 * i + 16], T.rland[:, 8 * slot(d, core) + 8:8 * slot(d, core) + 16], d, dir_engs[d], "rs")
                        for i, d in enumerate(dire)], local_sem=T.sem.ls)
    vec.wait_ge(T.sem.krA, 4)
    vec.wait_ge(T.sem.rs, 4 * 7)
    v("s32", tt(T.s32[:, :], T.rland[:, 0:32], T.rland[:, 32:64], Op.add))
    need("s32")
    v("s16", tt(T.s16[:, :], T.s32[:, 0:16], T.s32[:, 16:32], Op.add))
    need("s16")
    tt(T.ysum[:, :], T.s16[:, 0:8], T.s16[:, 8:16], Op.add).then_inc(T.sem.ys, 1)
    syn.wait_ge(T.sem.ys, 1)
    syn.dma_start(out=T.y[:, :], in_=T.ysum[:, :]).then_inc(T.sem.dY, 16)
    syn.wait_ge(T.sem.dY, 16)
    g.wait_ge(T.sem.ls, 12 * len(shar) + 8 * nd)
